import numpy as np
import ml_dtypes


def mxq(x, axis, fmt="e4m3"):
    dtype, down = {"e4m3": (ml_dtypes.float8_e4m3fn, 7), "e5m2": (ml_dtypes.float8_e5m2, 14)}[fmt]
    v = np.moveaxis(np.asarray(x, np.float32).astype(ml_dtypes.bfloat16).astype(np.float64), axis, -1)
    blocks = v.reshape(v.shape[:-1] + (-1, 32))
    amax = np.abs(blocks).max(-1, keepdims=True)
    byte = np.maximum(np.where(amax > 0, np.frexp(amax)[1] - 1 + 127, 0) - down, 1)
    scale = np.exp2(byte - 127.0)
    codes = (blocks / scale).astype(np.float32).astype(dtype).astype(np.float64)
    return np.moveaxis((codes * scale).reshape(v.shape), -1, axis)


WIDE = False


def mx_kscale(k):
    if not WIDE:
        return np.ones(k)
    levels = np.array([18, -18])
    if k % 512:
        return np.exp2(np.random.permutation(np.resize(levels, k // 32))).repeat(32)
    a = np.empty((k // 512, 16))
    for p in range(k // 512):
        a[p, :8] = np.random.permutation(np.resize(levels, 8))
        for g in range(8):
            far = levels[np.abs(levels - a[p, g]) >= 10]
            a[p, g + 8] = far[np.random.randint(len(far))]
    return np.exp2(a.ravel()).repeat(32)


def f64(x):
    return np.asarray(x).astype(np.float64)


def striped(idx):
    return np.tile(np.asarray(idx).reshape(-1, 16).T, (8, 1)).astype(np.uint16)


def unstriped(offs):
    return offs[:16].T.reshape(-1).astype(np.int64)


B, N, T, D, R = 2, 512, 2048, 512, 512


def setup_inputs():
    n = np.random.standard_normal
    idx = np.random.permutation(T)[:B * N]
    s = mx_kscale(D)[:, None]
    z = mx_kscale(R)[:, None]
    x = n((B, D, R))
    return {
        "xT": (x * s).astype(np.float32),
        "wT": (n((D, T)) * (1.00 / np.sqrt(D)) / s).astype(np.float32),
        "vT": (n((D, T)) / np.sqrt(D) / s).astype(np.float32),
        "wt": (np.random.uniform(0.5, 1.5, (B, R, 1)) * 1.0 / np.sqrt(R) * z).astype(np.float32),
        "xm": (x.transpose(0, 2, 1) / z).astype(np.float32),
        "offs": striped(idx),
    }


def reference(xT, wT, vT, wt, xm, offs):
    idx = unstriped(offs)
    pick = lambda x: x[:, idx].reshape(x.shape[0], B, N).transpose(1, 0, 2)
    xq = mxq(f64(xT), 1, "e4m3").transpose(0, 2, 1)
    a = xq @ mxq(pick(f64(wT)), 1, "e4m3")
    av = xq @ mxq(pick(f64(vT)), 1, "e4m3")
    g = f64(wt) * (1.0 / (1.0 + np.exp(-a)) - 1.0 / (1.0 + np.exp(-av)))
    dw = mxq(f64(xm), 1, "e4m3").transpose(0, 2, 1) @ mxq(g, 1, "e5m2")
    gw = np.zeros((D, T))
    gw[:, idx] = dw.transpose(1, 0, 2).reshape(D, B * N)
    return gw

@@ -1,0 +1,219 @@
+from contextlib import ExitStack
+
+import concourse.mybir as mybir
+from concourse.masks import make_identity
+
+B, N, T, D, R = 2, 512, 2048, 512, 512
+FLOPS = 3 * 2 * B * N * D * R
+
+F32 = mybir.dt.float32
+BF16 = mybir.dt.bfloat16
+U32 = mybir.dt.uint32
+U16 = mybir.dt.uint16
+U8 = mybir.dt.uint8
+E4M3 = mybir.dt.float8_e4m3fn_x4
+E5M2 = mybir.dt.float8_e5m2_x4
+MULT = mybir.AluOpType.mult
+COPY = mybir.ActivationFunctionType.Copy
+TANH = mybir.ActivationFunctionType.Tanh
+
+P = 128
+PACK = 4
+LIST_COLS = N // 16
+
+
+def tile_attend_gds_nce_kernel(tc, xT, wT, vT, wt, xm, offs, out):
+    nc = tc.nc
+    with ExitStack() as ctx:
+        keep = ctx.enter_context(tc.tile_pool(name="keep", bufs=1))
+        raw = ctx.enter_context(tc.tile_pool(name="raw", bufs=8))
+        rows_pool = ctx.enter_context(tc.tile_pool(name="rows_pool", bufs=4))
+        ring = ctx.enter_context(tc.tile_pool(name="ring", bufs=4))
+        mm_psum = ctx.enter_context(tc.psum_pool(name="mm_psum", bufs=4))
+        diff_psum = ctx.enter_context(tc.psum_pool(name="diff_psum", bufs=1))
+
+        offsets = keep.tile([P, B * LIST_COLS], U16, name="offsets")
+        weights = keep.tile([P, B, PACK], F32, name="weights")
+        ident = keep.tile([P, P], F32, name="ident")
+        placed = [keep.tile([P, T], F32, name="placed%d" % k) for k in range(D // P)]
+        warm = keep.tile([P, 8], F32, name="warm")
+        warm_out = keep.tile([P, 8], F32, name="warm_out")
+
+        nc.gpsimd.memset(warm[:], 0.0)
+        nc.scalar.activation(warm_out[:], warm[:], TANH)
+        make_identity(nc, ident[:])
+        for k, tile in enumerate(placed):
+            (nc.vector if k < 2 else nc.gpsimd).memset(tile[:], 0.0)
+
+        def group_offsets(b, i0=0, i1=N):
+            return offsets[:, b * LIST_COLS + i0 // 16 : b * LIST_COLS + i1 // 16]
+
+        windows = {}
+        picked = {}
+        codes = {}
+        for name in ("w", "v"):
+            for u in range(2):
+                windows[name, u] = keep.tile([P, T, 2], BF16, name="win_%s%d" % (name, u), align_bytes=64)
+            for b in range(B):
+                picked[name, b] = keep.tile([P, N, 2], U32, name="picked_%s%d" % (name, b), align_bytes=64)
+
+        def load_table(table, u, c0, c1, last):
+            if last:
+                stage = keep.tile([P, 2, c1 - c0], F32, name="last_stage", tag="last_stage")
+            else:
+                stage = raw.tile([P, 2, c1 - c0], F32, name="stage", tag="stage")
+            rows = table.rearrange("(p j) c -> p j c", j=PACK)
+            nc.sync.dma_start(out=stage[:], in_=rows[:, 2 * u : 2 * u + 2, c0:c1])
+            return stage
+
+        def cast_table(name, u, c0, c1, stage):
+            nc.scalar.activation(windows[name, u][:, c0:c1, :], stage[:].rearrange("p e c -> p c e"), COPY)
+
+        def load_rows(src):
+            stage = rows_pool.tile([P, PACK, 512], F32, name="rows", tag="rows")
+            nc.sync.dma_start(out=stage[:], in_=src.rearrange("(p j) c -> p j c", j=PACK))
+            return stage
+
+        def gather(name, u, b, i0=0, i1=N):
+            window = windows[name, u][:].rearrange("p c e -> p (c e)").bitcast(U32)
+            nc.vector.tensor_copy(picked[name, b][:, i0:i1, u], window.indirect(group_offsets(b, i0, i1)))
+
+        def quantize(key, values, fmt, c0=0, c1=512):
+            if key not in codes:
+                words = keep.tile([P, 512], U32, name="words_%s%d" % key, align_bytes=64)
+                scales = keep.tile([P, 512], U8, name="scales_%s%d" % key, align_bytes=64)
+                codes[key] = (words, scales, fmt)
+            words, scales, fmt = codes[key]
+            nc.vector.quantize_mx(out=words[:, c0:c1].bitcast(fmt), scales=scales[:, c0:c1], in_=values[:, PACK * c0 : PACK * c1])
+
+        def quantize_picked(name, b, c0=0, c1=512):
+            quantize((name, b), picked[name, b][:].rearrange("p n u -> p (n u)").bitcast(BF16), E4M3, c0, c1)
+
+        grouped = {}
+
+        def interleave(key, stage, on_scalar, c0=0, c1=512):
+            if key not in grouped:
+                grouped[key] = keep.tile([P, 512, PACK], BF16, name="grouped_%s%d" % key, align_bytes=64)
+            src = stage[:, :, c0:c1].rearrange("p j c -> p c j")
+            if on_scalar:
+                nc.scalar.copy(grouped[key][:, c0:c1, :], src)
+            else:
+                nc.vector.tensor_copy(grouped[key][:, c0:c1, :], src)
+            return grouped[key][:].rearrange("p c j -> p (c j)")
+
+        def product(stationary, k, moving):
+            s_words, s_scales, s_fmt = codes[stationary]
+            m_words, m_scales, m_fmt = codes[moving]
+            bank = mm_psum.tile([P, 512], F32, name="bank", tag="bank")
+            cols = slice(k * P, (k + 1) * P)
+            nc.tensor.matmul_mx(
+                out=bank[:],
+                lhsT=s_words[:, cols].bitcast(s_fmt),
+                lhsT_scale=s_scales[:, cols],
+                rhs=m_words[:].bitcast(m_fmt),
+                rhs_scale=m_scales[:],
+                start=True,
+                stop=True,
+            )
+            return bank
+
+        diffs = {}
+
+        def head(name, b):
+            first = name == "w"
+            banks = [product((name, b), c, ("xT", b)) for c in range(4)]
+            held = keep.tile([P, 4, PACK, P], F32, name="last_stage", tag="last_stage") if first and b == 0 else None
+            for c in range(4):
+                if held is not None:
+                    th = held[:, c]
+                else:
+                    th = ring.tile([P, PACK, P], F32, name="th", tag="th")
+                nc.scalar.activation(th[:, :, :], banks[c][:].rearrange("p (m t) -> p t m", t=PACK), TANH, scale=0.5 if first else -0.5)
+                if first:
+                    diffs[b, c] = diff_psum.tile([P, PACK, P], F32, name="diff%d" % c, tag="diff%d" % c)
+                for t in range(PACK):
+                    nc.tensor.matmul(
+                        diffs[b, c][:, t, :], th[:, t, :], ident[:], is_transpose=True,
+                        start=first and t == 0, stop=(not first) and t == PACK - 1,
+                    )
+
+        def weigh(b):
+            g = keep.tile([P, N, PACK], BF16, name="g%d" % b, align_bytes=64)
+            for c in range(4):
+                nc.vector.scalar_tensor_tensor(
+                    g[:, c * P : (c + 1) * P, :],
+                    diffs[b, c][:].rearrange("p t i -> p i t"),
+                    0.5,
+                    weights[:, b : b + 1, :].to_broadcast([P, P, PACK]),
+                    MULT,
+                    MULT,
+                )
+                if c == 2:
+                    quantize(("g", b), g[:].rearrange("p n t -> p (n t)"), E5M2, 0, 256)
+            quantize(("g", b), g[:].rearrange("p n t -> p (n t)"), E5M2, 256, 512)
+
+        def gradient(b, k):
+            bank = product(("xm", b), k, ("g", b))
+            dw = ring.tile([P, N], F32, name="dw", tag="dw")
+            nc.scalar.copy(dw[:], bank[:])
+            nc.vector.tensor_copy(placed[k][:].indirect(group_offsets(b)), dw[:])
+
+        quarters = [(c, c + 512) for c in range(0, T, 512)]
+        pieces = {
+            ("w", 0): quarters,
+            ("w", 1): quarters,
+            ("v", 0): quarters,
+            ("v", 1): quarters[:3] + [(1536, 1792), (1792, 2048)],
+        }
+        tables = {"w": wT, "v": vT}
+
+        def bring(name, u):
+            for c0, c1 in pieces[name, u]:
+                cast_table(name, u, c0, c1, load_table(tables[name], u, c0, c1, (name, u, c1) == ("v", 1, T)))
+
+        bring("w", 0)
+        nc.sync.dma_start(offsets[:], offs)
+        xT0 = load_rows(xT[0])
+        for b in range(B):
+            gather("w", 0, b)
+        quantize(("xT", 0), interleave(("xT", 0), xT0, False), E4M3)
+        bring("w", 1)
+        nc.sync.dma_start(out=weights[:], in_=wt.rearrange("b (p t) o -> p b (t o)", t=PACK))
+        for b in range(B):
+            gather("w", 1, b)
+        for b in range(B):
+            quantize_picked("w", b)
+        bring("v", 0)
+        for b in range(B):
+            gather("v", 0, b)
+        bring("v", 1)
+        xm0 = load_rows(xm[0])
+        xT1 = load_rows(xT[1])
+        xm1 = load_rows(xm[1])
+        head("w", 0)
+        gather("v", 1, 0, 0, 256)
+        gather("v", 1, 0, 256, 512)
+        quantize_picked("v", 0, 0, 256)
+        quantize_picked("v", 0, 256, 512)
+        head("v", 0)
+        quantize(("xm", 0), interleave(("xm", 0), xm0, True, 0, 128), E4M3, 0, 128)
+        weigh(0)
+        gradient(0, 0)
+        gather("v", 1, 1, 0, 256)
+        gather("v", 1, 1, 256, 512)
+        quantize_picked("v", 1)
+        quantize(("xm", 0), interleave(("xm", 0), xm0, True, 128, 256), E4M3, 128, 256)
+        for c in range(0, 512, 128):
+            xT1_grouped = interleave(("xT", 1), xT1, True, c, c + 128)
+        quantize(("xT", 1), xT1_grouped, E4M3)
+        gradient(0, 1)
+        quantize(("xm", 0), interleave(("xm", 0), xm0, True, 256, 512), E4M3, 256, 512)
+        head("w", 1)
+        gradient(0, 2)
+        head("v", 1)
+        quantize(("xm", 1), interleave(("xm", 1), xm1, True), E4M3)
+        weigh(1)
+        gradient(0, 3)
+        for k in range(D // P):
+            gradient(1, k)
+            nc.sync.dma_start(out=out[k * P : (k + 1) * P, :], in_=placed[k][:])

@@ -26,8 +26,8 @@ def tile_attend_gds_nce_kernel(tc, xT, wT, vT, wt, xm, offs, out):
     nc = tc.nc
     with ExitStack() as ctx:
         keep = ctx.enter_context(tc.tile_pool(name="keep", bufs=1))
-        raw = ctx.enter_context(tc.tile_pool(name="raw", bufs=8))
-        rows_pool = ctx.enter_context(tc.tile_pool(name="rows_pool", bufs=4))
+        raw = ctx.enter_context(tc.tile_pool(name="raw", bufs=5))
+        rows_pool = ctx.enter_context(tc.tile_pool(name="rows_pool", bufs=3))
         ring = ctx.enter_context(tc.tile_pool(name="ring", bufs=4))
         mm_psum = ctx.enter_context(tc.psum_pool(name="mm_psum", bufs=4))
         diff_psum = ctx.enter_context(tc.psum_pool(name="diff_psum", bufs=1))
@@ -66,8 +66,12 @@ def tile_attend_gds_nce_kernel(tc, xT, wT, vT, wt, xm, offs, out):
             nc.sync.dma_start(out=stage[:], in_=rows[:, 2 * u : 2 * u + 2, c0:c1])
             return stage
 
-        def cast_table(name, u, c0, c1, stage):
-            nc.scalar.activation(windows[name, u][:, c0:c1, :], stage[:].rearrange("p e c -> p c e"), COPY)
+        def cast_table(name, u, base, c0, c1, stage, on_scalar):
+            src = stage[:, :, c0 - base : c1 - base].rearrange("p e c -> p c e")
+            if on_scalar:
+                nc.scalar.activation(windows[name, u][:, c0:c1, :], src, COPY)
+            else:
+                nc.vector.tensor_copy(windows[name, u][:, c0:c1, :], src)
 
         def load_rows(src):
             stage = rows_pool.tile([P, PACK, 512], F32, name="rows", tag="rows")
@@ -94,11 +98,12 @@ def tile_attend_gds_nce_kernel(tc, xT, wT, vT, wt, xm, offs, out):
         def interleave(key, stage, on_scalar, c0=0, c1=512):
             if key not in grouped:
                 grouped[key] = keep.tile([P, 512, PACK], BF16, name="grouped_%s%d" % key, align_bytes=64)
-            src = stage[:, :, c0:c1].rearrange("p j c -> p c j")
+            src = stage[:, :, c0:c1].rearrange("p j (c i) -> p c j i", i=4)
+            dst = grouped[key][:, c0:c1, :].rearrange("p (c i) j -> p c j i", i=4)
             if on_scalar:
-                nc.scalar.copy(grouped[key][:, c0:c1, :], src)
+                nc.scalar.copy(dst, src)
             else:
-                nc.vector.tensor_copy(grouped[key][:, c0:c1, :], src)
+                nc.vector.tensor_copy(dst, src)
             return grouped[key][:].rearrange("p c j -> p (c j)")
 
         def product(stationary, k, moving):
@@ -152,31 +157,28 @@ def tile_attend_gds_nce_kernel(tc, xT, wT, vT, wt, xm, offs, out):
                     quantize(("g", b), g[:].rearrange("p n t -> p (n t)"), E5M2, 0, 256)
             quantize(("g", b), g[:].rearrange("p n t -> p (n t)"), E5M2, 256, 512)
 
+        dws = {}
+
         def gradient(b, k):
             bank = product(("xm", b), k, ("g", b))
-            dw = ring.tile([P, N], F32, name="dw", tag="dw")
-            nc.scalar.copy(dw[:], bank[:])
-            nc.vector.tensor_copy(placed[k][:].indirect(group_offsets(b)), dw[:])
+            dws[b, k] = ring.tile([P, N], F32, name="dw", tag="dw")
+            step = 256 if (b, k) == (0, 0) else N
+            for i0 in range(0, N, step):
+                nc.scalar.copy(dws[b, k][:, i0 : i0 + step], bank[:, i0 : i0 + step])
 
-        quarters = [(c, c + 512) for c in range(0, T, 512)]
-        pieces = {
-            ("w", 0): quarters,
-            ("w", 1): quarters,
-            ("v", 0): quarters,
-            ("v", 1): quarters[:3] + [(1536, 1792), (1792, 2048)],
-        }
+        def scatter(b, k, i0=0, i1=N):
+            nc.vector.tensor_copy(placed[k][:].indirect(group_offsets(b, i0, i1)), dws[b, k][:, i0:i1])
+
         tables = {"w": wT, "v": vT}
 
         def bring(name, u):
-            for c0, c1 in pieces[name, u]:
-                cast_table(name, u, c0, c1, load_table(tables[name], u, c0, c1, (name, u, c1) == ("v", 1, T)))
+            for c0 in (0, 1024):
+                cast_table(name, u, c0, c0, c0 + 1024, load_table(tables[name], u, c0, c0 + 1024, False), True)
 
         bring("w", 0)
         nc.sync.dma_start(offsets[:], offs)
-        xT0 = load_rows(xT[0])
         for b in range(B):
             gather("w", 0, b)
-        quantize(("xT", 0), interleave(("xT", 0), xT0, False), E4M3)
         bring("w", 1)
         nc.sync.dma_start(out=weights[:], in_=wt.rearrange("b (p t) o -> p b (t o)", t=PACK))
         for b in range(B):
@@ -186,7 +188,14 @@ def tile_attend_gds_nce_kernel(tc, xT, wT, vT, wt, xm, offs, out):
         bring("v", 0)
         for b in range(B):
             gather("v", 0, b)
-        bring("v", 1)
+        xT0 = load_rows(xT[0])
+        interleave(("xT", 0), xT0, True, 0, 384)
+        quantize(("xT", 0), interleave(("xT", 0), xT0, False, 384, 512), E4M3)
+        cast_table("v", 1, 0, 0, 1024, load_table(vT, 1, 0, 1024, False), True)
+        cast_table("v", 1, 1024, 1024, 1536, load_table(vT, 1, 1024, 1536, False), False)
+        last = load_table(vT, 1, 1536, T, True)
+        cast_table("v", 1, 1536, 1536, 1728, last, True)
+        cast_table("v", 1, 1536, 1728, T, last, False)
         xm0 = load_rows(xm[0])
         xT1 = load_rows(xT[1])
         xm1 = load_rows(xm[1])
@@ -196,13 +205,13 @@ def tile_attend_gds_nce_kernel(tc, xT, wT, vT, wt, xm, offs, out):
         quantize_picked("v", 0, 0, 256)
         quantize_picked("v", 0, 256, 512)
         head("v", 0)
-        quantize(("xm", 0), interleave(("xm", 0), xm0, True, 0, 128), E4M3, 0, 128)
+        interleave(("xm", 0), xm0, True, 0, 128)
+        quantize(("xm", 0), interleave(("xm", 0), xm0, True, 128, 256), E4M3, 0, 256)
         weigh(0)
         gradient(0, 0)
         gather("v", 1, 1, 0, 256)
         gather("v", 1, 1, 256, 512)
         quantize_picked("v", 1)
-        quantize(("xm", 0), interleave(("xm", 0), xm0, True, 128, 256), E4M3, 128, 256)
         for c in range(0, 512, 128):
             xT1_grouped = interleave(("xT", 1), xT1, True, c, c + 128)
         quantize(("xT", 1), xT1_grouped, E4M3)
@@ -211,9 +220,14 @@ def tile_attend_gds_nce_kernel(tc, xT, wT, vT, wt, xm, offs, out):
         head("w", 1)
         gradient(0, 2)
         head("v", 1)
+        gradient(0, 3)
         quantize(("xm", 1), interleave(("xm", 1), xm1, True), E4M3)
         weigh(1)
-        gradient(0, 3)
+        scatter(0, 0, 0, 256)
+        scatter(0, 0, 256, 512)
+        for k in range(1, D // P):
+            scatter(0, k)
         for k in range(D // P):
             gradient(1, k)
+            scatter(1, k)
             nc.sync.dma_start(out=out[k * P : (k + 1) * P, :], in_=placed[k][:])

@@ -20,6 +20,7 @@ TANH = mybir.ActivationFunctionType.Tanh
 P = 128
 PACK = 4
 LIST_COLS = N // 16
+BANK = 2048
 
 
 def tile_attend_gds_nce_kernel(tc, xT, wT, vT, wt, xm, offs, out):
@@ -29,11 +30,12 @@ def tile_attend_gds_nce_kernel(tc, xT, wT, vT, wt, xm, offs, out):
         raw = ctx.enter_context(tc.tile_pool(name="raw", bufs=5))
         rows_pool = ctx.enter_context(tc.tile_pool(name="rows_pool", bufs=3))
         ring = ctx.enter_context(tc.tile_pool(name="ring", bufs=4))
-        mm_psum = ctx.enter_context(tc.psum_pool(name="mm_psum", bufs=4))
+        score_psum = ctx.enter_context(tc.psum_pool(name="score_psum", bufs=3))
         diff_psum = ctx.enter_context(tc.psum_pool(name="diff_psum", bufs=1))
 
         offsets = keep.tile([P, B * LIST_COLS], U16, name="offsets")
         weights = keep.tile([P, B, PACK], F32, name="weights")
+        half_weights = keep.tile([P, B, PACK], F32, name="half_weights")
         ident = keep.tile([P, P], F32, name="ident")
         placed = [keep.tile([P, T], F32, name="placed%d" % k) for k in range(D // P)]
         warm = keep.tile([P, 8], F32, name="warm")
@@ -106,10 +108,9 @@ def tile_attend_gds_nce_kernel(tc, xT, wT, vT, wt, xm, offs, out):
                 nc.vector.tensor_copy(dst, src)
             return grouped[key][:].rearrange("p c j -> p (c j)")
 
-        def product(stationary, k, moving):
+        def product(bank, stationary, k, moving):
             s_words, s_scales, s_fmt = codes[stationary]
             m_words, m_scales, m_fmt = codes[moving]
-            bank = mm_psum.tile([P, 512], F32, name="bank", tag="bank")
             cols = slice(k * P, (k + 1) * P)
             nc.tensor.matmul_mx(
                 out=bank[:],
@@ -126,48 +127,67 @@ def tile_attend_gds_nce_kernel(tc, xT, wT, vT, wt, xm, offs, out):
 
         def head(name, b):
             first = name == "w"
-            banks = [product((name, b), c, ("xT", b)) for c in range(4)]
-            held = keep.tile([P, 4, PACK, P], F32, name="last_stage", tag="last_stage") if first and b == 0 else None
+            held = keep.tile([P, 4, PACK, P], F32, name="last_stage", tag="last_stage") if first else None
+            if first and b == 0:
+                for q in range(4):
+                    diffs[b, q] = diff_psum.tile([P, PACK, P], F32, name="diff%d" % q, offset=q * BANK)
+            if first and b == 1:
+                wide = diff_psum.tile([P, 4, PACK, P], F32, name="wide", offset=BANK)
+                for q in range(4):
+                    diffs[b, q] = wide[:, q]
             for c in range(4):
+                bank = product(score_psum.tile([P, R], F32, name="score", tag="score"), (name, b), c, ("xT", b))
                 if held is not None:
                     th = held[:, c]
                 else:
                     th = ring.tile([P, PACK, P], F32, name="th", tag="th")
-                nc.scalar.activation(th[:, :, :], banks[c][:].rearrange("p (m t) -> p t m", t=PACK), TANH, scale=0.5 if first else -0.5)
-                if first:
-                    diffs[b, c] = diff_psum.tile([P, PACK, P], F32, name="diff%d" % c, tag="diff%d" % c)
+                nc.scalar.activation(th[:, :, :], bank[:].rearrange("p (m t) -> p t m", t=PACK), TANH, scale=0.5 if first else -0.5)
                 for t in range(PACK):
+                    bank_index, place = (c, t) if b == 0 else (t, c)
                     nc.tensor.matmul(
-                        diffs[b, c][:, t, :], th[:, t, :], ident[:], is_transpose=True,
-                        start=first and t == 0, stop=(not first) and t == PACK - 1,
+                        diffs[b, bank_index][:, place, :], th[:, t, :], ident[:], is_transpose=True,
+                        start=first and place == 0, stop=(not first) and place == PACK - 1,
                     )
 
-        def weigh(b):
+        def weigh_on_vector(b):
             g = keep.tile([P, N, PACK], BF16, name="g%d" % b, align_bytes=64)
             for c in range(4):
-                nc.vector.scalar_tensor_tensor(
+                nc.vector.tensor_tensor(
                     g[:, c * P : (c + 1) * P, :],
                     diffs[b, c][:].rearrange("p t i -> p i t"),
-                    0.5,
-                    weights[:, b : b + 1, :].to_broadcast([P, P, PACK]),
-                    MULT,
+                    half_weights[:, b : b + 1, :].to_broadcast([P, P, PACK]),
                     MULT,
                 )
                 if c == 2:
                     quantize(("g", b), g[:].rearrange("p n t -> p (n t)"), E5M2, 0, 256)
             quantize(("g", b), g[:].rearrange("p n t -> p (n t)"), E5M2, 256, 512)
 
+        def weigh_on_scalar(b):
+            planes = keep.tile([P, PACK, N], BF16, name="g_planes", tag="g_planes", align_bytes=64)
+            for t in range(PACK):
+                nc.scalar.activation(planes[:, t, :], diffs[b, t].rearrange("p c i -> p (c i)"), COPY, scale=half_weights[:, b, t : t + 1])
+            quantize(("g", b), interleave(("g", b), planes, True), E5M2)
+
         dws = {}
 
         def gradient(b, k):
-            bank = product(("xm", b), k, ("g", b))
-            dws[b, k] = ring.tile([P, N], F32, name="dw", tag="dw")
-            step = 256 if (b, k) == (0, 0) else N
-            for i0 in range(0, N, step):
-                nc.scalar.copy(dws[b, k][:, i0 : i0 + step], bank[:, i0 : i0 + step])
+            if (b, k) == (0, 0):
+                bank = diff_psum.tile([P, N], F32, name="first_grad", offset=4 * BANK)
+            else:
+                bank = diff_psum.tile([P, N], F32, name="grad", tag="grad", offset=0)
+            product(bank, ("xm", b), k, ("g", b))
+            halves = b == 0 and k in (0, 3)
+            for i0, i1 in ((0, 256), (256, N)) if halves else ((0, N),):
+                if (b, k, i0) == (0, 3, 256):
+                    dw = keep.tile([P, i1 - i0], F32, name="g_planes", tag="g_planes", align_bytes=64)
+                else:
+                    dw = ring.tile([P, i1 - i0], F32, name="dw", tag="dw")
+                nc.scalar.copy(dw[:], bank[:, i0:i1])
+                dws.setdefault((b, k), []).append((i0, i1, dw))
 
-        def scatter(b, k, i0=0, i1=N):
-            nc.vector.tensor_copy(placed[k][:].indirect(group_offsets(b, i0, i1)), dws[b, k][:, i0:i1])
+        def scatter(b, k):
+            for i0, i1, dw in dws[b, k]:
+                nc.vector.tensor_copy(placed[k][:].indirect(group_offsets(b, i0, i1)), dw[:])
 
         tables = {"w": wT, "v": vT}
 
@@ -181,6 +201,7 @@ def tile_attend_gds_nce_kernel(tc, xT, wT, vT, wt, xm, offs, out):
             gather("w", 0, b)
         bring("w", 1)
         nc.sync.dma_start(out=weights[:], in_=wt.rearrange("b (p t) o -> p b (t o)", t=PACK))
+        nc.vector.tensor_scalar_mul(half_weights[:], weights[:], 0.5)
         for b in range(B):
             gather("w", 1, b)
         for b in range(B):
@@ -189,15 +210,14 @@ def tile_attend_gds_nce_kernel(tc, xT, wT, vT, wt, xm, offs, out):
         for b in range(B):
             gather("v", 0, b)
         xT0 = load_rows(xT[0])
-        interleave(("xT", 0), xT0, True, 0, 384)
-        quantize(("xT", 0), interleave(("xT", 0), xT0, False, 384, 512), E4M3)
+        quantize(("xT", 0), interleave(("xT", 0), xT0, True), E4M3)
         cast_table("v", 1, 0, 0, 1024, load_table(vT, 1, 0, 1024, False), True)
         cast_table("v", 1, 1024, 1024, 1536, load_table(vT, 1, 1024, 1536, False), False)
         last = load_table(vT, 1, 1536, T, True)
         cast_table("v", 1, 1536, 1536, 1728, last, True)
         cast_table("v", 1, 1536, 1728, T, last, False)
-        xm0 = load_rows(xm[0])
         xT1 = load_rows(xT[1])
+        xm0 = load_rows(xm[0])
         xm1 = load_rows(xm[1])
         head("w", 0)
         gather("v", 1, 0, 0, 256)
@@ -205,27 +225,27 @@ def tile_attend_gds_nce_kernel(tc, xT, wT, vT, wt, xm, offs, out):
         quantize_picked("v", 0, 0, 256)
         quantize_picked("v", 0, 256, 512)
         head("v", 0)
-        interleave(("xm", 0), xm0, True, 0, 128)
-        quantize(("xm", 0), interleave(("xm", 0), xm0, True, 128, 256), E4M3, 0, 256)
-        weigh(0)
+        quantize(("xm", 0), interleave(("xm", 0), xm0, True, 0, 128), E4M3, 0, 128)
+        weigh_on_vector(0)
         gradient(0, 0)
+        quantize(("xm", 0), interleave(("xm", 0), xm0, True, 128, 256), E4M3, 128, 256)
+        for c in range(0, 512, 128):
+            xT1_grouped = interleave(("xT", 1), xT1, c < 384, c, c + 128)
+        quantize(("xT", 1), xT1_grouped, E4M3)
         gather("v", 1, 1, 0, 256)
         gather("v", 1, 1, 256, 512)
         quantize_picked("v", 1)
-        for c in range(0, 512, 128):
-            xT1_grouped = interleave(("xT", 1), xT1, True, c, c + 128)
-        quantize(("xT", 1), xT1_grouped, E4M3)
-        gradient(0, 1)
         quantize(("xm", 0), interleave(("xm", 0), xm0, True, 256, 512), E4M3, 256, 512)
+        gradient(0, 1)
         head("w", 1)
         gradient(0, 2)
         head("v", 1)
+        quantize(("xm", 1), interleave(("xm", 1), xm1, True, 0, 128), E4M3, 0, 128)
+        weigh_on_scalar(1)
         gradient(0, 3)
-        quantize(("xm", 1), interleave(("xm", 1), xm1, True), E4M3)
-        weigh(1)
-        scatter(0, 0, 0, 256)
-        scatter(0, 0, 256, 512)
-        for k in range(1, D // P):
+        quantize(("xm", 1), interleave(("xm", 1), xm1, True, 128, 256), E4M3, 128, 256)
+        quantize(("xm", 1), interleave(("xm", 1), xm1, True, 256, 512), E4M3, 256, 512)
+        for k in range(D // P):
             scatter(0, k)
         for k in range(D // P):
             gradient(1, k)

@@ -9,28 +9,30 @@ FLOPS = 3 * 2 * B * N * D * R
 F32 = mybir.dt.float32
 BF16 = mybir.dt.bfloat16
 U32 = mybir.dt.uint32
+I32 = mybir.dt.int32
 U16 = mybir.dt.uint16
 U8 = mybir.dt.uint8
 E4M3 = mybir.dt.float8_e4m3fn_x4
 E5M2 = mybir.dt.float8_e5m2_x4
 MULT = mybir.AluOpType.mult
+ADD = mybir.AluOpType.add
 COPY = mybir.ActivationFunctionType.Copy
 TANH = mybir.ActivationFunctionType.Tanh
 
 P = 128
 PACK = 4
 LIST_COLS = N // 16
-BANK = 2048
+HALF = N // 2
 
 
 def tile_attend_gds_nce_kernel(tc, xT, wT, vT, wt, xm, offs, out):
     nc = tc.nc
     with ExitStack() as ctx:
         keep = ctx.enter_context(tc.tile_pool(name="keep", bufs=1))
-        raw = ctx.enter_context(tc.tile_pool(name="raw", bufs=5))
-        rows_pool = ctx.enter_context(tc.tile_pool(name="rows_pool", bufs=3))
+        raw = ctx.enter_context(tc.tile_pool(name="raw", bufs=8))
+        shared = ctx.enter_context(tc.tile_pool(name="shared", bufs=1))
         ring = ctx.enter_context(tc.tile_pool(name="ring", bufs=4))
-        score_psum = ctx.enter_context(tc.psum_pool(name="score_psum", bufs=3))
+        product_psum = ctx.enter_context(tc.psum_pool(name="product_psum", bufs=4))
         diff_psum = ctx.enter_context(tc.psum_pool(name="diff_psum", bufs=1))
 
         offsets = keep.tile([P, B * LIST_COLS], U16, name="offsets")
@@ -45,7 +47,7 @@ def tile_attend_gds_nce_kernel(tc, xT, wT, vT, wt, xm, offs, out):
         nc.scalar.activation(warm_out[:], warm[:], TANH)
         make_identity(nc, ident[:])
         for k, tile in enumerate(placed):
-            (nc.vector if k < 2 else nc.gpsimd).memset(tile[:], 0.0)
+            (nc.vector if k < 1 else nc.gpsimd).memset(tile[:], 0.0)
 
         def group_offsets(b, i0=0, i1=N):
             return offsets[:, b * LIST_COLS + i0 // 16 : b * LIST_COLS + i1 // 16]
@@ -53,15 +55,14 @@ def tile_attend_gds_nce_kernel(tc, xT, wT, vT, wt, xm, offs, out):
         windows = {}
         picked = {}
         codes = {}
+        after_g0 = {("v", 1): 0, ("xT", 1): 2048}
         for name in ("w", "v"):
             for u in range(2):
                 windows[name, u] = keep.tile([P, T, 2], BF16, name="win_%s%d" % (name, u), align_bytes=64)
-            for b in range(B):
-                picked[name, b] = keep.tile([P, N, 2], U32, name="picked_%s%d" % (name, b), align_bytes=64)
 
-        def load_table(table, u, c0, c1, last):
-            if last:
-                stage = keep.tile([P, 2, c1 - c0], F32, name="last_stage", tag="last_stage")
+        def load_table(table, u, c0, c1, tag=None):
+            if tag:
+                stage = keep.tile([P, 2, c1 - c0], F32, name=tag, tag=tag)
             else:
                 stage = raw.tile([P, 2, c1 - c0], F32, name="stage", tag="stage")
             rows = table.rearrange("(p j) c -> p j c", j=PACK)
@@ -76,39 +77,51 @@ def tile_attend_gds_nce_kernel(tc, xT, wT, vT, wt, xm, offs, out):
                 nc.vector.tensor_copy(windows[name, u][:, c0:c1, :], src)
 
         def load_rows(src):
-            stage = rows_pool.tile([P, PACK, 512], F32, name="rows", tag="rows")
+            stage = raw.tile([P, PACK, 512], F32, name="stage", tag="stage")
             nc.sync.dma_start(out=stage[:], in_=src.rearrange("(p j) c -> p j c", j=PACK))
             return stage
 
+        def window_words(name, u):
+            return windows[name, u][:].rearrange("p c e -> p (c e)").bitcast(U32)
+
         def gather(name, u, b, i0=0, i1=N):
-            window = windows[name, u][:].rearrange("p c e -> p (c e)").bitcast(U32)
-            nc.vector.tensor_copy(picked[name, b][:, i0:i1, u], window.indirect(group_offsets(b, i0, i1)))
+            if (name, b) not in picked:
+                tag = "picked_w%d" % b
+                picked[name, b] = keep.tile([P, N, 2], U32, name=tag, tag=tag, align_bytes=64)[:]
+            nc.vector.tensor_copy(picked[name, b][:, i0:i1, u], window_words(name, u).indirect(group_offsets(b, i0, i1)))
 
         def quantize(key, values, fmt, c0=0, c1=512):
             if key not in codes:
-                words = keep.tile([P, 512], U32, name="words_%s%d" % key, align_bytes=64)
+                if key in after_g0:
+                    words = shared.tile([P, 512], U32, name="words_%s%d" % key, align_bytes=64, offset=after_g0[key])
+                else:
+                    words = keep.tile([P, 512], U32, name="words_%s%d" % key, align_bytes=64)
                 scales = keep.tile([P, 512], U8, name="scales_%s%d" % key, align_bytes=64)
                 codes[key] = (words, scales, fmt)
             words, scales, fmt = codes[key]
             nc.vector.quantize_mx(out=words[:, c0:c1].bitcast(fmt), scales=scales[:, c0:c1], in_=values[:, PACK * c0 : PACK * c1])
 
         def quantize_picked(name, b, c0=0, c1=512):
-            quantize((name, b), picked[name, b][:].rearrange("p n u -> p (n u)").bitcast(BF16), E4M3, c0, c1)
+            quantize((name, b), picked[name, b].rearrange("p n u -> p (n u)").bitcast(BF16), E4M3, c0, c1)
 
         grouped = {}
 
-        def interleave(key, stage, on_scalar, c0=0, c1=512):
+        def interleave(key, stage, engine, c0=0, c1=512, tag=None):
             if key not in grouped:
-                grouped[key] = keep.tile([P, 512, PACK], BF16, name="grouped_%s%d" % key, align_bytes=64)
+                tag = tag or "grouped_%s%d" % key
+                grouped[key] = keep.tile([P, 512, PACK], BF16, name=tag, tag=tag, align_bytes=64)
             src = stage[:, :, c0:c1].rearrange("p j (c i) -> p c j i", i=4)
             dst = grouped[key][:, c0:c1, :].rearrange("p (c i) j -> p c j i", i=4)
-            if on_scalar:
+            if engine == "scalar":
                 nc.scalar.copy(dst, src)
-            else:
+            elif engine == "vector":
                 nc.vector.tensor_copy(dst, src)
+            else:
+                nc.gpsimd.tensor_scalar(grouped[key][:, c0:c1, :], stage[:, :, c0:c1].rearrange("p j c -> p c j"), 1.0, 0.0, MULT, ADD)
             return grouped[key][:].rearrange("p c j -> p (c j)")
 
-        def product(bank, stationary, k, moving):
+        def product(stationary, k, moving):
+            bank = product_psum.tile([P, 512], F32, name="bank", tag="bank")
             s_words, s_scales, s_fmt = codes[stationary]
             m_words, m_scales, m_fmt = codes[moving]
             cols = slice(k * P, (k + 1) * P)
@@ -125,129 +138,148 @@ def tile_attend_gds_nce_kernel(tc, xT, wT, vT, wt, xm, offs, out):
 
         diffs = {}
 
-        def head(name, b):
+        def diff_bank(b, q):
+            if (b, q) not in diffs:
+                diffs[b, q] = diff_psum.tile([P, PACK, P], F32, name="diff%d" % q, tag="diff%d" % q)
+            return diffs[b, q]
+
+        def score(name, b, c, th):
             first = name == "w"
-            held = keep.tile([P, 4, PACK, P], F32, name="last_stage", tag="last_stage") if first else None
-            if first and b == 0:
-                for q in range(4):
-                    diffs[b, q] = diff_psum.tile([P, PACK, P], F32, name="diff%d" % q, offset=q * BANK)
-            if first and b == 1:
-                wide = diff_psum.tile([P, 4, PACK, P], F32, name="wide", offset=BANK)
-                for q in range(4):
-                    diffs[b, q] = wide[:, q]
-            for c in range(4):
-                bank = product(score_psum.tile([P, R], F32, name="score", tag="score"), (name, b), c, ("xT", b))
-                if held is not None:
-                    th = held[:, c]
-                else:
-                    th = ring.tile([P, PACK, P], F32, name="th", tag="th")
-                nc.scalar.activation(th[:, :, :], bank[:].rearrange("p (m t) -> p t m", t=PACK), TANH, scale=0.5 if first else -0.5)
-                for t in range(PACK):
-                    bank_index, place = (c, t) if b == 0 else (t, c)
-                    nc.tensor.matmul(
-                        diffs[b, bank_index][:, place, :], th[:, t, :], ident[:], is_transpose=True,
-                        start=first and place == 0, stop=(not first) and place == PACK - 1,
-                    )
-
-        def weigh_on_vector(b):
-            g = keep.tile([P, N, PACK], BF16, name="g%d" % b, align_bytes=64)
-            for c in range(4):
-                nc.vector.tensor_tensor(
-                    g[:, c * P : (c + 1) * P, :],
-                    diffs[b, c][:].rearrange("p t i -> p i t"),
-                    half_weights[:, b : b + 1, :].to_broadcast([P, P, PACK]),
-                    MULT,
-                )
-                if c == 2:
-                    quantize(("g", b), g[:].rearrange("p n t -> p (n t)"), E5M2, 0, 256)
-            quantize(("g", b), g[:].rearrange("p n t -> p (n t)"), E5M2, 256, 512)
-
-        def weigh_on_scalar(b):
-            planes = keep.tile([P, PACK, N], BF16, name="g_planes", tag="g_planes", align_bytes=64)
+            bank = product((name, b), c, ("xT", b))
+            nc.scalar.activation(th, bank[:].rearrange("p (m t) -> p t m", t=PACK), TANH, scale=0.5 if first else -0.5)
             for t in range(PACK):
-                nc.scalar.activation(planes[:, t, :], diffs[b, t].rearrange("p c i -> p (c i)"), COPY, scale=half_weights[:, b, t : t + 1])
-            quantize(("g", b), interleave(("g", b), planes, True), E5M2)
+                if b == 0:
+                    q, place = c, t
+                    opens, closes = t == 0, t == PACK - 1
+                else:
+                    q, place = 2 * (c // 2) + t // 2, 2 * (t % 2) + c % 2
+                    opens, closes = c % 2 == 0 and t % 2 == 0, c % 2 == 1 and t % 2 == 1
+                nc.tensor.matmul(
+                    diff_bank(b, q)[:, place, :], th[:, t, :], ident[:], is_transpose=True,
+                    start=first and opens, stop=(not first) and closes,
+                )
+
+        def ring_th():
+            return ring.tile([P, PACK, P], F32, name="th", tag="th")[:]
 
         dws = {}
 
-        def gradient(b, k):
-            if (b, k) == (0, 0):
-                bank = diff_psum.tile([P, N], F32, name="first_grad", offset=4 * BANK)
+        def leave(b, k, bank, i0, i1, offset=None):
+            if offset is not None:
+                dw = shared.tile([P, i1 - i0], F32, name="held_dw", align_bytes=64, offset=offset)
             else:
-                bank = diff_psum.tile([P, N], F32, name="grad", tag="grad", offset=0)
-            product(bank, ("xm", b), k, ("g", b))
-            halves = b == 0 and k in (0, 3)
-            for i0, i1 in ((0, 256), (256, N)) if halves else ((0, N),):
-                if (b, k, i0) == (0, 3, 256):
-                    dw = keep.tile([P, i1 - i0], F32, name="g_planes", tag="g_planes", align_bytes=64)
-                else:
-                    dw = ring.tile([P, i1 - i0], F32, name="dw", tag="dw")
-                nc.scalar.copy(dw[:], bank[:, i0:i1])
-                dws.setdefault((b, k), []).append((i0, i1, dw))
+                dw = ring.tile([P, i1 - i0], F32, name="dw", tag="dw")
+            nc.scalar.copy(dw[:], bank[:, i0:i1])
+            dws.setdefault((b, k), []).append((i0, i1, dw))
 
-        def scatter(b, k):
-            for i0, i1, dw in dws[b, k]:
-                nc.vector.tensor_copy(placed[k][:].indirect(group_offsets(b, i0, i1)), dw[:])
+        def gradient(b, k, pieces):
+            bank = product(("xm", b), k, ("g", b))
+            for i0, i1, offset in pieces:
+                leave(b, k, bank, i0, i1, offset)
 
-        tables = {"w": wT, "v": vT}
+        def scatter(b, k, piece):
+            i0, i1, dw = dws[b, k][piece]
+            nc.vector.tensor_copy(placed[k][:].indirect(group_offsets(b, i0, i1)), dw[:])
 
-        def bring(name, u):
-            for c0 in (0, 1024):
-                cast_table(name, u, c0, c0, c0 + 1024, load_table(tables[name], u, c0, c0 + 1024, False), True)
+        def bring(table, name, u, c0, c1, split, tag=None):
+            stage = load_table(table, u, c0, c1, tag)
+            if split > c0:
+                cast_table(name, u, c0, c0, split, stage, True)
+            if split < c1:
+                cast_table(name, u, c0, split, c1, stage, False)
 
-        bring("w", 0)
+        bring(wT, "w", 0, 0, 1024, 1024)
         nc.sync.dma_start(offsets[:], offs)
+        bring(wT, "w", 0, 1024, T, 1408)
         for b in range(B):
             gather("w", 0, b)
-        bring("w", 1)
+        bring(wT, "w", 1, 0, 1024, 1024)
         nc.sync.dma_start(out=weights[:], in_=wt.rearrange("b (p t) o -> p b (t o)", t=PACK))
         nc.vector.tensor_scalar_mul(half_weights[:], weights[:], 0.5)
+        bring(wT, "w", 1, 1024, T, 1408)
         for b in range(B):
             gather("w", 1, b)
-        for b in range(B):
-            quantize_picked("w", b)
-        bring("v", 0)
-        for b in range(B):
-            gather("v", 0, b)
-        xT0 = load_rows(xT[0])
-        quantize(("xT", 0), interleave(("xT", 0), xT0, True), E4M3)
-        cast_table("v", 1, 0, 0, 1024, load_table(vT, 1, 0, 1024, False), True)
-        cast_table("v", 1, 1024, 1024, 1536, load_table(vT, 1, 1024, 1536, False), False)
-        last = load_table(vT, 1, 1536, T, True)
-        cast_table("v", 1, 1536, 1536, 1728, last, True)
-        cast_table("v", 1, 1536, 1728, T, last, False)
+        quantize_picked("w", 0)
+        quantize(("xT", 0), interleave(("xT", 0), load_rows(xT[0]), "scalar"), E4M3)
+        quantize_picked("w", 1)
+        bring(vT, "v", 0, 0, 1024, 1024, "held")
+        held = keep.tile([P, 4, PACK, P], F32, name="held", tag="held")
+        for c in range(4):
+            score("w", 0, c, held[:, c])
+        bring(vT, "v", 0, 1024, T, 1024)
+        teacher = keep.tile([P, 3 * N], U32, name="teacher", align_bytes=64)
+        picked["v", 0] = teacher[:, N : 3 * N].rearrange("p (n u) -> p n u", u=2)
+        gather("v", 0, 0)
+        nc.vector.tensor_copy(teacher[:, 0:N], window_words("v", 0).indirect(group_offsets(1)))
+        bring(vT, "v", 1, 0, 1024, 1024)
+        bring(vT, "v", 1, 1024, 1536, 1024)
+        bring(vT, "v", 1, 1536, T, 1728)
         xT1 = load_rows(xT[1])
         xm0 = load_rows(xm[0])
         xm1 = load_rows(xm[1])
-        head("w", 0)
-        gather("v", 1, 0, 0, 256)
-        gather("v", 1, 0, 256, 512)
-        quantize_picked("v", 0, 0, 256)
-        quantize_picked("v", 0, 256, 512)
-        head("v", 0)
-        quantize(("xm", 0), interleave(("xm", 0), xm0, True, 0, 128), E4M3, 0, 128)
-        weigh_on_vector(0)
-        gradient(0, 0)
-        quantize(("xm", 0), interleave(("xm", 0), xm0, True, 128, 256), E4M3, 128, 256)
+        gather("v", 1, 0, 0, HALF)
+        gather("v", 1, 0, HALF, N)
+        quantize_picked("v", 0, 0, HALF)
+        quantize_picked("v", 0, HALF, N)
+        for c in range(4):
+            score("v", 0, c, ring_th())
+        nc.vector.tensor_copy(teacher[:, 2 * N : 3 * N], window_words("v", 1).indirect(group_offsets(1)))
+        picked["v", 1] = keep.tile([P, N, 2], U32, name="picked_v1", align_bytes=64)[:]
+        nc.vector.tensor_copy(
+            picked["v", 1].bitcast(I32), teacher[:].bitcast(I32).rearrange("p (u n) -> p n u", u=3)[:, :, ::2]
+        )
+        g0 = shared.tile([P, N, PACK], BF16, name="g0", align_bytes=64, offset=0)
+        g0_flat = g0[:].rearrange("p n t -> p (n t)")
+        for c in range(4):
+            nc.vector.tensor_tensor(
+                g0[:, c * P : (c + 1) * P, :],
+                diffs[0, c][:].rearrange("p t i -> p i t"),
+                half_weights[:, 0:1, :].to_broadcast([P, P, PACK]),
+                MULT,
+            )
+            if c == 2:
+                quantize(("g", 0), g0_flat, E5M2, 0, HALF)
+        quantize(("xm", 0), interleave(("xm", 0), xm0, "scalar", 0, 128), E4M3, 0, 128)
+        quantize(("g", 0), g0_flat, E5M2, HALF, N)
+        gradient(0, 0, ((0, HALF, None), (HALF, N, None)))
         for c in range(0, 512, 128):
-            xT1_grouped = interleave(("xT", 1), xT1, c < 384, c, c + 128)
+            xT1_grouped = interleave(("xT", 1), xT1, "scalar", c, c + 128)
         quantize(("xT", 1), xT1_grouped, E4M3)
-        gather("v", 1, 1, 0, 256)
-        gather("v", 1, 1, 256, 512)
         quantize_picked("v", 1)
-        quantize(("xm", 0), interleave(("xm", 0), xm0, True, 256, 512), E4M3, 256, 512)
-        gradient(0, 1)
-        head("w", 1)
-        gradient(0, 2)
-        head("v", 1)
-        quantize(("xm", 1), interleave(("xm", 1), xm1, True, 0, 128), E4M3, 0, 128)
-        weigh_on_scalar(1)
-        gradient(0, 3)
-        quantize(("xm", 1), interleave(("xm", 1), xm1, True, 128, 256), E4M3, 128, 256)
-        quantize(("xm", 1), interleave(("xm", 1), xm1, True, 256, 512), E4M3, 256, 512)
+        quantize(("xm", 0), interleave(("xm", 0), xm0, "scalar", 128, 256), E4M3, 128, 256)
+        gradient(0, 1, ((0, N, None),))
+        quantize(("xm", 0), interleave(("xm", 0), xm0, "scalar", 256, 512), E4M3, 256, 512)
+        for c in range(4):
+            score("w", 1, c, ring_th())
+            score("v", 1, c, ring_th())
+            if c == 1:
+                gradient(0, 2, ((0, N, None),))
+        last_bank = product(("xm", 0), 3, ("g", 0))
+        leave(0, 3, last_bank, 0, HALF)
+        planes = shared.tile([P, PACK, N], BF16, name="g_planes", align_bytes=64, offset=4096)
+        for h in range(2):
+            for t in range(PACK):
+                src = diffs[1, 2 * h + t // 2][:, 2 * (t % 2) : 2 * (t % 2) + 2, :].rearrange("p c i -> p (c i)")
+                nc.scalar.activation(planes[:, t, h * HALF : (h + 1) * HALF], src, COPY, scale=half_weights[:, 1, t : t + 1])
+            quantize(("g", 1), interleave(("g", 1), planes, "scalar", h * HALF, (h + 1) * HALF), E5M2, h * HALF, (h + 1) * HALF)
+        leave(0, 3, last_bank, HALF, N, 4096)
+        quantize(("xm", 1), interleave(("xm", 1), xm1, "scalar", 0, 128), E4M3, 0, 128)
+        late = shared.tile([P, 384, PACK], BF16, name="late", align_bytes=64, offset=5120)
         for k in range(D // P):
-            scatter(0, k)
+            for piece in range(len(dws[0, k])):
+                scatter(0, k, piece)
         for k in range(D // P):
-            gradient(1, k)
-            scatter(1, k)
+            if k < 3:
+                c = k * P
+                nc.scalar.copy(
+                    late[:, c : c + P, :].rearrange("p (c i) j -> p c j i", i=4),
+                    xm1[:, :, c + P : c + 2 * P].rearrange("p j (c i) -> p c j i", i=4),
+                )
+                words, scales, fmt = codes["xm", 1]
+                nc.vector.quantize_mx(
+                    out=words[:, c + P : c + 2 * P].bitcast(fmt), scales=scales[:, c + P : c + 2 * P],
+                    in_=late[:, c : c + P, :].rearrange("p c j -> p (c j)"),
+                )
+            gradient(1, k, ((0, N, None),))
+            scatter(1, k, 0)
             nc.sync.dma_start(out=out[k * P : (k + 1) * P, :], in_=placed[k][:])

@@ -46,8 +46,8 @@ def tile_attend_gds_nce_kernel(tc, xT, wT, vT, wt, xm, offs, out):
         nc.gpsimd.memset(warm[:], 0.0)
         nc.scalar.activation(warm_out[:], warm[:], TANH)
         make_identity(nc, ident[:])
-        for k, tile in enumerate(placed):
-            (nc.vector if k < 1 else nc.gpsimd).memset(tile[:], 0.0)
+        for tile in placed:
+            nc.vector.memset(tile[:], 0.0)
 
         def group_offsets(b, i0=0, i1=N):
             return offsets[:, b * LIST_COLS + i0 // 16 : b * LIST_COLS + i1 // 16]

@@ -29,7 +29,7 @@ def tile_attend_gds_nce_kernel(tc, xT, wT, vT, wt, xm, offs, out):
     nc = tc.nc
     with ExitStack() as ctx:
         keep = ctx.enter_context(tc.tile_pool(name="keep", bufs=1))
-        raw = ctx.enter_context(tc.tile_pool(name="raw", bufs=8))
+        raw = ctx.enter_context(tc.tile_pool(name="raw", bufs=7))
         shared = ctx.enter_context(tc.tile_pool(name="shared", bufs=1))
         ring = ctx.enter_context(tc.tile_pool(name="ring", bufs=4))
         product_psum = ctx.enter_context(tc.psum_pool(name="product_psum", bufs=4))
@@ -76,9 +76,9 @@ def tile_attend_gds_nce_kernel(tc, xT, wT, vT, wt, xm, offs, out):
             else:
                 nc.vector.tensor_copy(windows[name, u][:, c0:c1, :], src)
 
-        def load_rows(src):
-            stage = raw.tile([P, PACK, 512], F32, name="stage", tag="stage")
-            nc.sync.dma_start(out=stage[:], in_=src.rearrange("(p j) c -> p j c", j=PACK))
+        def load_rows(src, c0=0, c1=512):
+            stage = raw.tile([P, PACK, c1 - c0], F32, name="stage", tag="stage")
+            nc.sync.dma_start(out=stage[:], in_=src.rearrange("(p j) c -> p j c", j=PACK)[:, :, c0:c1])
             return stage
 
         def window_words(name, u):
@@ -106,11 +106,11 @@ def tile_attend_gds_nce_kernel(tc, xT, wT, vT, wt, xm, offs, out):
 
         grouped = {}
 
-        def interleave(key, stage, engine, c0=0, c1=512, tag=None):
+        def interleave(key, stage, engine, c0=0, c1=512, tag=None, base=0):
             if key not in grouped:
                 tag = tag or "grouped_%s%d" % key
                 grouped[key] = keep.tile([P, 512, PACK], BF16, name=tag, tag=tag, align_bytes=64)
-            src = stage[:, :, c0:c1].rearrange("p j (c i) -> p c j i", i=4)
+            src = stage[:, :, c0 - base : c1 - base].rearrange("p j (c i) -> p c j i", i=4)
             dst = grouped[key][:, c0:c1, :].rearrange("p (c i) j -> p c j i", i=4)
             if engine == "scalar":
                 nc.scalar.copy(dst, src)
@@ -194,27 +194,29 @@ def tile_attend_gds_nce_kernel(tc, xT, wT, vT, wt, xm, offs, out):
         for b in range(B):
             gather("w", 0, b)
         bring(wT, "w", 1, 0, 1024, 1024)
-        nc.sync.dma_start(out=weights[:], in_=wt.rearrange("b (p t) o -> p b (t o)", t=PACK))
-        nc.vector.tensor_scalar_mul(half_weights[:], weights[:], 0.5)
         bring(wT, "w", 1, 1024, T, 1408)
         for b in range(B):
             gather("w", 1, b)
         quantize_picked("w", 0)
         quantize(("xT", 0), interleave(("xT", 0), load_rows(xT[0]), "scalar"), E4M3)
         quantize_picked("w", 1)
-        bring(vT, "v", 0, 0, 1024, 1024, "held")
-        held = keep.tile([P, 4, PACK, P], F32, name="held", tag="held")
-        for c in range(4):
-            score("w", 0, c, held[:, c])
-        bring(vT, "v", 0, 1024, T, 1024)
+        bring(vT, "v", 0, 0, 1024, 1024)
+        bring(vT, "v", 0, 1024, T, 1408, "early")
+        early = keep.tile([P, 3, PACK, P], F32, name="early", tag="early")
+        for c in range(3):
+            score("w", 0, c, early[:, c])
         teacher = keep.tile([P, 3 * N], U32, name="teacher", align_bytes=64)
         picked["v", 0] = teacher[:, N : 3 * N].rearrange("p (n u) -> p n u", u=2)
         gather("v", 0, 0)
         nc.vector.tensor_copy(teacher[:, 0:N], window_words("v", 0).indirect(group_offsets(1)))
-        bring(vT, "v", 1, 0, 1024, 1024)
+        bring(vT, "v", 1, 0, 1024, 768)
         bring(vT, "v", 1, 1024, 1536, 1024)
-        bring(vT, "v", 1, 1536, T, 1728)
-        xT1 = load_rows(xT[1])
+        bring(vT, "v", 1, 1536, T, 1728, "held")
+        held = keep.tile([P, PACK, P], F32, name="held", tag="held")
+        score("w", 0, 3, held[:])
+        nc.sync.dma_start(out=weights[:], in_=wt.rearrange("b (p t) o -> p b (t o)", t=PACK))
+        nc.gpsimd.tensor_scalar(half_weights[:], weights[:], 0.5, 0.0, MULT, ADD)
+        xT1 = [load_rows(xT[1], c, c + 256) for c in (0, 256)]
         xm0 = load_rows(xm[0])
         xm1 = load_rows(xm[1])
         gather("v", 1, 0, 0, HALF)
@@ -243,7 +245,7 @@ def tile_attend_gds_nce_kernel(tc, xT, wT, vT, wt, xm, offs, out):
         quantize(("g", 0), g0_flat, E5M2, HALF, N)
         gradient(0, 0, ((0, HALF, None), (HALF, N, None)))
         for c in range(0, 512, 128):
-            xT1_grouped = interleave(("xT", 1), xT1, "scalar", c, c + 128)
+            xT1_grouped = interleave(("xT", 1), xT1[c // 256], "scalar", c, c + 128, base=c // 256 * 256)
         quantize(("xT", 1), xT1_grouped, E4M3)
         quantize_picked("v", 1)
         quantize(("xm", 0), interleave(("xm", 0), xm0, "scalar", 128, 256), E4M3, 128, 256)

@@ -251,6 +251,9 @@ def tile_attend_gds_nce_kernel(tc, xT, wT, vT, wt, xm, offs, out):
         quantize(("xm", 0), interleave(("xm", 0), xm0, "scalar", 128, 256), E4M3, 128, 256)
         gradient(0, 1, ((0, N, None),))
         quantize(("xm", 0), interleave(("xm", 0), xm0, "scalar", 256, 512), E4M3, 256, 512)
+        for c in range(0, 512, 128):
+            xm1_grouped = interleave(("xm", 1), xm1, "gpsimd", c, c + 128, tag="grouped_xm0")
+        quantize(("xm", 1), xm1_grouped, E4M3)
         for c in range(4):
             score("w", 1, c, ring_th())
             score("v", 1, c, ring_th())
@@ -263,25 +266,12 @@ def tile_attend_gds_nce_kernel(tc, xT, wT, vT, wt, xm, offs, out):
             for t in range(PACK):
                 src = diffs[1, 2 * h + t // 2][:, 2 * (t % 2) : 2 * (t % 2) + 2, :].rearrange("p c i -> p (c i)")
                 nc.scalar.activation(planes[:, t, h * HALF : (h + 1) * HALF], src, COPY, scale=half_weights[:, 1, t : t + 1])
-            quantize(("g", 1), interleave(("g", 1), planes, "scalar", h * HALF, (h + 1) * HALF), E5M2, h * HALF, (h + 1) * HALF)
+            quantize(("g", 1), interleave(("g", 1), planes, "scalar" if h else "gpsimd", h * HALF, (h + 1) * HALF), E5M2, h * HALF, (h + 1) * HALF)
         leave(0, 3, last_bank, HALF, N, 4096)
-        quantize(("xm", 1), interleave(("xm", 1), xm1, "scalar", 0, 128), E4M3, 0, 128)
-        late = shared.tile([P, 384, PACK], BF16, name="late", align_bytes=64, offset=5120)
         for k in range(D // P):
             for piece in range(len(dws[0, k])):
                 scatter(0, k, piece)
         for k in range(D // P):
-            if k < 3:
-                c = k * P
-                nc.scalar.copy(
-                    late[:, c : c + P, :].rearrange("p (c i) j -> p c j i", i=4),
-                    xm1[:, :, c + P : c + 2 * P].rearrange("p j (c i) -> p c j i", i=4),
-                )
-                words, scales, fmt = codes["xm", 1]
-                nc.vector.quantize_mx(
-                    out=words[:, c + P : c + 2 * P].bitcast(fmt), scales=scales[:, c + P : c + 2 * P],
-                    in_=late[:, c : c + P, :].rearrange("p c j -> p (c j)"),
-                )
             gradient(1, k, ((0, N, None),))
             scatter(1, k, 0)
             nc.sync.dma_start(out=out[k * P : (k + 1) * P, :], in_=placed[k][:])

@@ -9,7 +9,6 @@ FLOPS = 3 * 2 * B * N * D * R
 F32 = mybir.dt.float32
 BF16 = mybir.dt.bfloat16
 U32 = mybir.dt.uint32
-I32 = mybir.dt.int32
 U16 = mybir.dt.uint16
 U8 = mybir.dt.uint8
 E4M3 = mybir.dt.float8_e4m3fn_x4
@@ -55,7 +54,12 @@ def tile_attend_gds_nce_kernel(tc, xT, wT, vT, wt, xm, offs, out):
         windows = {}
         picked = {}
         codes = {}
-        after_g0 = {("v", 1): 0, ("xT", 1): 2048}
+        after_g0 = {("v", 1): 0}
+        padded_words = keep.tile([P, HALF + N], U32, name="padded_words", align_bytes=64)
+        padded_scales = keep.tile([P, HALF + N], U8, name="padded_scales", align_bytes=64)
+        nc.vector.memset(padded_words[:, 0:HALF], 0)
+        nc.vector.memset(padded_scales[:, 0:HALF], 0)
+        codes["g", 0] = (padded_words[:, HALF:], padded_scales[:, HALF:], E5M2)
         for name in ("w", "v"):
             for u in range(2):
                 windows[name, u] = keep.tile([P, T, 2], BF16, name="win_%s%d" % (name, u), align_bytes=64)
@@ -164,12 +168,12 @@ def tile_attend_gds_nce_kernel(tc, xT, wT, vT, wt, xm, offs, out):
 
         dws = {}
 
-        def leave(b, k, bank, i0, i1, offset=None):
+        def leave(b, k, bank, i0, i1, offset=None, shift=0):
             if offset is not None:
                 dw = shared.tile([P, i1 - i0], F32, name="held_dw", align_bytes=64, offset=offset)
             else:
                 dw = ring.tile([P, i1 - i0], F32, name="dw", tag="dw")
-            nc.scalar.copy(dw[:], bank[:, i0:i1])
+            nc.scalar.copy(dw[:], bank[:, shift + i0 : shift + i1])
             dws.setdefault((b, k), []).append((i0, i1, dw))
 
         def gradient(b, k, pieces):
@@ -219,6 +223,9 @@ def tile_attend_gds_nce_kernel(tc, xT, wT, vT, wt, xm, offs, out):
         xT1 = [load_rows(xT[1], c, c + 256) for c in (0, 256)]
         xm0 = load_rows(xm[0])
         xm1 = load_rows(xm[1])
+        grouped["xT", 1] = shared.tile([P, 512, PACK], BF16, name="grouped_xT1", align_bytes=64, offset=0)
+        for c in range(0, 512, 128):
+            xT1_grouped = interleave(("xT", 1), xT1[c // 256], "scalar", c, c + 128, base=c // 256 * 256)
         gather("v", 1, 0, 0, HALF)
         gather("v", 1, 0, HALF, N)
         quantize_picked("v", 0, 0, HALF)
@@ -226,38 +233,42 @@ def tile_attend_gds_nce_kernel(tc, xT, wT, vT, wt, xm, offs, out):
         for c in range(4):
             score("v", 0, c, ring_th())
         nc.vector.tensor_copy(teacher[:, 2 * N : 3 * N], window_words("v", 1).indirect(group_offsets(1)))
-        picked["v", 1] = keep.tile([P, N, 2], U32, name="picked_v1", align_bytes=64)[:]
-        nc.vector.tensor_copy(
-            picked["v", 1].bitcast(I32), teacher[:].bitcast(I32).rearrange("p (u n) -> p n u", u=3)[:, :, ::2]
-        )
+        quantize(("xT", 1), xT1_grouped, E4M3)
         g0 = shared.tile([P, N, PACK], BF16, name="g0", align_bytes=64, offset=0)
         g0_flat = g0[:].rearrange("p n t -> p (n t)")
-        for c in range(4):
+
+        def weigh(c):
             nc.vector.tensor_tensor(
                 g0[:, c * P : (c + 1) * P, :],
                 diffs[0, c][:].rearrange("p t i -> p i t"),
                 half_weights[:, 0:1, :].to_broadcast([P, P, PACK]),
                 MULT,
             )
-            if c == 2:
-                quantize(("g", 0), g0_flat, E5M2, 0, HALF)
+
+        weigh(0)
+        weigh(1)
+        quantize(("g", 0), g0_flat, E5M2, 0, HALF)
         quantize(("xm", 0), interleave(("xm", 0), xm0, "scalar", 0, 128), E4M3, 0, 128)
+        codes["g_first", 0] = (padded_words[:, 0:N], padded_scales[:, 0:N], E5M2)
+        leave(0, 0, product(("xm", 0), 0, ("g_first", 0)), 0, HALF, shift=HALF)
+        weigh(2)
+        weigh(3)
         quantize(("g", 0), g0_flat, E5M2, HALF, N)
-        gradient(0, 0, ((0, HALF, None), (HALF, N, None)))
-        for c in range(0, 512, 128):
-            xT1_grouped = interleave(("xT", 1), xT1[c // 256], "scalar", c, c + 128, base=c // 256 * 256)
-        quantize(("xT", 1), xT1_grouped, E4M3)
-        quantize_picked("v", 1)
+        gradient(0, 0, ((HALF, N, None),))
+        picked["v", 1] = keep.tile([P, N, 2], U32, name="picked_v1", align_bytes=64)[:]
+        nc.scalar.copy(picked["v", 1], teacher[:].rearrange("p (u n) -> p n u", u=3)[:, :, ::2])
         quantize(("xm", 0), interleave(("xm", 0), xm0, "scalar", 128, 256), E4M3, 128, 256)
+        quantize_picked("v", 1)
         gradient(0, 1, ((0, N, None),))
         quantize(("xm", 0), interleave(("xm", 0), xm0, "scalar", 256, 512), E4M3, 256, 512)
         for c in range(0, 512, 128):
             xm1_grouped = interleave(("xm", 1), xm1, "gpsimd", c, c + 128, tag="grouped_xm0")
         quantize(("xm", 1), xm1_grouped, E4M3)
-        for c in range(4):
-            score("w", 1, c, ring_th())
-            score("v", 1, c, ring_th())
-            if c == 1:
+        for h in range(2):
+            for name in ("w", "v"):
+                for c in (2 * h, 2 * h + 1):
+                    score(name, 1, c, ring_th())
+            if h == 0:
                 gradient(0, 2, ((0, N, None),))
         last_bank = product(("xm", 0), 3, ("g", 0))
         leave(0, 3, last_bank, 0, HALF)
@@ -271,7 +282,13 @@ def tile_attend_gds_nce_kernel(tc, xT, wT, vT, wt, xm, offs, out):
         for k in range(D // P):
             for piece in range(len(dws[0, k])):
                 scatter(0, k, piece)
-        for k in range(D // P):
+        first_bank = product(("xm", 1), 0, ("g", 1))
+        leave(1, 0, first_bank, 0, HALF)
+        gradient(1, 1, ((0, N, None),))
+        leave(1, 0, first_bank, HALF, N)
+        for k in (2, 3):
             gradient(1, k, ((0, N, None),))
-            scatter(1, k, 0)
-            nc.sync.dma_start(out=out[k * P : (k + 1) * P, :], in_=placed[k][:])
+        for k, piece in ((0, 0), (1, 0), (0, 1), (2, 0), (3, 0)):
+            scatter(1, k, piece)
+            if piece == len(dws[1, k]) - 1:
+                nc.sync.dma_start(out=out[k * P : (k + 1) * P, :], in_=placed[k][:])

@@ -9,6 +9,7 @@ FLOPS = 3 * 2 * B * N * D * R
 F32 = mybir.dt.float32
 BF16 = mybir.dt.bfloat16
 U32 = mybir.dt.uint32
+I32 = mybir.dt.int32
 U16 = mybir.dt.uint16
 U8 = mybir.dt.uint8
 E4M3 = mybir.dt.float8_e4m3fn_x4
@@ -36,7 +37,6 @@ def tile_attend_gds_nce_kernel(tc, xT, wT, vT, wt, xm, offs, out):
 
         offsets = keep.tile([P, B * LIST_COLS], U16, name="offsets")
         weights = keep.tile([P, B, PACK], F32, name="weights")
-        half_weights = keep.tile([P, B, PACK], F32, name="half_weights")
         ident = keep.tile([P, P], F32, name="ident")
         placed = [keep.tile([P, T], F32, name="placed%d" % k) for k in range(D // P)]
         warm = keep.tile([P, 8], F32, name="warm")
@@ -54,11 +54,10 @@ def tile_attend_gds_nce_kernel(tc, xT, wT, vT, wt, xm, offs, out):
         windows = {}
         picked = {}
         codes = {}
-        after_g0 = {("v", 1): 0}
         padded_words = keep.tile([P, HALF + N], U32, name="padded_words", align_bytes=64)
         padded_scales = keep.tile([P, HALF + N], U8, name="padded_scales", align_bytes=64)
-        nc.vector.memset(padded_words[:, 0:HALF], 0)
-        nc.vector.memset(padded_scales[:, 0:HALF], 0)
+        nc.gpsimd.memset(padded_words[:, 0:HALF], 0)
+        nc.gpsimd.memset(padded_scales[:, 0:HALF], 0)
         codes["g", 0] = (padded_words[:, HALF:], padded_scales[:, HALF:], E5M2)
         for name in ("w", "v"):
             for u in range(2):
@@ -94,35 +93,23 @@ def tile_attend_gds_nce_kernel(tc, xT, wT, vT, wt, xm, offs, out):
                 picked[name, b] = keep.tile([P, N, 2], U32, name=tag, tag=tag, align_bytes=64)[:]
             nc.vector.tensor_copy(picked[name, b][:, i0:i1, u], window_words(name, u).indirect(group_offsets(b, i0, i1)))
 
-        def quantize(key, values, fmt, c0=0, c1=512):
+        def flat(view):
+            return view.rearrange("p a b -> p (a b)")
+
+        def quantize(key, values, fmt, c0):
             if key not in codes:
-                if key in after_g0:
-                    words = shared.tile([P, 512], U32, name="words_%s%d" % key, align_bytes=64, offset=after_g0[key])
-                else:
-                    words = keep.tile([P, 512], U32, name="words_%s%d" % key, align_bytes=64)
+                words = keep.tile([P, 512], U32, name="words_%s%d" % key, align_bytes=64)
                 scales = keep.tile([P, 512], U8, name="scales_%s%d" % key, align_bytes=64)
                 codes[key] = (words, scales, fmt)
             words, scales, fmt = codes[key]
-            nc.vector.quantize_mx(out=words[:, c0:c1].bitcast(fmt), scales=scales[:, c0:c1], in_=values[:, PACK * c0 : PACK * c1])
+            c1 = c0 + values.shape[1] // PACK
+            nc.vector.quantize_mx(out=words[:, c0:c1].bitcast(fmt), scales=scales[:, c0:c1], in_=values)
 
-        def quantize_picked(name, b, c0=0, c1=512):
-            quantize((name, b), picked[name, b].rearrange("p n u -> p (n u)").bitcast(BF16), E4M3, c0, c1)
+        def interleave(dst, src):
+            nc.scalar.copy(dst.rearrange("p (c i) j -> p c j i", i=4), src.rearrange("p j (c i) -> p c j i", i=4))
 
-        grouped = {}
-
-        def interleave(key, stage, engine, c0=0, c1=512, tag=None, base=0):
-            if key not in grouped:
-                tag = tag or "grouped_%s%d" % key
-                grouped[key] = keep.tile([P, 512, PACK], BF16, name=tag, tag=tag, align_bytes=64)
-            src = stage[:, :, c0 - base : c1 - base].rearrange("p j (c i) -> p c j i", i=4)
-            dst = grouped[key][:, c0:c1, :].rearrange("p (c i) j -> p c j i", i=4)
-            if engine == "scalar":
-                nc.scalar.copy(dst, src)
-            elif engine == "vector":
-                nc.vector.tensor_copy(dst, src)
-            else:
-                nc.gpsimd.tensor_scalar(grouped[key][:, c0:c1, :], stage[:, :, c0:c1].rearrange("p j c -> p c j"), 1.0, 0.0, MULT, ADD)
-            return grouped[key][:].rearrange("p c j -> p (c j)")
+        def interleave_on_gpsimd(dst, src):
+            nc.gpsimd.tensor_scalar(dst, src.rearrange("p j c -> p c j"), 1.0, 0.0, MULT, ADD)
 
         def product(stationary, k, moving):
             bank = product_psum.tile([P, 512], F32, name="bank", tag="bank")
@@ -147,10 +134,15 @@ def tile_attend_gds_nce_kernel(tc, xT, wT, vT, wt, xm, offs, out):
                 diffs[b, q] = diff_psum.tile([P, PACK, P], F32, name="diff%d" % q, tag="diff%d" % q)
             return diffs[b, q]
 
+        def squash(name, th, bank):
+            nc.scalar.activation(th, bank[:].rearrange("p (m t) -> p t m", t=PACK), TANH, scale=0.5 if name == "w" else -0.5)
+
         def score(name, b, c, th):
+            squash(name, th, product((name, b), c, ("xT", b)))
+            turn(name, b, c, th)
+
+        def turn(name, b, c, th):
             first = name == "w"
-            bank = product((name, b), c, ("xT", b))
-            nc.scalar.activation(th, bank[:].rearrange("p (m t) -> p t m", t=PACK), TANH, scale=0.5 if first else -0.5)
             for t in range(PACK):
                 if b == 0:
                     q, place = c, t
@@ -173,7 +165,7 @@ def tile_attend_gds_nce_kernel(tc, xT, wT, vT, wt, xm, offs, out):
                 dw = shared.tile([P, i1 - i0], F32, name="held_dw", align_bytes=64, offset=offset)
             else:
                 dw = ring.tile([P, i1 - i0], F32, name="dw", tag="dw")
-            nc.scalar.copy(dw[:], bank[:, shift + i0 : shift + i1])
+            nc.scalar.activation(dw[:], bank[:, shift + i0 : shift + i1], COPY, scale=0.5)
             dws.setdefault((b, k), []).append((i0, i1, dw))
 
         def gradient(b, k, pieces):
@@ -201,84 +193,108 @@ def tile_attend_gds_nce_kernel(tc, xT, wT, vT, wt, xm, offs, out):
         bring(wT, "w", 1, 1024, T, 1408)
         for b in range(B):
             gather("w", 1, b)
-        quantize_picked("w", 0)
-        quantize(("xT", 0), interleave(("xT", 0), load_rows(xT[0]), "scalar"), E4M3)
-        quantize_picked("w", 1)
+        quantize(("w", 0), flat(picked["w", 0]).bitcast(BF16), E4M3, 0)
+        xT0_grouped = keep.tile([P, 512, PACK], BF16, name="xT0_grouped", align_bytes=64)
+        interleave(xT0_grouped[:], load_rows(xT[0])[:])
+        quantize(("xT", 0), flat(xT0_grouped[:]), E4M3, 0)
+        quantize(("w", 1), flat(picked["w", 1]).bitcast(BF16), E4M3, 0)
         bring(vT, "v", 0, 0, 1024, 1024)
         bring(vT, "v", 0, 1024, T, 1408, "early")
         early = keep.tile([P, 3, PACK, P], F32, name="early", tag="early")
         for c in range(3):
             score("w", 0, c, early[:, c])
-        teacher = keep.tile([P, 3 * N], U32, name="teacher", align_bytes=64)
-        picked["v", 0] = teacher[:, N : 3 * N].rearrange("p (n u) -> p n u", u=2)
-        gather("v", 0, 0)
-        nc.vector.tensor_copy(teacher[:, 0:N], window_words("v", 0).indirect(group_offsets(1)))
+        teacher = keep.tile([P, 12 * HALF], U32, name="teacher", align_bytes=64)
+        blocks = teacher[:].rearrange("p (k n) -> p k n", n=HALF)
+        nc.vector.tensor_copy(teacher[:, 0 : B * N], window_words("v", 0).indirect(offsets[:]))
+
+        def gather_half(q, block):
+            nc.vector.tensor_copy(blocks[:, block, :], window_words("v", 1).indirect(offsets[:, q * 16 : (q + 1) * 16]))
+
         bring(vT, "v", 1, 0, 1024, 768)
         bring(vT, "v", 1, 1024, 1536, 1024)
         bring(vT, "v", 1, 1536, T, 1728, "held")
         held = keep.tile([P, PACK, P], F32, name="held", tag="held")
         score("w", 0, 3, held[:])
         nc.sync.dma_start(out=weights[:], in_=wt.rearrange("b (p t) o -> p b (t o)", t=PACK))
-        nc.gpsimd.tensor_scalar(half_weights[:], weights[:], 0.5, 0.0, MULT, ADD)
-        xT1 = [load_rows(xT[1], c, c + 256) for c in (0, 256)]
+        xT1 = load_rows(xT[1])
         xm0 = load_rows(xm[0])
         xm1 = load_rows(xm[1])
-        grouped["xT", 1] = shared.tile([P, 512, PACK], BF16, name="grouped_xT1", align_bytes=64, offset=0)
-        for c in range(0, 512, 128):
-            xT1_grouped = interleave(("xT", 1), xT1[c // 256], "scalar", c, c + 128, base=c // 256 * 256)
-        gather("v", 1, 0, 0, HALF)
-        gather("v", 1, 0, HALF, N)
-        quantize_picked("v", 0, 0, HALF)
-        quantize_picked("v", 0, HALF, N)
+        for q, block in ((0, 4), (1, 5), (2, 8)):
+            gather_half(q, block)
+        woven = [teacher[:, block * HALF : (block + 2) * HALF] for block in (6, 9)]
+        for q in range(2):
+            nc.scalar.copy(woven[q].rearrange("p (n u) -> p n u", u=2), blocks[:, q : q + 5 : 4, :].rearrange("p u n -> p n u"))
+        xT1_low = keep.tile([P, 256, PACK], BF16, name="xT1_low", align_bytes=64)
+        for c in (0, 128):
+            interleave(xT1_low[:, c : c + 128, :], xT1[:, :, c : c + 128])
+        for q in range(2):
+            quantize(("v", 0), woven[q].bitcast(BF16), E4M3, q * HALF)
+        gather_half(3, 9)
         for c in range(4):
             score("v", 0, c, ring_th())
-        nc.vector.tensor_copy(teacher[:, 2 * N : 3 * N], window_words("v", 1).indirect(group_offsets(1)))
-        quantize(("xT", 1), xT1_grouped, E4M3)
-        g0 = shared.tile([P, N, PACK], BF16, name="g0", align_bytes=64, offset=0)
-        g0_flat = g0[:].rearrange("p n t -> p (n t)")
+        picked_v1 = shared.tile([P, N, 2], U32, name="picked_v1", align_bytes=64, offset=3072)
+        nc.vector.tensor_copy(
+            picked_v1[:].bitcast(I32), teacher[:].bitcast(I32).rearrange("p (k n) -> p n k", n=N)[:, :, 1:5:3]
+        )
+        quantize(("xT", 1), flat(xT1_low[:]), E4M3, 0)
+        quantize(("v", 1), flat(picked_v1[:]).bitcast(BF16), E4M3, 0)
+        xT1_high = shared.tile([P, 256, PACK], BF16, name="xT1_high", align_bytes=64, offset=3072)
+        interleave_on_gpsimd(xT1_high[:, 128:256, :], xT1[:, :, 384:512])
+        xm0_most = shared.tile([P, 384, PACK], BF16, name="xm0_most", align_bytes=64, offset=0)
+        interleave(xm0_most[:, 0:128, :], xm0[:, :, 0:128])
+        quantize(("xm", 0), flat(xm0_most[:, 0:128, :]), E4M3, 0)
+        interleave(xT1_high[:, 0:128, :], xT1[:, :, 256:384])
 
-        def weigh(c):
-            nc.vector.tensor_tensor(
-                g0[:, c * P : (c + 1) * P, :],
-                diffs[0, c][:].rearrange("p t i -> p i t"),
-                half_weights[:, 0:1, :].to_broadcast([P, P, PACK]),
-                MULT,
-            )
+        def weigh(g, c):
+            nc.vector.tensor_tensor(g, diffs[0, c][:].rearrange("p t i -> p i t"), weights[:, 0:1, :].to_broadcast([P, P, PACK]), MULT)
 
-        weigh(0)
-        weigh(1)
-        quantize(("g", 0), g0_flat, E5M2, 0, HALF)
-        quantize(("xm", 0), interleave(("xm", 0), xm0, "scalar", 0, 128), E4M3, 0, 128)
+        g0 = keep.tile([P, 384, PACK], BF16, name="g0", align_bytes=64)
+        weigh(g0[:, 0:128, :], 0)
+        weigh(g0[:, 128:256, :], 1)
+        quantize(("g", 0), flat(g0[:, 0:256, :]), E5M2, 0)
+        quantize(("xT", 1), flat(xT1_high[:]), E4M3, 256)
         codes["g_first", 0] = (padded_words[:, 0:N], padded_scales[:, 0:N], E5M2)
         leave(0, 0, product(("xm", 0), 0, ("g_first", 0)), 0, HALF, shift=HALF)
-        weigh(2)
-        weigh(3)
-        quantize(("g", 0), g0_flat, E5M2, HALF, N)
+        weigh(g0[:, 256:384, :], 2)
+        g0_last = shared.tile([P, 128, PACK], BF16, name="g0_last", align_bytes=64, offset=3072)
+        weigh(g0_last[:], 3)
+        quantize(("g", 0), flat(g0[:, 256:384, :]), E5M2, 256)
+        quantize(("g", 0), flat(g0_last[:]), E5M2, 384)
+        for c in (128, 256):
+            interleave(xm0_most[:, c : c + 128, :], xm0[:, :, c : c + 128])
+            quantize(("xm", 0), flat(xm0_most[:, c : c + 128, :]), E4M3, c)
         gradient(0, 0, ((HALF, N, None),))
-        picked["v", 1] = keep.tile([P, N, 2], U32, name="picked_v1", align_bytes=64)[:]
-        nc.scalar.copy(picked["v", 1], teacher[:].rearrange("p (u n) -> p n u", u=3)[:, :, ::2])
-        quantize(("xm", 0), interleave(("xm", 0), xm0, "scalar", 128, 256), E4M3, 128, 256)
-        quantize_picked("v", 1)
         gradient(0, 1, ((0, N, None),))
-        quantize(("xm", 0), interleave(("xm", 0), xm0, "scalar", 256, 512), E4M3, 256, 512)
+        xm0_last = shared.tile([P, 128, PACK], BF16, name="xm0_last", align_bytes=64, offset=3072)
+        interleave(xm0_last[:], xm0[:, :, 384:512])
+        quantize(("xm", 0), flat(xm0_last[:]), E4M3, 384)
+        xm1_grouped = shared.tile([P, 512, PACK], BF16, name="xm1_grouped", align_bytes=64, offset=0)
         for c in range(0, 512, 128):
-            xm1_grouped = interleave(("xm", 1), xm1, "gpsimd", c, c + 128, tag="grouped_xm0")
-        quantize(("xm", 1), xm1_grouped, E4M3)
-        for h in range(2):
-            for name in ("w", "v"):
-                for c in (2 * h, 2 * h + 1):
-                    score(name, 1, c, ring_th())
-            if h == 0:
+            interleave_on_gpsimd(xm1_grouped[:, c : c + 128, :], xm1[:, :, c : c + 128])
+        quantize(("xm", 1), flat(xm1_grouped[:]), E4M3, 0)
+        steps = [(name, c) for h in range(2) for name in ("w", "v") for c in (2 * h, 2 * h + 1)]
+        squashed = []
+        for s, (name, c) in enumerate(steps):
+            squashed.append(ring_th())
+            squash(name, squashed[s], product((name, 1), c, ("xT", 1)))
+            if s == 3:
                 gradient(0, 2, ((0, N, None),))
-        last_bank = product(("xm", 0), 3, ("g", 0))
-        leave(0, 3, last_bank, 0, HALF)
-        planes = shared.tile([P, PACK, N], BF16, name="g_planes", align_bytes=64, offset=4096)
+                last_bank = product(("xm", 0), 3, ("g", 0))
+                leave(0, 3, last_bank, 0, HALF)
+            if s >= 2:
+                turn(steps[s - 2][0], 1, steps[s - 2][1], squashed[s - 2])
+        for s in (6, 7):
+            turn(steps[s][0], 1, steps[s][1], squashed[s])
+        planes = shared.tile([P, PACK, N], BF16, name="g_planes", align_bytes=64, offset=8192)
+        g1 = keep.tile([P, N, PACK], BF16, name="g1", align_bytes=64)
         for h in range(2):
             for t in range(PACK):
                 src = diffs[1, 2 * h + t // 2][:, 2 * (t % 2) : 2 * (t % 2) + 2, :].rearrange("p c i -> p (c i)")
-                nc.scalar.activation(planes[:, t, h * HALF : (h + 1) * HALF], src, COPY, scale=half_weights[:, 1, t : t + 1])
-            quantize(("g", 1), interleave(("g", 1), planes, "scalar" if h else "gpsimd", h * HALF, (h + 1) * HALF), E5M2, h * HALF, (h + 1) * HALF)
-        leave(0, 3, last_bank, HALF, N, 4096)
+                nc.scalar.activation(planes[:, t, h * HALF : (h + 1) * HALF], src, COPY, scale=weights[:, 1, t : t + 1])
+            half = g1[:, h * HALF : (h + 1) * HALF, :]
+            (interleave if h else interleave_on_gpsimd)(half, planes[:, :, h * HALF : (h + 1) * HALF])
+            quantize(("g", 1), flat(half), E5M2, h * HALF)
+        leave(0, 3, last_bank, HALF, N, 8192)
         for k in range(D // P):
             for piece in range(len(dws[0, k])):
                 scatter(0, k, piece)

@@ -29,7 +29,7 @@ def tile_attend_gds_nce_kernel(tc, xT, wT, vT, wt, xm, offs, out):
     nc = tc.nc
     with ExitStack() as ctx:
         keep = ctx.enter_context(tc.tile_pool(name="keep", bufs=1))
-        raw = ctx.enter_context(tc.tile_pool(name="raw", bufs=7))
+        raw = ctx.enter_context(tc.tile_pool(name="raw", bufs=6))
         shared = ctx.enter_context(tc.tile_pool(name="shared", bufs=1))
         ring = ctx.enter_context(tc.tile_pool(name="ring", bufs=4))
         product_psum = ctx.enter_context(tc.psum_pool(name="product_psum", bufs=4))
@@ -218,7 +218,8 @@ def tile_attend_gds_nce_kernel(tc, xT, wT, vT, wt, xm, offs, out):
         nc.sync.dma_start(out=weights[:], in_=wt.rearrange("b (p t) o -> p b (t o)", t=PACK))
         xT1 = load_rows(xT[1])
         xm0 = load_rows(xm[0])
-        xm1 = load_rows(xm[1])
+        xm1 = shared.tile([P, PACK, 512], F32, name="xm1", align_bytes=64, offset=8192)
+        nc.sync.dma_start(out=xm1[:], in_=xm[1].rearrange("(p j) c -> p j c", j=PACK))
         for q, block in ((0, 4), (1, 5), (2, 8)):
             gather_half(q, block)
         woven = [teacher[:, block * HALF : (block + 2) * HALF] for block in (6, 9)]
@@ -255,6 +256,8 @@ def tile_attend_gds_nce_kernel(tc, xT, wT, vT, wt, xm, offs, out):
         quantize(("xT", 1), flat(xT1_high[:]), E4M3, 256)
         codes["g_first", 0] = (padded_words[:, 0:N], padded_scales[:, 0:N], E5M2)
         leave(0, 0, product(("xm", 0), 0, ("g_first", 0)), 0, HALF, shift=HALF)
+        steps = [(name, c) for h in range(2) for name in ("w", "v") for c in (2 * h, 2 * h + 1)]
+        scores = [product(("w", 1), c, ("xT", 1)) for c in range(2)]
         weigh(g0[:, 256:384, :], 2)
         g0_last = shared.tile([P, 128, PACK], BF16, name="g0_last", align_bytes=64, offset=3072)
         weigh(g0_last[:], 3)
@@ -272,11 +275,10 @@ def tile_attend_gds_nce_kernel(tc, xT, wT, vT, wt, xm, offs, out):
         for c in range(0, 512, 128):
             interleave_on_gpsimd(xm1_grouped[:, c : c + 128, :], xm1[:, :, c : c + 128])
         quantize(("xm", 1), flat(xm1_grouped[:]), E4M3, 0)
-        steps = [(name, c) for h in range(2) for name in ("w", "v") for c in (2 * h, 2 * h + 1)]
         squashed = []
         for s, (name, c) in enumerate(steps):
             squashed.append(ring_th())
-            squash(name, squashed[s], product((name, 1), c, ("xT", 1)))
+            squash(name, squashed[s], scores[s] if s < 2 else product((name, 1), c, ("xT", 1)))
             if s == 3:
                 gradient(0, 2, ((0, N, None),))
                 last_bank = product(("xm", 0), 3, ("g", 0))
@@ -285,26 +287,31 @@ def tile_attend_gds_nce_kernel(tc, xT, wT, vT, wt, xm, offs, out):
                 turn(steps[s - 2][0], 1, steps[s - 2][1], squashed[s - 2])
         for s in (6, 7):
             turn(steps[s][0], 1, steps[s][1], squashed[s])
-        planes = shared.tile([P, PACK, N], BF16, name="g_planes", align_bytes=64, offset=8192)
         g1 = keep.tile([P, N, PACK], BF16, name="g1", align_bytes=64)
-        for h in range(2):
+        codes["g", 1] = codes["g", 0]
+
+        def weigh_half(h):
+            planes = shared.tile([P, PACK, HALF], BF16, name="planes%d" % h, align_bytes=64, offset=16384 + 2048 * h)
             for t in range(PACK):
                 src = diffs[1, 2 * h + t // 2][:, 2 * (t % 2) : 2 * (t % 2) + 2, :].rearrange("p c i -> p (c i)")
-                nc.scalar.activation(planes[:, t, h * HALF : (h + 1) * HALF], src, COPY, scale=weights[:, 1, t : t + 1])
+                nc.scalar.activation(planes[:, t, :], src, COPY, scale=weights[:, 1, t : t + 1])
             half = g1[:, h * HALF : (h + 1) * HALF, :]
-            (interleave if h else interleave_on_gpsimd)(half, planes[:, :, h * HALF : (h + 1) * HALF])
+            interleave(half, planes[:])
             quantize(("g", 1), flat(half), E5M2, h * HALF)
-        leave(0, 3, last_bank, HALF, N, 8192)
-        for k in range(D // P):
-            for piece in range(len(dws[0, k])):
-                scatter(0, k, piece)
-        first_bank = product(("xm", 1), 0, ("g", 1))
-        leave(1, 0, first_bank, 0, HALF)
-        gradient(1, 1, ((0, N, None),))
-        leave(1, 0, first_bank, HALF, N)
+
+        weigh_half(0)
+        leave(0, 3, last_bank, HALF, N, 15872)
+        leave(1, 0, product(("xm", 1), 0, ("g_first", 0)), 0, HALF, shift=HALF)
+        second_bank = product(("xm", 1), 1, ("g_first", 0))
+        weigh_half(1)
+        leave(1, 1, second_bank, 0, HALF, 18432, shift=HALF)
+        for k in range(2):
+            gradient(1, k, ((HALF, N, None),))
         for k in (2, 3):
             gradient(1, k, ((0, N, None),))
-        for k, piece in ((0, 0), (1, 0), (0, 1), (2, 0), (3, 0)):
-            scatter(1, k, piece)
-            if piece == len(dws[1, k]) - 1:
-                nc.sync.dma_start(out=out[k * P : (k + 1) * P, :], in_=placed[k][:])
+        for b in range(B):
+            for k in range(D // P):
+                for piece in range(len(dws[b, k])):
+                    scatter(b, k, piece)
+                if b == 1:
+                    nc.sync.dma_start(out=out[k * P : (k + 1) * P, :], in_=placed[k][:])

@@ -73,11 +73,12 @@ def tile_attend_gds_nce_kernel(tc, xT, wT, vT, wt, xm, offs, out):
             return stage
 
         def cast_table(name, u, base, c0, c1, stage, on_scalar):
-            src = stage[:, :, c0 - base : c1 - base].rearrange("p e c -> p c e")
+            src = stage[:, :, c0 - base : c1 - base].rearrange("p e (c i) -> p c e i", i=4)
+            dst = windows[name, u][:, c0:c1, :].rearrange("p (c i) e -> p c e i", i=4)
             if on_scalar:
-                nc.scalar.activation(windows[name, u][:, c0:c1, :], src, COPY)
+                nc.scalar.activation(dst, src, COPY)
             else:
-                nc.vector.tensor_copy(windows[name, u][:, c0:c1, :], src)
+                nc.vector.tensor_copy(dst, src)
 
         def load_rows(src, c0=0, c1=512):
             stage = raw.tile([P, PACK, c1 - c0], F32, name="stage", tag="stage")
@@ -224,7 +225,10 @@ def tile_attend_gds_nce_kernel(tc, xT, wT, vT, wt, xm, offs, out):
             gather_half(q, block)
         woven = [teacher[:, block * HALF : (block + 2) * HALF] for block in (6, 9)]
         for q in range(2):
-            nc.scalar.copy(woven[q].rearrange("p (n u) -> p n u", u=2), blocks[:, q : q + 5 : 4, :].rearrange("p u n -> p n u"))
+            nc.scalar.copy(
+                woven[q].rearrange("p (c i u) -> p c u i", i=4, u=2),
+                blocks[:, q : q + 5 : 4, :].rearrange("p u (c i) -> p c u i", i=4),
+            )
         xT1_low = keep.tile([P, 256, PACK], BF16, name="xT1_low", align_bytes=64)
         for c in (0, 128):
             interleave(xT1_low[:, c : c + 128, :], xT1[:, :, c : c + 128])
@@ -235,7 +239,8 @@ def tile_attend_gds_nce_kernel(tc, xT, wT, vT, wt, xm, offs, out):
             score("v", 0, c, ring_th())
         picked_v1 = shared.tile([P, N, 2], U32, name="picked_v1", align_bytes=64, offset=3072)
         nc.vector.tensor_copy(
-            picked_v1[:].bitcast(I32), teacher[:].bitcast(I32).rearrange("p (k n) -> p n k", n=N)[:, :, 1:5:3]
+            picked_v1[:].bitcast(I32).rearrange("p (c i) u -> p c u i", i=4),
+            teacher[:].bitcast(I32).rearrange("p (k c i) -> p c k i", k=6, i=4)[:, :, 1:5:3, :],
         )
         quantize(("xT", 1), flat(xT1_low[:]), E4M3, 0)
         quantize(("v", 1), flat(picked_v1[:]).bitcast(BF16), E4M3, 0)
@@ -247,7 +252,12 @@ def tile_attend_gds_nce_kernel(tc, xT, wT, vT, wt, xm, offs, out):
         interleave(xT1_high[:, 0:128, :], xT1[:, :, 256:384])
 
         def weigh(g, c):
-            nc.vector.tensor_tensor(g, diffs[0, c][:].rearrange("p t i -> p i t"), weights[:, 0:1, :].to_broadcast([P, P, PACK]), MULT)
+            nc.vector.tensor_tensor(
+                g.rearrange("p (c i) t -> p c t i", i=2),
+                diffs[0, c][:].rearrange("p t (c i) -> p c t i", i=2),
+                weights[:, 0:1, :].rearrange("p o (t z) -> p o t z", z=1).to_broadcast([P, P // 2, PACK, 2]),
+                MULT,
+            )
 
         g0 = keep.tile([P, 384, PACK], BF16, name="g0", align_bytes=64)
         weigh(g0[:, 0:128, :], 0)

@@ -229,7 +229,7 @@ def tile_attend_gds_nce_kernel(tc, xT, wT, vT, wt, xm, offs, out):
                 woven[q].rearrange("p (c i u) -> p c u i", i=4, u=2),
                 blocks[:, q : q + 5 : 4, :].rearrange("p u (c i) -> p c u i", i=4),
             )
-        xT1_low = keep.tile([P, 256, PACK], BF16, name="xT1_low", align_bytes=64)
+        xT1_low = keep.tile([P, 512, PACK], BF16, name="xT1_low", align_bytes=64)
         for c in (0, 128):
             interleave(xT1_low[:, c : c + 128, :], xT1[:, :, c : c + 128])
         for q in range(2):
@@ -237,19 +237,18 @@ def tile_attend_gds_nce_kernel(tc, xT, wT, vT, wt, xm, offs, out):
         gather_half(3, 9)
         for c in range(4):
             score("v", 0, c, ring_th())
-        picked_v1 = shared.tile([P, N, 2], U32, name="picked_v1", align_bytes=64, offset=3072)
+        picked_v1 = keep.tile([P, N, 2], U32, name="picked_v1", align_bytes=64)
         nc.vector.tensor_copy(
             picked_v1[:].bitcast(I32).rearrange("p (c i) u -> p c u i", i=4),
             teacher[:].bitcast(I32).rearrange("p (k c i) -> p c k i", k=6, i=4)[:, :, 1:5:3, :],
         )
-        quantize(("xT", 1), flat(xT1_low[:]), E4M3, 0)
+        quantize(("xT", 1), flat(xT1_low[:, 0:256, :]), E4M3, 0)
         quantize(("v", 1), flat(picked_v1[:]).bitcast(BF16), E4M3, 0)
-        xT1_high = shared.tile([P, 256, PACK], BF16, name="xT1_high", align_bytes=64, offset=3072)
-        interleave_on_gpsimd(xT1_high[:, 128:256, :], xT1[:, :, 384:512])
         xm0_most = shared.tile([P, 384, PACK], BF16, name="xm0_most", align_bytes=64, offset=0)
         interleave(xm0_most[:, 0:128, :], xm0[:, :, 0:128])
         quantize(("xm", 0), flat(xm0_most[:, 0:128, :]), E4M3, 0)
-        interleave(xT1_high[:, 0:128, :], xT1[:, :, 256:384])
+        for c in (256, 384):
+            interleave(xT1_low[:, c : c + 128, :], xT1[:, :, c : c + 128])
 
         def weigh(g, c):
             nc.vector.tensor_tensor(
@@ -259,20 +258,18 @@ def tile_attend_gds_nce_kernel(tc, xT, wT, vT, wt, xm, offs, out):
                 MULT,
             )
 
-        g0 = keep.tile([P, 384, PACK], BF16, name="g0", align_bytes=64)
+        g0 = shared.tile([P, N, PACK], BF16, name="g0", align_bytes=64, offset=3072)
         weigh(g0[:, 0:128, :], 0)
         weigh(g0[:, 128:256, :], 1)
         quantize(("g", 0), flat(g0[:, 0:256, :]), E5M2, 0)
-        quantize(("xT", 1), flat(xT1_high[:]), E4M3, 256)
         codes["g_first", 0] = (padded_words[:, 0:N], padded_scales[:, 0:N], E5M2)
         leave(0, 0, product(("xm", 0), 0, ("g_first", 0)), 0, HALF, shift=HALF)
         steps = [(name, c) for h in range(2) for name in ("w", "v") for c in (2 * h, 2 * h + 1)]
-        scores = [product(("w", 1), c, ("xT", 1)) for c in range(2)]
         weigh(g0[:, 256:384, :], 2)
-        g0_last = shared.tile([P, 128, PACK], BF16, name="g0_last", align_bytes=64, offset=3072)
-        weigh(g0_last[:], 3)
-        quantize(("g", 0), flat(g0[:, 256:384, :]), E5M2, 256)
-        quantize(("g", 0), flat(g0_last[:]), E5M2, 384)
+        weigh(g0[:, 384:512, :], 3)
+        quantize(("xT", 1), flat(xT1_low[:, 256:512, :]), E4M3, 256)
+        quantize(("g", 0), flat(g0[:, 256:512, :]), E5M2, 256)
+        scores = [product(("w", 1), c, ("xT", 1)) for c in range(2)]
         for c in (128, 256):
             interleave(xm0_most[:, c : c + 128, :], xm0[:, :, c : c + 128])
             quantize(("xm", 0), flat(xm0_most[:, c : c + 128, :]), E4M3, c)
@@ -323,5 +320,7 @@ def tile_attend_gds_nce_kernel(tc, xT, wT, vT, wt, xm, offs, out):
             for k in range(D // P):
                 for piece in range(len(dws[b, k])):
                     scatter(b, k, piece)
-                if b == 1:
+                if b == 1 and k < 3:
                     nc.sync.dma_start(out=out[k * P : (k + 1) * P, :], in_=placed[k][:])
+        nc.sync.dma_start(out=out[3 * P :, 0 : T // 2], in_=placed[3][:, 0 : T // 2])
+        nc.scalar.dma_start(out=out[3 * P :, T // 2 :], in_=placed[3][:, T // 2 :])

@@ -29,7 +29,8 @@ def tile_attend_gds_nce_kernel(tc, xT, wT, vT, wt, xm, offs, out):
     nc = tc.nc
     with ExitStack() as ctx:
         keep = ctx.enter_context(tc.tile_pool(name="keep", bufs=1))
-        raw = ctx.enter_context(tc.tile_pool(name="raw", bufs=6))
+        raw = ctx.enter_context(tc.tile_pool(name="raw", bufs=2))
+        staged = ctx.enter_context(tc.tile_pool(name="staged", bufs=1))
         shared = ctx.enter_context(tc.tile_pool(name="shared", bufs=1))
         ring = ctx.enter_context(tc.tile_pool(name="ring", bufs=4))
         product_psum = ctx.enter_context(tc.psum_pool(name="product_psum", bufs=4))
@@ -45,8 +46,8 @@ def tile_attend_gds_nce_kernel(tc, xT, wT, vT, wt, xm, offs, out):
         nc.gpsimd.memset(warm[:], 0.0)
         nc.scalar.activation(warm_out[:], warm[:], TANH)
         make_identity(nc, ident[:])
-        for tile in placed:
-            nc.vector.memset(tile[:], 0.0)
+        for k, tile in enumerate(placed):
+            (nc.vector if k < 3 else nc.gpsimd).memset(tile[:], 0.0)
 
         def group_offsets(b, i0=0, i1=N):
             return offsets[:, b * LIST_COLS + i0 // 16 : b * LIST_COLS + i1 // 16]
@@ -63,11 +64,8 @@ def tile_attend_gds_nce_kernel(tc, xT, wT, vT, wt, xm, offs, out):
             for u in range(2):
                 windows[name, u] = keep.tile([P, T, 2], BF16, name="win_%s%d" % (name, u), align_bytes=64)
 
-        def load_table(table, u, c0, c1, tag=None):
-            if tag:
-                stage = keep.tile([P, 2, c1 - c0], F32, name=tag, tag=tag)
-            else:
-                stage = raw.tile([P, 2, c1 - c0], F32, name="stage", tag="stage")
+        def load_table(table, u, c0, c1, offset, name):
+            stage = staged.tile([P, 2, c1 - c0], F32, name=name, offset=offset)
             rows = table.rearrange("(p j) c -> p j c", j=PACK)
             nc.sync.dma_start(out=stage[:], in_=rows[:, 2 * u : 2 * u + 2, c0:c1])
             return stage
@@ -178,20 +176,19 @@ def tile_attend_gds_nce_kernel(tc, xT, wT, vT, wt, xm, offs, out):
             i0, i1, dw = dws[b, k][piece]
             nc.vector.tensor_copy(placed[k][:].indirect(group_offsets(b, i0, i1)), dw[:])
 
-        def bring(table, name, u, c0, c1, split, tag=None):
-            stage = load_table(table, u, c0, c1, tag)
+        def bring(table, name, u, c0, c1, split, offset):
+            stage = load_table(table, u, c0, c1, offset, "stage_%s%d_%d" % (name, u, c0))
             if split > c0:
                 cast_table(name, u, c0, c0, split, stage, True)
             if split < c1:
                 cast_table(name, u, c0, split, c1, stage, False)
 
-        bring(wT, "w", 0, 0, 1024, 1024)
+        bring(wT, "w", 0, 0, T, 768, 0)
         nc.sync.dma_start(offsets[:], offs)
-        bring(wT, "w", 0, 1024, T, 1408)
         for b in range(B):
             gather("w", 0, b)
-        bring(wT, "w", 1, 0, 1024, 1024)
-        bring(wT, "w", 1, 1024, T, 1408)
+        bring(wT, "w", 1, 0, 1024, 1024, 16384)
+        bring(wT, "w", 1, 1024, T, 1408, 24576)
         for b in range(B):
             gather("w", 1, b)
         quantize(("w", 0), flat(picked["w", 0]).bitcast(BF16), E4M3, 0)
@@ -199,9 +196,9 @@ def tile_attend_gds_nce_kernel(tc, xT, wT, vT, wt, xm, offs, out):
         interleave(xT0_grouped[:], load_rows(xT[0])[:])
         quantize(("xT", 0), flat(xT0_grouped[:]), E4M3, 0)
         quantize(("w", 1), flat(picked["w", 1]).bitcast(BF16), E4M3, 0)
-        bring(vT, "v", 0, 0, 1024, 1024)
-        bring(vT, "v", 0, 1024, T, 1408, "early")
-        early = keep.tile([P, 3, PACK, P], F32, name="early", tag="early")
+        bring(vT, "v", 0, 0, 1024, 1024, 0)
+        bring(vT, "v", 0, 1024, T, 1408, 8192)
+        early = staged.tile([P, 3, PACK, P], F32, name="early", offset=8192)
         for c in range(3):
             score("w", 0, c, early[:, c])
         teacher = keep.tile([P, 12 * HALF], U32, name="teacher", align_bytes=64)
@@ -211,13 +208,13 @@ def tile_attend_gds_nce_kernel(tc, xT, wT, vT, wt, xm, offs, out):
         def gather_half(q, block):
             nc.vector.tensor_copy(blocks[:, block, :], window_words("v", 1).indirect(offsets[:, q * 16 : (q + 1) * 16]))
 
-        bring(vT, "v", 1, 0, 1024, 768)
-        bring(vT, "v", 1, 1024, 1536, 1024)
-        bring(vT, "v", 1, 1536, T, 1728, "held")
-        held = keep.tile([P, PACK, P], F32, name="held", tag="held")
+        bring(vT, "v", 1, 0, 1024, 768, 16384)
+        bring(vT, "v", 1, 1024, 1536, 1024, 24576)
+        bring(vT, "v", 1, 1536, T, 1728, 28672)
+        held = staged.tile([P, PACK, P], F32, name="held", offset=28672)
         score("w", 0, 3, held[:])
-        nc.sync.dma_start(out=weights[:], in_=wt.rearrange("b (p t) o -> p b (t o)", t=PACK))
         xT1 = load_rows(xT[1])
+        nc.sync.dma_start(out=weights[:], in_=wt.rearrange("b (p t) o -> p b (t o)", t=PACK))
         xm0 = load_rows(xm[0])
         xm1 = shared.tile([P, PACK, 512], F32, name="xm1", align_bytes=64, offset=8192)
         nc.sync.dma_start(out=xm1[:], in_=xm[1].rearrange("(p j) c -> p j c", j=PACK))

@@ -185,12 +185,18 @@ def tile_attend_gds_nce_kernel(tc, xT, wT, vT, wt, xm, offs, out):
 
         bring(wT, "w", 0, 0, T, 768, 0)
         nc.sync.dma_start(offsets[:], offs)
-        for b in range(B):
-            gather("w", 0, b)
+        student = keep.tile([P, 2, B * N], U32, name="student", align_bytes=64)
+        nc.vector.tensor_copy(student[:, 0, :], window_words("w", 0).indirect(offsets[:]))
         bring(wT, "w", 1, 0, 1024, 1024, 16384)
         bring(wT, "w", 1, 1024, T, 1408, 24576)
         for b in range(B):
-            gather("w", 1, b)
+            nc.vector.tensor_copy(student[:, 1, b * N : (b + 1) * N], window_words("w", 1).indirect(group_offsets(b)))
+        for b in range(B):
+            picked["w", b] = keep.tile([P, N, 2], U32, name="picked_w%d" % b, align_bytes=64)[:]
+            nc.vector.tensor_copy(
+                picked["w", b].bitcast(I32).rearrange("p (c i) u -> p c u i", i=4),
+                student[:, :, b * N : (b + 1) * N].bitcast(I32).rearrange("p u (c i) -> p c u i", i=4),
+            )
         quantize(("w", 0), flat(picked["w", 0]).bitcast(BF16), E4M3, 0)
         xT0_grouped = keep.tile([P, 512, PACK], BF16, name="xT0_grouped", align_bytes=64)
         interleave(xT0_grouped[:], load_rows(xT[0])[:])

@@ -40,11 +40,7 @@ def tile_attend_gds_nce_kernel(tc, xT, wT, vT, wt, xm, offs, out):
         weights = keep.tile([P, B, PACK], F32, name="weights")
         ident = keep.tile([P, P], F32, name="ident")
         placed = [keep.tile([P, T], F32, name="placed%d" % k) for k in range(D // P)]
-        warm = keep.tile([P, 8], F32, name="warm")
-        warm_out = keep.tile([P, 8], F32, name="warm_out")
 
-        nc.gpsimd.memset(warm[:], 0.0)
-        nc.scalar.activation(warm_out[:], warm[:], TANH)
         make_identity(nc, ident[:])
         for k, tile in enumerate(placed):
             (nc.vector if k < 3 else nc.gpsimd).memset(tile[:], 0.0)
@@ -187,8 +183,7 @@ def tile_attend_gds_nce_kernel(tc, xT, wT, vT, wt, xm, offs, out):
         nc.sync.dma_start(offsets[:], offs)
         student = keep.tile([P, 2, B * N], U32, name="student", align_bytes=64)
         nc.vector.tensor_copy(student[:, 0, :], window_words("w", 0).indirect(offsets[:]))
-        bring(wT, "w", 1, 0, 1024, 1024, 16384)
-        bring(wT, "w", 1, 1024, T, 1408, 24576)
+        bring(wT, "w", 1, 0, T, 768, 16384)
         for b in range(B):
             nc.vector.tensor_copy(student[:, 1, b * N : (b + 1) * N], window_words("w", 1).indirect(group_offsets(b)))
         for b in range(B):

@@ -183,7 +183,7 @@ def tile_attend_gds_nce_kernel(tc, xT, wT, vT, wt, xm, offs, out):
         nc.sync.dma_start(offsets[:], offs)
         student = keep.tile([P, 2, B * N], U32, name="student", align_bytes=64)
         nc.vector.tensor_copy(student[:, 0, :], window_words("w", 0).indirect(offsets[:]))
-        bring(wT, "w", 1, 0, T, 768, 16384)
+        bring(wT, "w", 1, 0, T, 704, 16384)
         for b in range(B):
             nc.vector.tensor_copy(student[:, 1, b * N : (b + 1) * N], window_words("w", 1).indirect(group_offsets(b)))
         for b in range(B):
@@ -198,7 +198,7 @@ def tile_attend_gds_nce_kernel(tc, xT, wT, vT, wt, xm, offs, out):
         quantize(("xT", 0), flat(xT0_grouped[:]), E4M3, 0)
         quantize(("w", 1), flat(picked["w", 1]).bitcast(BF16), E4M3, 0)
         bring(vT, "v", 0, 0, 1024, 1024, 0)
-        bring(vT, "v", 0, 1024, T, 1408, 8192)
+        bring(vT, "v", 0, 1024, T, 1536, 8192)
         early = staged.tile([P, 3, PACK, P], F32, name="early", offset=8192)
         for c in range(3):
             score("w", 0, c, early[:, c])
@@ -209,7 +209,7 @@ def tile_attend_gds_nce_kernel(tc, xT, wT, vT, wt, xm, offs, out):
         def gather_half(q, block):
             nc.vector.tensor_copy(blocks[:, block, :], window_words("v", 1).indirect(offsets[:, q * 16 : (q + 1) * 16]))
 
-        bring(vT, "v", 1, 0, 1024, 768, 16384)
+        bring(vT, "v", 1, 0, 1024, 640, 16384)
         bring(vT, "v", 1, 1024, 1536, 1024, 24576)
         bring(vT, "v", 1, 1536, T, 1728, 28672)
         held = staged.tile([P, PACK, P], F32, name="held", offset=28672)

@@ -33,7 +33,6 @@ def tile_attend_gds_nce_kernel(tc, xT, wT, vT, wt, xm, offs, out):
         staged = ctx.enter_context(tc.tile_pool(name="staged", bufs=1))
         shared = ctx.enter_context(tc.tile_pool(name="shared", bufs=1))
         ring = ctx.enter_context(tc.tile_pool(name="ring", bufs=4))
-        product_psum = ctx.enter_context(tc.psum_pool(name="product_psum", bufs=4))
         diff_psum = ctx.enter_context(tc.psum_pool(name="diff_psum", bufs=1))
 
         offsets = keep.tile([P, B * LIST_COLS], U16, name="offsets")
@@ -103,20 +102,26 @@ def tile_attend_gds_nce_kernel(tc, xT, wT, vT, wt, xm, offs, out):
         def interleave(dst, src):
             nc.scalar.copy(dst.rearrange("p (c i) j -> p c j i", i=4), src.rearrange("p j (c i) -> p c j i", i=4))
 
+        def deal(dst, src, m0, m1):
+            nc.scalar.copy(
+                dst.rearrange("p (t m) j -> p m j t", t=PACK)[:, m0:m1],
+                src.rearrange("p j (m t) -> p m j t", t=PACK)[:, m0:m1],
+            )
+
         def interleave_on_gpsimd(dst, src):
             nc.gpsimd.tensor_scalar(dst, src.rearrange("p j c -> p c j"), 1.0, 0.0, MULT, ADD)
 
-        def product(stationary, k, moving):
-            bank = product_psum.tile([P, 512], F32, name="bank", tag="bank")
+        def product(stationary, k, moving, tag, n0=0, n1=512):
+            bank = diff_psum.tile([P, 512], F32, name=tag, tag=tag)
             s_words, s_scales, s_fmt = codes[stationary]
             m_words, m_scales, m_fmt = codes[moving]
             cols = slice(k * P, (k + 1) * P)
             nc.tensor.matmul_mx(
-                out=bank[:],
+                out=bank[:, n0:n1],
                 lhsT=s_words[:, cols].bitcast(s_fmt),
                 lhsT_scale=s_scales[:, cols],
-                rhs=m_words[:].bitcast(m_fmt),
-                rhs_scale=m_scales[:],
+                rhs=m_words[:, n0:n1].bitcast(m_fmt),
+                rhs_scale=m_scales[:, n0:n1],
                 start=True,
                 stop=True,
             )
@@ -129,16 +134,19 @@ def tile_attend_gds_nce_kernel(tc, xT, wT, vT, wt, xm, offs, out):
                 diffs[b, q] = diff_psum.tile([P, PACK, P], F32, name="diff%d" % q, tag="diff%d" % q)
             return diffs[b, q]
 
-        def squash(name, th, bank):
+        def squash(name, th, bank, t0=0, t1=PACK):
+            nc.scalar.activation(flat(th[:, t0:t1, :]), bank[:, t0 * P : t1 * P], TANH, scale=0.5 if name == "w" else -0.5)
+
+        def squash_rows(name, th, bank):
             nc.scalar.activation(th, bank[:].rearrange("p (m t) -> p t m", t=PACK), TANH, scale=0.5 if name == "w" else -0.5)
 
         def score(name, b, c, th):
-            squash(name, th, product((name, b), c, ("xT", b)))
+            squash(name, th, product((name, b), c, ("xT", b), "bank%d" % c))
             turn(name, b, c, th)
 
-        def turn(name, b, c, th):
+        def turn(name, b, c, th, t0=0, t1=PACK):
             first = name == "w"
-            for t in range(PACK):
+            for t in range(t0, t1):
                 if b == 0:
                     q, place = c, t
                     opens, closes = t == 0, t == PACK - 1
@@ -163,8 +171,8 @@ def tile_attend_gds_nce_kernel(tc, xT, wT, vT, wt, xm, offs, out):
             nc.scalar.activation(dw[:], bank[:, shift + i0 : shift + i1], COPY, scale=0.5)
             dws.setdefault((b, k), []).append((i0, i1, dw))
 
-        def gradient(b, k, pieces):
-            bank = product(("xm", b), k, ("g", b))
+        def gradient(b, k, tag, pieces):
+            bank = product(("xm", b), k, ("g", b), tag)
             for i0, i1, offset in pieces:
                 leave(b, k, bank, i0, i1, offset)
 
@@ -194,7 +202,7 @@ def tile_attend_gds_nce_kernel(tc, xT, wT, vT, wt, xm, offs, out):
             )
         quantize(("w", 0), flat(picked["w", 0]).bitcast(BF16), E4M3, 0)
         xT0_grouped = keep.tile([P, 512, PACK], BF16, name="xT0_grouped", align_bytes=64)
-        interleave(xT0_grouped[:], load_rows(xT[0])[:])
+        deal(xT0_grouped[:], load_rows(xT[0])[:], 0, P)
         quantize(("xT", 0), flat(xT0_grouped[:]), E4M3, 0)
         quantize(("w", 1), flat(picked["w", 1]).bitcast(BF16), E4M3, 0)
         bring(vT, "v", 0, 0, 1024, 1024, 0)
@@ -202,51 +210,53 @@ def tile_attend_gds_nce_kernel(tc, xT, wT, vT, wt, xm, offs, out):
         early = staged.tile([P, 3, PACK, P], F32, name="early", offset=8192)
         for c in range(3):
             score("w", 0, c, early[:, c])
-        teacher = keep.tile([P, 12 * HALF], U32, name="teacher", align_bytes=64)
+        teacher = keep.tile([P, 16 * HALF], U32, name="teacher", align_bytes=64)
         blocks = teacher[:].rearrange("p (k n) -> p k n", n=HALF)
-        nc.vector.tensor_copy(teacher[:, 0 : B * N], window_words("v", 0).indirect(offsets[:]))
+        first_words = teacher[:, 8 * HALF + P : 10 * HALF + P].rearrange("p (i u) -> p i u", u=2)
+        nc.vector.tensor_copy(teacher[:, HALF : B * N], window_words("v", 0).indirect(offsets[:, 16:]))
+        nc.vector.tensor_copy(first_words[:, :, 0], window_words("v", 0).indirect(offsets[:, 0:16]))
 
         def gather_half(q, block):
             nc.vector.tensor_copy(blocks[:, block, :], window_words("v", 1).indirect(offsets[:, q * 16 : (q + 1) * 16]))
 
         bring(vT, "v", 1, 0, 1024, 640, 16384)
-        bring(vT, "v", 1, 1024, 1536, 1024, 24576)
-        bring(vT, "v", 1, 1536, T, 1728, 28672)
+        bring(vT, "v", 1, 1024, 1792, 1024 + 192, 24576)
+        bring(vT, "v", 1, 1792, T, 1792 + (T - 1792) * 3 // 8, 24576 + 8 * (1792 - 1024))
         held = staged.tile([P, PACK, P], F32, name="held", offset=28672)
         score("w", 0, 3, held[:])
-        xT1 = load_rows(xT[1])
-        nc.sync.dma_start(out=weights[:], in_=wt.rearrange("b (p t) o -> p b (t o)", t=PACK))
         xm0 = load_rows(xm[0])
-        xm1 = shared.tile([P, PACK, 512], F32, name="xm1", align_bytes=64, offset=8192)
+        nc.sync.dma_start(out=weights[:], in_=wt.rearrange("b (p t) o -> p b (t o)", t=PACK))
+        xT1 = staged.tile([P, PACK, 512], F32, name="xT1", offset=0)
+        nc.sync.dma_start(out=xT1[:], in_=xT[1].rearrange("(p j) c -> p j c", j=PACK))
+        xm1 = staged.tile([P, PACK, 512], F32, name="xm1", offset=16384)
         nc.sync.dma_start(out=xm1[:], in_=xm[1].rearrange("(p j) c -> p j c", j=PACK))
-        for q, block in ((0, 4), (1, 5), (2, 8)):
-            gather_half(q, block)
-        woven = [teacher[:, block * HALF : (block + 2) * HALF] for block in (6, 9)]
-        for q in range(2):
-            nc.scalar.copy(
-                woven[q].rearrange("p (c i u) -> p c u i", i=4, u=2),
-                blocks[:, q : q + 5 : 4, :].rearrange("p u (c i) -> p c u i", i=4),
-            )
-        xT1_low = keep.tile([P, 512, PACK], BF16, name="xT1_low", align_bytes=64)
-        for c in (0, 128):
-            interleave(xT1_low[:, c : c + 128, :], xT1[:, :, c : c + 128])
-        for q in range(2):
-            quantize(("v", 0), woven[q].bitcast(BF16), E4M3, q * HALF)
-        gather_half(3, 9)
-        for c in range(4):
-            score("v", 0, c, ring_th())
-        picked_v1 = keep.tile([P, N, 2], U32, name="picked_v1", align_bytes=64)
+
+        nc.vector.tensor_copy(first_words[:, :, 1], window_words("v", 1).indirect(offsets[:, 0:16]))
+        for c in range(2):
+            quantize(("v", 0), flat(first_words[:, c * P : (c + 1) * P, :]).bitcast(BF16), E4M3, c * P)
+        for q in (1, 2, 3):
+            gather_half(q, 7 + q)
+        woven = teacher[:, 4 * HALF : 6 * HALF]
         nc.vector.tensor_copy(
-            picked_v1[:].bitcast(I32).rearrange("p (c i) u -> p c u i", i=4),
-            teacher[:].bitcast(I32).rearrange("p (k c i) -> p c k i", k=6, i=4)[:, :, 1:5:3, :],
+            woven.bitcast(I32).rearrange("p (c i u) -> p c u i", i=4, u=2),
+            blocks[:, 1:9:7, :].bitcast(I32).rearrange("p u (c i) -> p c u i", i=4),
         )
-        quantize(("xT", 1), flat(xT1_low[:, 0:256, :]), E4M3, 0)
-        quantize(("v", 1), flat(picked_v1[:]).bitcast(BF16), E4M3, 0)
-        xm0_most = shared.tile([P, 384, PACK], BF16, name="xm0_most", align_bytes=64, offset=0)
-        interleave(xm0_most[:, 0:128, :], xm0[:, :, 0:128])
-        quantize(("xm", 0), flat(xm0_most[:, 0:128, :]), E4M3, 0)
-        for c in (256, 384):
-            interleave(xT1_low[:, c : c + 128, :], xT1[:, :, c : c + 128])
+        xm0_parts = {}
+
+        def group_xm0(k):
+            xm0_parts[k] = shared.tile([P, P, PACK], BF16, name="xm0_%d" % k, align_bytes=64, offset=1024 * k)
+            interleave(xm0_parts[k][:], xm0[:, :, k * P : (k + 1) * P])
+
+        def quantize_xm0(k):
+            quantize(("xm", 0), flat(xm0_parts[k][:]), E4M3, k * P)
+
+        first_th = shared.tile([P, PACK, P], F32, name="first_th", align_bytes=64, offset=16384)
+        for c in range(2):
+            th = first_th[:] if c == 0 else ring_th()
+            halves = [product(("v", 0), c, ("xT", 0), "bank%d" % (2 * c + h), h * HALF, (h + 1) * HALF) for h in range(2)]
+            for h in range(2):
+                squash("v", th, halves[h], 2 * h, 2 * h + 2)
+                turn("v", 0, c, th, 2 * h, 2 * h + 2)
 
         def weigh(g, c):
             nc.vector.tensor_tensor(
@@ -256,69 +266,117 @@ def tile_attend_gds_nce_kernel(tc, xT, wT, vT, wt, xm, offs, out):
                 MULT,
             )
 
-        g0 = shared.tile([P, N, PACK], BF16, name="g0", align_bytes=64, offset=3072)
-        weigh(g0[:, 0:128, :], 0)
-        weigh(g0[:, 128:256, :], 1)
-        quantize(("g", 0), flat(g0[:, 0:256, :]), E5M2, 0)
+        g0a = shared.tile([P, HALF, PACK], BF16, name="g0a", align_bytes=64, offset=4096)
+        g0b = shared.tile([P, HALF, PACK], BF16, name="g0b", align_bytes=64, offset=12288)
+        for k in range(4):
+            group_xm0(k)
+        weigh(g0a[:, 0:128, :], 0)
+        late_words = shared.tile([P, HALF], U32, name="late_words", align_bytes=64, offset=16384)
+        late_scales = shared.tile([P, HALF], U8, name="late_scales", align_bytes=64, offset=17408)
+        codes["v_late", 0] = (late_words, late_scales, E4M3)
+        quantize(("v_late", 0), woven.bitcast(BF16), E4M3, 0)
+        weigh(g0a[:, 128:256, :], 1)
+        quantize_xm0(0)
+        quantize(("g", 0), flat(g0a[:]), E5M2, 0)
         codes["g_first", 0] = (padded_words[:, 0:N], padded_scales[:, 0:N], E5M2)
-        leave(0, 0, product(("xm", 0), 0, ("g_first", 0)), 0, HALF, shift=HALF)
-        steps = [(name, c) for h in range(2) for name in ("w", "v") for c in (2 * h, 2 * h + 1)]
-        weigh(g0[:, 256:384, :], 2)
-        weigh(g0[:, 384:512, :], 3)
-        quantize(("xT", 1), flat(xT1_low[:, 256:512, :]), E4M3, 256)
-        quantize(("g", 0), flat(g0[:, 256:512, :]), E5M2, 256)
-        scores = [product(("w", 1), c, ("xT", 1)) for c in range(2)]
-        for c in (128, 256):
-            interleave(xm0_most[:, c : c + 128, :], xm0[:, :, c : c + 128])
-            quantize(("xm", 0), flat(xm0_most[:, c : c + 128, :]), E4M3, c)
-        gradient(0, 0, ((HALF, N, None),))
-        gradient(0, 1, ((0, N, None),))
-        xm0_last = shared.tile([P, 128, PACK], BF16, name="xm0_last", align_bytes=64, offset=3072)
-        interleave(xm0_last[:], xm0[:, :, 384:512])
-        quantize(("xm", 0), flat(xm0_last[:]), E4M3, 384)
-        xm1_grouped = shared.tile([P, 512, PACK], BF16, name="xm1_grouped", align_bytes=64, offset=0)
+        first_bank = product(("xm", 0), 0, ("g_first", 0), "bank0")
+        squashed = {}
+        for c in (2, 3):
+            squashed[c] = ring_th()
+            squash("v", squashed[c], product(("v_late", 0), c - 2, ("xT", 0), "diff%d" % (c - 2)))
+        leave(0, 0, first_bank, 0, HALF, shift=HALF)
+        scatter(0, 0, 0)
+        for c in (2, 3):
+            turn("v", 0, c, squashed[c])
+        picked_v1 = shared.tile([P, N, 2], U32, name="picked_v1", align_bytes=64, offset=4096)
+        nc.vector.tensor_copy(
+            picked_v1[:].bitcast(I32).rearrange("p (h c i) u -> p h c u i", h=2, i=4),
+            teacher[:, 2 * HALF : 2 * HALF + 14 * HALF].bitcast(I32).rearrange("p (u h c i) -> p h c u i", u=2, h=7, i=4)[:, 0:2],
+        )
+        quantize_xm0(1)
+        quantize_xm0(3)
+        quantize(("v", 1), flat(picked_v1[:]).bitcast(BF16), E4M3, 0)
+        quantize_xm0(2)
+        second_bank = product(("xm", 0), 1, ("g_first", 0), "bank1")
+        third_bank = product(("xm", 0), 2, ("g_first", 0), "bank2")
+
+        def chunk_planes(c, pool, offset):
+            planes = pool.tile([P, PACK, P], BF16, name="planes%d" % c, align_bytes=64, offset=offset)
+            for t in range(PACK):
+                nc.scalar.activation(planes[:, t, :], diffs[0, c][:, t, :], COPY, scale=weights[:, 0, t : t + 1])
+            interleave_on_gpsimd(g0b[:, (c - 2) * P : (c - 1) * P, :], planes[:])
+
+        def scaled_planes(b, h, offset):
+            planes = shared.tile([P, PACK, HALF], BF16, name="planes%d%d" % (b, h), align_bytes=64, offset=offset)
+            for t in range(PACK):
+                src = diffs[b, 2 * h + t // 2][:, 2 * (t % 2) : 2 * (t % 2) + 2, :].rearrange("p c i -> p (c i)")
+                nc.scalar.activation(planes[:, t, :], src, COPY, scale=weights[:, b, t : t + 1])
+            return planes
+
+        xT1_grouped = shared.tile([P, 512, PACK], BF16, name="xT1_grouped", align_bytes=64, offset=5120)
+        interleave_on_gpsimd(xT1_grouped[:, 0:P, :], xT1[:, :, 0:P])
+        chunk_planes(2, shared, 11264)
+        leave(0, 1, second_bank, 0, HALF, shift=HALF)
+        scatter(0, 1, 0)
+        chunk_planes(3, staged, 8192)
+        quantize(("g", 0), flat(g0b[:]), E5M2, HALF)
+        for c in (128, 256, 384):
+            interleave(xT1_grouped[:, c : c + P, :], xT1[:, :, c : c + P])
+        quantize(("xT", 1), flat(xT1_grouped[:]), E4M3, 0)
+        dw = staged.tile([P, HALF], F32, name="dw_after_xT1", offset=7680)
+        nc.scalar.activation(dw[:], third_bank[:, HALF:N], COPY, scale=0.5)
+        dws[0, 2] = [(0, HALF, dw)]
+        scatter(0, 2, 0)
+        for k in range(2):
+            gradient(0, k, "bank%d" % k, ((HALF, N, None),))
+            scatter(0, k, 1)
+        xm1_grouped = shared.tile([P, 512, PACK], BF16, name="xm1_grouped", align_bytes=64, offset=5120)
         for c in range(0, 512, 128):
             interleave_on_gpsimd(xm1_grouped[:, c : c + 128, :], xm1[:, :, c : c + 128])
-        quantize(("xm", 1), flat(xm1_grouped[:]), E4M3, 0)
-        squashed = []
-        for s, (name, c) in enumerate(steps):
-            squashed.append(ring_th())
-            squash(name, squashed[s], scores[s] if s < 2 else product((name, 1), c, ("xT", 1)))
-            if s == 3:
-                gradient(0, 2, ((0, N, None),))
-                last_bank = product(("xm", 0), 3, ("g", 0))
-                leave(0, 3, last_bank, 0, HALF)
-            if s >= 2:
-                turn(steps[s - 2][0], 1, steps[s - 2][1], squashed[s - 2])
-        for s in (6, 7):
-            turn(steps[s][0], 1, steps[s][1], squashed[s])
         g1 = keep.tile([P, N, PACK], BF16, name="g1", align_bytes=64)
         codes["g", 1] = codes["g", 0]
 
-        def weigh_half(h):
-            planes = shared.tile([P, PACK, HALF], BF16, name="planes%d" % h, align_bytes=64, offset=16384 + 2048 * h)
-            for t in range(PACK):
-                src = diffs[1, 2 * h + t // 2][:, 2 * (t % 2) : 2 * (t % 2) + 2, :].rearrange("p c i -> p (c i)")
-                nc.scalar.activation(planes[:, t, :], src, COPY, scale=weights[:, 1, t : t + 1])
-            half = g1[:, h * HALF : (h + 1) * HALF, :]
-            interleave(half, planes[:])
-            quantize(("g", 1), flat(half), E5M2, h * HALF)
+        def heads(steps, tags, squashed):
+            banks = [product((name, 1), c, ("xT", 1), tag) for (name, c), tag in zip(steps, tags)]
+            for (name, c), bank, th in zip(steps, banks, squashed):
+                squash_rows(name, th, bank)
+                turn(name, 1, c, th)
 
-        weigh_half(0)
+        def squash_tile(name, count, offset):
+            tile = staged.tile([P, count, PACK, P], F32, name=name, offset=offset)
+            return [tile[:, j] for j in range(count)]
+
+        heads((("w", 0), ("w", 1), ("v", 0), ("v", 1)), ("diff2", "diff3", "bank3", "bank2"),
+              squash_tile("th_w01", 2, 24576) + squash_tile("th_v0", 1, 28672) + squash_tile("th_v1", 1, 30720))
+        quantize(("xm", 1), flat(xm1_grouped[:]), E4M3, 0)
+        last_bank = product(("xm", 0), 3, ("g", 0), "bank1")
+        for k, bank, i0, offset in ((2, product(("xm", 0), 2, ("g", 0), "bank0"), HALF, 16384), (3, last_bank, 0, 17408)):
+            dw = staged.tile([P, HALF], F32, name="dw_after_xm1_%d" % k, offset=offset)
+            nc.scalar.activation(dw[:], bank[:, i0 : i0 + HALF], COPY, scale=0.5)
+            dws.setdefault((0, k), []).append((i0, i0 + HALF, dw))
+            scatter(0, k, -1)
+        interleave_on_gpsimd(g1[:, 0:HALF, :], scaled_planes(1, 0, 16384)[:])
+        quantize(("g", 1), flat(g1[:, 0:HALF, :]), E5M2, 0)
         leave(0, 3, last_bank, HALF, N, 15872)
-        leave(1, 0, product(("xm", 1), 0, ("g_first", 0)), 0, HALF, shift=HALF)
-        second_bank = product(("xm", 1), 1, ("g_first", 0))
-        weigh_half(1)
-        leave(1, 1, second_bank, 0, HALF, 18432, shift=HALF)
+        scatter(0, 3, 1)
+        heads((("w", 2), ("w", 3), ("v", 2), ("v", 3)), ("bank3", "bank2", "bank0", "diff1"),
+              squash_tile("th_w2", 1, 24576) + squash_tile("th_w3", 1, 30720) + squash_tile("th_v2", 1, 28672) + squash_tile("th_v3", 1, 26624))
+        planes = scaled_planes(1, 1, 17408)
+        leave(1, 0, product(("xm", 1), 0, ("g_first", 0), "diff1"), 0, HALF, shift=HALF)
+        scatter(1, 0, 0)
+        second_bank = product(("xm", 1), 1, ("g_first", 0), "diff2")
+        interleave(g1[:, HALF:N, :], planes[:])
+        quantize(("g", 1), flat(g1[:, HALF:N, :]), E5M2, HALF)
+        leave(1, 1, second_bank, 0, HALF, 18944, shift=HALF)
+        scatter(1, 1, 0)
         for k in range(2):
-            gradient(1, k, ((HALF, N, None),))
-        for k in (2, 3):
-            gradient(1, k, ((0, N, None),))
-        for b in range(B):
-            for k in range(D // P):
-                for piece in range(len(dws[b, k])):
-                    scatter(b, k, piece)
-                if b == 1 and k < 3:
-                    nc.sync.dma_start(out=out[k * P : (k + 1) * P, :], in_=placed[k][:])
+            gradient(1, k, "bank%d" % (k + 2), ((HALF, N, None),))
+            scatter(1, k, 1)
+            nc.sync.dma_start(out=out[k * P : (k + 1) * P, :], in_=placed[k][:])
+        gradient(1, 2, "bank0", ((0, N, None),))
+        scatter(1, 2, 0)
+        nc.sync.dma_start(out=out[2 * P : 3 * P, :], in_=placed[2][:])
+        gradient(1, 3, "bank1", ((0, N, None),))
+        scatter(1, 3, 0)
         nc.sync.dma_start(out=out[3 * P :, 0 : T // 2], in_=placed[3][:, 0 : T // 2])
         nc.scalar.dma_start(out=out[3 * P :, T // 2 :], in_=placed[3][:, T // 2 :])

@@ -224,10 +224,15 @@ def tile_attend_gds_nce_kernel(tc, xT, wT, vT, wt, xm, offs, out):
         bring(vT, "v", 1, 1792, T, 1792 + (T - 1792) * 3 // 8, 24576 + 8 * (1792 - 1024))
         held = staged.tile([P, PACK, P], F32, name="held", offset=28672)
         score("w", 0, 3, held[:])
-        xm0 = load_rows(xm[0])
+        xT1_rows = xT[1].rearrange("(p j) c -> p j c", j=PACK)
+        xT1a = staged.tile([P, PACK, HALF], F32, name="xT1a", offset=0)
+        nc.sync.dma_start(out=xT1a[:], in_=xT1_rows[:, :, 0:HALF])
         nc.sync.dma_start(out=weights[:], in_=wt.rearrange("b (p t) o -> p b (t o)", t=PACK))
-        xT1 = staged.tile([P, PACK, 512], F32, name="xT1", offset=0)
-        nc.sync.dma_start(out=xT1[:], in_=xT[1].rearrange("(p j) c -> p j c", j=PACK))
+        xm0 = load_rows(xm[0], 0, HALF)
+        xT1b = staged.tile([P, PACK, HALF], F32, name="xT1b", offset=4096)
+        nc.sync.dma_start(out=xT1b[:], in_=xT1_rows[:, :, HALF:])
+        xm0b = staged.tile([P, PACK, HALF], F32, name="xm0b", offset=8192)
+        nc.sync.dma_start(out=xm0b[:], in_=xm[0].rearrange("(p j) c -> p j c", j=PACK)[:, :, HALF:])
         xm1 = staged.tile([P, PACK, 512], F32, name="xm1", offset=16384)
         nc.sync.dma_start(out=xm1[:], in_=xm[1].rearrange("(p j) c -> p j c", j=PACK))
 
@@ -241,6 +246,9 @@ def tile_attend_gds_nce_kernel(tc, xT, wT, vT, wt, xm, offs, out):
             woven.bitcast(I32).rearrange("p (c i u) -> p c u i", i=4, u=2),
             blocks[:, 1:9:7, :].bitcast(I32).rearrange("p u (c i) -> p c u i", i=4),
         )
+        xT1_grouped = keep.tile([P, HALF, PACK], BF16, name="xT1_grouped", align_bytes=64)
+        interleave(xT1_grouped[:, 0:HALF, :], xT1a[:])
+        quantize(("xT", 1), flat(xT1_grouped[:, 0:HALF, :]), E4M3, 0)
         xm0_parts = {}
 
         def group_xm0(k):
@@ -266,10 +274,11 @@ def tile_attend_gds_nce_kernel(tc, xT, wT, vT, wt, xm, offs, out):
                 MULT,
             )
 
-        g0a = shared.tile([P, HALF, PACK], BF16, name="g0a", align_bytes=64, offset=4096)
-        g0b = shared.tile([P, HALF, PACK], BF16, name="g0b", align_bytes=64, offset=12288)
-        for k in range(4):
+        g0a = shared.tile([P, HALF, PACK], BF16, name="g0a", align_bytes=64, offset=8192)
+        for k in range(2):
             group_xm0(k)
+        xT1b_grouped = keep.tile([P, HALF, PACK], BF16, name="xT1b_grouped", align_bytes=64)
+        interleave(xT1b_grouped[:], xT1b[:])
         weigh(g0a[:, 0:128, :], 0)
         late_words = shared.tile([P, HALF], U32, name="late_words", align_bytes=64, offset=16384)
         late_scales = shared.tile([P, HALF], U8, name="late_scales", align_bytes=64, offset=17408)
@@ -288,17 +297,25 @@ def tile_attend_gds_nce_kernel(tc, xT, wT, vT, wt, xm, offs, out):
         scatter(0, 0, 0)
         for c in (2, 3):
             turn("v", 0, c, squashed[c])
-        picked_v1 = shared.tile([P, N, 2], U32, name="picked_v1", align_bytes=64, offset=4096)
+        picked_v1 = shared.tile([P, N, 2], U32, name="picked_v1", align_bytes=64, offset=1536)
         nc.vector.tensor_copy(
             picked_v1[:].bitcast(I32).rearrange("p (h c i) u -> p h c u i", h=2, i=4),
             teacher[:, 2 * HALF : 2 * HALF + 14 * HALF].bitcast(I32).rearrange("p (u h c i) -> p h c u i", u=2, h=7, i=4)[:, 0:2],
         )
         quantize_xm0(1)
-        quantize_xm0(3)
+        quantize(("xT", 1), flat(xT1b_grouped[:]), E4M3, HALF)
         quantize(("v", 1), flat(picked_v1[:]).bitcast(BF16), E4M3, 0)
-        quantize_xm0(2)
         second_bank = product(("xm", 0), 1, ("g_first", 0), "bank1")
-        third_bank = product(("xm", 0), 2, ("g_first", 0), "bank2")
+        xm0_rest = shared.tile([P, HALF, PACK], BF16, name="xm0_rest", align_bytes=64, offset=9728)
+        interleave(xm0_rest[:], xm0b[:])
+        quantize(("xm", 0), flat(xm0_rest[:]), E4M3, HALF)
+        dw = staged.tile([P, HALF], F32, name="dw_after_xm0", offset=8192)
+        nc.scalar.activation(dw[:], second_bank[:, HALF:N], COPY, scale=0.5)
+        dws[0, 1] = [(0, HALF, dw)]
+        scatter(0, 1, 0)
+        early_banks = [product(("xm", 0), k, ("g_first", 0), "bank%d" % k) for k in (2, 3)]
+
+        g0b = shared.tile([P, HALF, PACK], BF16, name="g0b", align_bytes=64, offset=11264)
 
         def chunk_planes(c, pool, offset):
             planes = pool.tile([P, PACK, P], BF16, name="planes%d" % c, align_bytes=64, offset=offset)
@@ -313,24 +330,14 @@ def tile_attend_gds_nce_kernel(tc, xT, wT, vT, wt, xm, offs, out):
                 nc.scalar.activation(planes[:, t, :], src, COPY, scale=weights[:, b, t : t + 1])
             return planes
 
-        xT1_grouped = shared.tile([P, 512, PACK], BF16, name="xT1_grouped", align_bytes=64, offset=5120)
-        interleave_on_gpsimd(xT1_grouped[:, 0:P, :], xT1[:, :, 0:P])
-        chunk_planes(2, shared, 11264)
-        leave(0, 1, second_bank, 0, HALF, shift=HALF)
-        scatter(0, 1, 0)
-        chunk_planes(3, staged, 8192)
-        quantize(("g", 0), flat(g0b[:]), E5M2, HALF)
-        for c in (128, 256, 384):
-            interleave(xT1_grouped[:, c : c + P, :], xT1[:, :, c : c + P])
-        quantize(("xT", 1), flat(xT1_grouped[:]), E4M3, 0)
-        dw = staged.tile([P, HALF], F32, name="dw_after_xT1", offset=7680)
-        nc.scalar.activation(dw[:], third_bank[:, HALF:N], COPY, scale=0.5)
-        dws[0, 2] = [(0, HALF, dw)]
+        chunk_planes(2, shared, 14336)
+        chunk_planes(3, shared, 15360)
+        leave(0, 2, early_banks[0], 0, HALF, shift=HALF)
         scatter(0, 2, 0)
-        for k in range(2):
-            gradient(0, k, "bank%d" % k, ((HALF, N, None),))
-            scatter(0, k, 1)
-        xm1_grouped = shared.tile([P, 512, PACK], BF16, name="xm1_grouped", align_bytes=64, offset=5120)
+        quantize(("g", 0), flat(g0b[:]), E5M2, HALF)
+        leave(0, 3, early_banks[1], 0, HALF, 15360, shift=HALF)
+        scatter(0, 3, 0)
+        xm1_grouped = shared.tile([P, 512, PACK], BF16, name="xm1_grouped", align_bytes=64, offset=10240)
         for c in range(0, 512, 128):
             interleave_on_gpsimd(xm1_grouped[:, c : c + 128, :], xm1[:, :, c : c + 128])
         g1 = keep.tile([P, N, PACK], BF16, name="g1", align_bytes=64)
@@ -346,22 +353,22 @@ def tile_attend_gds_nce_kernel(tc, xT, wT, vT, wt, xm, offs, out):
             tile = staged.tile([P, count, PACK, P], F32, name=name, offset=offset)
             return [tile[:, j] for j in range(count)]
 
-        heads((("w", 0), ("w", 1), ("v", 0), ("v", 1)), ("diff2", "diff3", "bank3", "bank2"),
+        heads((("w", 0), ("w", 1), ("v", 0), ("v", 1)), ("bank0", "bank1", "diff2", "diff3"),
               squash_tile("th_w01", 2, 24576) + squash_tile("th_v0", 1, 28672) + squash_tile("th_v1", 1, 30720))
+        planes = scaled_planes(1, 0, 16384)
+        for k, tag in ((0, "bank2"), (1, "bank0")):
+            gradient(0, k, tag, ((HALF, N, None),))
+            scatter(0, k, 1)
+        interleave(g1[:, 0:HALF, :], planes[:])
+        late_banks = [product(("xm", 0), k, ("g", 0), tag) for k, tag in ((2, "bank3"), (3, "bank2"))]
         quantize(("xm", 1), flat(xm1_grouped[:]), E4M3, 0)
-        last_bank = product(("xm", 0), 3, ("g", 0), "bank1")
-        for k, bank, i0, offset in ((2, product(("xm", 0), 2, ("g", 0), "bank0"), HALF, 16384), (3, last_bank, 0, 17408)):
-            dw = staged.tile([P, HALF], F32, name="dw_after_xm1_%d" % k, offset=offset)
-            nc.scalar.activation(dw[:], bank[:, i0 : i0 + HALF], COPY, scale=0.5)
-            dws.setdefault((0, k), []).append((i0, i0 + HALF, dw))
-            scatter(0, k, -1)
-        interleave_on_gpsimd(g1[:, 0:HALF, :], scaled_planes(1, 0, 16384)[:])
         quantize(("g", 1), flat(g1[:, 0:HALF, :]), E5M2, 0)
-        leave(0, 3, last_bank, HALF, N, 15872)
-        scatter(0, 3, 1)
-        heads((("w", 2), ("w", 3), ("v", 2), ("v", 3)), ("bank3", "bank2", "bank0", "diff1"),
+        for k in (2, 3):
+            leave(0, k, late_banks[k - 2], HALF, N, 16384 + 1024 * (k - 2))
+            scatter(0, k, 1)
+        heads((("w", 2), ("w", 3), ("v", 2), ("v", 3)), ("bank1", "bank0", "diff0", "diff1"),
               squash_tile("th_w2", 1, 24576) + squash_tile("th_w3", 1, 30720) + squash_tile("th_v2", 1, 28672) + squash_tile("th_v3", 1, 26624))
-        planes = scaled_planes(1, 1, 17408)
+        planes = scaled_planes(1, 1, 18432)
         leave(1, 0, product(("xm", 1), 0, ("g_first", 0), "diff1"), 0, HALF, shift=HALF)
         scatter(1, 0, 0)
         second_bank = product(("xm", 1), 1, ("g_first", 0), "diff2")

@@ -131,7 +131,8 @@ def tile_attend_gds_nce_kernel(tc, xT, wT, vT, wt, xm, offs, out):
 
         def diff_bank(b, q):
             if (b, q) not in diffs:
-                diffs[b, q] = diff_psum.tile([P, PACK, P], F32, name="diff%d" % q, tag="diff%d" % q)
+                tag = "bank%d" % q if b == 1 and q >= 2 else "diff%d" % q
+                diffs[b, q] = diff_psum.tile([P, PACK, P], F32, name=tag, tag=tag)
             return diffs[b, q]
 
         def squash(name, th, bank, t0=0, t1=PACK):
@@ -172,7 +173,7 @@ def tile_attend_gds_nce_kernel(tc, xT, wT, vT, wt, xm, offs, out):
             dws.setdefault((b, k), []).append((i0, i1, dw))
 
         def gradient(b, k, tag, pieces):
-            bank = product(("xm", b), k, ("g", b), tag)
+            bank = product(("xm", 0), k, ("g", 0), tag) if b == 0 else product(("xm1", k // 2), k % 2, ("g", 1), tag)
             for i0, i1, offset in pieces:
                 leave(b, k, bank, i0, i1, offset)
 
@@ -335,8 +336,6 @@ def tile_attend_gds_nce_kernel(tc, xT, wT, vT, wt, xm, offs, out):
         leave(0, 2, early_banks[0], 0, HALF, shift=HALF)
         scatter(0, 2, 0)
         quantize(("g", 0), flat(g0b[:]), E5M2, HALF)
-        leave(0, 3, early_banks[1], 0, HALF, 15360, shift=HALF)
-        scatter(0, 3, 0)
         xm1_grouped = shared.tile([P, 512, PACK], BF16, name="xm1_grouped", align_bytes=64, offset=10240)
         for c in range(0, 512, 128):
             interleave_on_gpsimd(xm1_grouped[:, c : c + 128, :], xm1[:, :, c : c + 128])
@@ -354,30 +353,42 @@ def tile_attend_gds_nce_kernel(tc, xT, wT, vT, wt, xm, offs, out):
             return [tile[:, j] for j in range(count)]
 
         heads((("w", 0), ("w", 1), ("v", 0), ("v", 1)), ("bank0", "bank1", "diff2", "diff3"),
-              squash_tile("th_w01", 2, 24576) + squash_tile("th_v0", 1, 28672) + squash_tile("th_v1", 1, 30720))
-        planes = scaled_planes(1, 0, 16384)
-        for k, tag in ((0, "bank2"), (1, "bank0")):
+              squash_tile("th_w0", 1, 12288) + squash_tile("th_w1", 1, 26624) + squash_tile("th_v0", 1, 28672) + squash_tile("th_v1", 1, 30720))
+        dw = staged.tile([P, HALF], F32, name="dw_after_turns", offset=12288)
+        nc.scalar.activation(dw[:], early_banks[1][:, HALF:N], COPY, scale=0.5)
+        dws[0, 3] = [(0, HALF, dw)]
+        scatter(0, 3, 0)
+        for k, tag in ((0, "diff2"), (1, "diff3")):
             gradient(0, k, tag, ((HALF, N, None),))
             scatter(0, k, 1)
+        planes = scaled_planes(1, 0, 16384)
         interleave(g1[:, 0:HALF, :], planes[:])
-        late_banks = [product(("xm", 0), k, ("g", 0), tag) for k, tag in ((2, "bank3"), (3, "bank2"))]
-        quantize(("xm", 1), flat(xm1_grouped[:]), E4M3, 0)
+        late_banks = [product(("xm", 0), k, ("g", 0), tag) for k, tag in ((2, "diff2"), (3, "diff3"))]
+        xm1_words = keep.tile([P, N], U32, name="xm1_words", align_bytes=64)
+
+        def quantize_xm1(h, offset):
+            scales = shared.tile([P, HALF], U8, name="xm1_scales%d" % h, align_bytes=64, offset=offset)
+            codes["xm1", h] = (xm1_words[:, h * HALF : (h + 1) * HALF], scales, E4M3)
+            quantize(("xm1", h), flat(xm1_grouped[:, h * HALF : (h + 1) * HALF, :]), E4M3, 0)
+
+        quantize_xm1(0, 17664)
         quantize(("g", 1), flat(g1[:, 0:HALF, :]), E5M2, 0)
         for k in (2, 3):
-            leave(0, k, late_banks[k - 2], HALF, N, 16384 + 1024 * (k - 2))
+            leave(0, k, late_banks[k - 2], HALF, N, 15616 + 1024 * (k - 2))
             scatter(0, k, 1)
         heads((("w", 2), ("w", 3), ("v", 2), ("v", 3)), ("bank1", "bank0", "diff0", "diff1"),
               squash_tile("th_w2", 1, 24576) + squash_tile("th_w3", 1, 30720) + squash_tile("th_v2", 1, 28672) + squash_tile("th_v3", 1, 26624))
         planes = scaled_planes(1, 1, 18432)
-        leave(1, 0, product(("xm", 1), 0, ("g_first", 0), "diff1"), 0, HALF, shift=HALF)
+        leave(1, 0, product(("xm1", 0), 0, ("g_first", 0), "diff1"), 0, HALF, shift=HALF)
         scatter(1, 0, 0)
-        second_bank = product(("xm", 1), 1, ("g_first", 0), "diff2")
+        second_bank = product(("xm1", 0), 1, ("g_first", 0), "bank2")
         interleave(g1[:, HALF:N, :], planes[:])
         quantize(("g", 1), flat(g1[:, HALF:N, :]), E5M2, HALF)
+        quantize_xm1(1, 19968)
         leave(1, 1, second_bank, 0, HALF, 18944, shift=HALF)
         scatter(1, 1, 0)
         for k in range(2):
-            gradient(1, k, "bank%d" % (k + 2), ((HALF, N, None),))
+            gradient(1, k, "diff%d" % (k + 2), ((HALF, N, None),))
             scatter(1, k, 1)
             nc.sync.dma_start(out=out[k * P : (k + 1) * P, :], in_=placed[k][:])
         gradient(1, 2, "bank0", ((0, N, None),))

@@ -213,9 +213,7 @@ def tile_attend_gds_nce_kernel(tc, xT, wT, vT, wt, xm, offs, out):
             score("w", 0, c, early[:, c])
         teacher = keep.tile([P, 16 * HALF], U32, name="teacher", align_bytes=64)
         blocks = teacher[:].rearrange("p (k n) -> p k n", n=HALF)
-        first_words = teacher[:, 8 * HALF + P : 10 * HALF + P].rearrange("p (i u) -> p i u", u=2)
-        nc.vector.tensor_copy(teacher[:, HALF : B * N], window_words("v", 0).indirect(offsets[:, 16:]))
-        nc.vector.tensor_copy(first_words[:, :, 0], window_words("v", 0).indirect(offsets[:, 0:16]))
+        nc.vector.tensor_copy(teacher[:, 0 : B * N], window_words("v", 0).indirect(offsets[:]))
 
         def gather_half(q, block):
             nc.vector.tensor_copy(blocks[:, block, :], window_words("v", 1).indirect(offsets[:, q * 16 : (q + 1) * 16]))
@@ -237,16 +235,23 @@ def tile_attend_gds_nce_kernel(tc, xT, wT, vT, wt, xm, offs, out):
         xm1 = staged.tile([P, PACK, 512], F32, name="xm1", offset=16384)
         nc.sync.dma_start(out=xm1[:], in_=xm[1].rearrange("(p j) c -> p j c", j=PACK))
 
-        nc.vector.tensor_copy(first_words[:, :, 1], window_words("v", 1).indirect(offsets[:, 0:16]))
+        pairs = teacher[:, 0 : 8 * HALF].rearrange("p (u n) -> p u n", u=2)
+        for q in range(2):
+            gather_half(q, 4 + q)
         for c in range(2):
-            quantize(("v", 0), flat(first_words[:, c * P : (c + 1) * P, :]).bitcast(BF16), E4M3, c * P)
-        for q in (1, 2, 3):
+            nc.scalar.copy(
+                teacher[:, (8 + c) * HALF + P : (9 + c) * HALF + P].rearrange("p (c i u) -> p c u i", i=4, u=2),
+                pairs[:, :, c * P : (c + 1) * P].rearrange("p u (c i) -> p c u i", i=4),
+            )
+            quantize(("v", 0), teacher[:, (8 + c) * HALF + P : (9 + c) * HALF + P].bitcast(BF16), E4M3, c * P)
+        for q in (2, 3):
             gather_half(q, 7 + q)
-        woven = teacher[:, 4 * HALF : 6 * HALF]
+        woven = teacher[:, 7 * HALF : 9 * HALF]
         nc.vector.tensor_copy(
             woven.bitcast(I32).rearrange("p (c i u) -> p c u i", i=4, u=2),
-            blocks[:, 1:9:7, :].bitcast(I32).rearrange("p u (c i) -> p c u i", i=4),
+            pairs[:, :, HALF:N].bitcast(I32).rearrange("p u (c i) -> p c u i", i=4),
         )
+        quantize(("v", 0), woven.bitcast(BF16), E4M3, HALF)
         xT1_grouped = keep.tile([P, HALF, PACK], BF16, name="xT1_grouped", align_bytes=64)
         interleave(xT1_grouped[:, 0:HALF, :], xT1a[:])
         quantize(("xT", 1), flat(xT1_grouped[:, 0:HALF, :]), E4M3, 0)
@@ -259,9 +264,8 @@ def tile_attend_gds_nce_kernel(tc, xT, wT, vT, wt, xm, offs, out):
         def quantize_xm0(k):
             quantize(("xm", 0), flat(xm0_parts[k][:]), E4M3, k * P)
 
-        first_th = shared.tile([P, PACK, P], F32, name="first_th", align_bytes=64, offset=16384)
         for c in range(2):
-            th = first_th[:] if c == 0 else ring_th()
+            th = ring_th()
             halves = [product(("v", 0), c, ("xT", 0), "bank%d" % (2 * c + h), h * HALF, (h + 1) * HALF) for h in range(2)]
             for h in range(2):
                 squash("v", th, halves[h], 2 * h, 2 * h + 2)
@@ -281,10 +285,6 @@ def tile_attend_gds_nce_kernel(tc, xT, wT, vT, wt, xm, offs, out):
         xT1b_grouped = keep.tile([P, HALF, PACK], BF16, name="xT1b_grouped", align_bytes=64)
         interleave(xT1b_grouped[:], xT1b[:])
         weigh(g0a[:, 0:128, :], 0)
-        late_words = shared.tile([P, HALF], U32, name="late_words", align_bytes=64, offset=16384)
-        late_scales = shared.tile([P, HALF], U8, name="late_scales", align_bytes=64, offset=17408)
-        codes["v_late", 0] = (late_words, late_scales, E4M3)
-        quantize(("v_late", 0), woven.bitcast(BF16), E4M3, 0)
         weigh(g0a[:, 128:256, :], 1)
         quantize_xm0(0)
         quantize(("g", 0), flat(g0a[:]), E5M2, 0)
@@ -293,7 +293,7 @@ def tile_attend_gds_nce_kernel(tc, xT, wT, vT, wt, xm, offs, out):
         squashed = {}
         for c in (2, 3):
             squashed[c] = ring_th()
-            squash("v", squashed[c], product(("v_late", 0), c - 2, ("xT", 0), "diff%d" % (c - 2)))
+            squash("v", squashed[c], product(("v", 0), c, ("xT", 0), "diff%d" % (c - 2)))
         leave(0, 0, first_bank, 0, HALF, shift=HALF)
         scatter(0, 0, 0)
         for c in (2, 3):
@@ -314,7 +314,7 @@ def tile_attend_gds_nce_kernel(tc, xT, wT, vT, wt, xm, offs, out):
         nc.scalar.activation(dw[:], second_bank[:, HALF:N], COPY, scale=0.5)
         dws[0, 1] = [(0, HALF, dw)]
         scatter(0, 1, 0)
-        early_banks = [product(("xm", 0), k, ("g_first", 0), "bank%d" % k) for k in (2, 3)]
+        early_banks = [product(("xm", 0), 2, ("g_first", 0), "bank2")]
 
         g0b = shared.tile([P, HALF, PACK], BF16, name="g0b", align_bytes=64, offset=11264)
 
@@ -336,10 +336,16 @@ def tile_attend_gds_nce_kernel(tc, xT, wT, vT, wt, xm, offs, out):
         leave(0, 2, early_banks[0], 0, HALF, shift=HALF)
         scatter(0, 2, 0)
         quantize(("g", 0), flat(g0b[:]), E5M2, HALF)
-        xm1_grouped = shared.tile([P, 512, PACK], BF16, name="xm1_grouped", align_bytes=64, offset=10240)
-        for c in range(0, 512, 128):
-            interleave_on_gpsimd(xm1_grouped[:, c : c + 128, :], xm1[:, :, c : c + 128])
-        g1 = keep.tile([P, N, PACK], BF16, name="g1", align_bytes=64)
+        xm1_halves = {}
+
+        def group_xm1(h, offset):
+            xm1_halves[h] = shared.tile([P, HALF, PACK], BF16, name="xm1_grouped%d" % h, align_bytes=64, offset=offset)
+            for c in (0, P):
+                interleave_on_gpsimd(xm1_halves[h][:, c : c + P, :], xm1[:, :, h * HALF + c : h * HALF + c + P])
+
+        group_xm1(0, 10240)
+        g1a = shared.tile([P, HALF, PACK], BF16, name="g1a", align_bytes=64, offset=0)
+        g1b = keep.tile([P, HALF, PACK], BF16, name="g1b", align_bytes=64)
         codes["g", 1] = codes["g", 0]
 
         def heads(steps, tags, squashed):
@@ -352,38 +358,48 @@ def tile_attend_gds_nce_kernel(tc, xT, wT, vT, wt, xm, offs, out):
             tile = staged.tile([P, count, PACK, P], F32, name=name, offset=offset)
             return [tile[:, j] for j in range(count)]
 
-        heads((("w", 0), ("w", 1), ("v", 0), ("v", 1)), ("bank0", "bank1", "diff2", "diff3"),
-              squash_tile("th_w0", 1, 12288) + squash_tile("th_w1", 1, 26624) + squash_tile("th_v0", 1, 28672) + squash_tile("th_v1", 1, 30720))
-        dw = staged.tile([P, HALF], F32, name="dw_after_turns", offset=12288)
-        nc.scalar.activation(dw[:], early_banks[1][:, HALF:N], COPY, scale=0.5)
-        dws[0, 3] = [(0, HALF, dw)]
-        scatter(0, 3, 0)
-        for k, tag in ((0, "diff2"), (1, "diff3")):
-            gradient(0, k, tag, ((HALF, N, None),))
-            scatter(0, k, 1)
+        first_steps = (("w", 0), ("w", 1), ("v", 0), ("v", 1))
+        score_banks = [product((name, 1), c, ("xT", 1), tag) for (name, c), tag in zip(first_steps, ("bank0", "bank1", "diff2", "diff3"))]
+        squashed = squash_tile("th_w01", 2, 24576) + squash_tile("th_v0", 1, 28672) + squash_tile("th_v1", 1, 30720)
+        for (name, c), bank, th in zip(first_steps, score_banks, squashed):
+            squash_rows(name, th, bank)
+            if (name, c) == ("w", 0):
+                leave(0, 3, product(("xm", 0), 3, ("g_first", 0), "bank0"), 0, HALF, shift=HALF)
+                scatter(0, 3, 0)
+            if (name, c) == ("w", 1):
+                student_banks = [product(("w", 1), c, ("xT", 1), tag) for c, tag in ((2, "bank3"), (3, "bank1"))]
+            if (name, c) == ("v", 1):
+                gradient(0, 0, "diff2", ((HALF, N, None),))
+                scatter(0, 0, 1)
+            turn(name, 1, c, th)
+        gradient(0, 1, "diff3", ((HALF, N, None),))
+        scatter(0, 1, 1)
         planes = scaled_planes(1, 0, 16384)
-        interleave(g1[:, 0:HALF, :], planes[:])
+        interleave(g1a[:], planes[:])
         late_banks = [product(("xm", 0), k, ("g", 0), tag) for k, tag in ((2, "diff2"), (3, "diff3"))]
         xm1_words = keep.tile([P, N], U32, name="xm1_words", align_bytes=64)
 
         def quantize_xm1(h, offset):
             scales = shared.tile([P, HALF], U8, name="xm1_scales%d" % h, align_bytes=64, offset=offset)
             codes["xm1", h] = (xm1_words[:, h * HALF : (h + 1) * HALF], scales, E4M3)
-            quantize(("xm1", h), flat(xm1_grouped[:, h * HALF : (h + 1) * HALF, :]), E4M3, 0)
+            quantize(("xm1", h), flat(xm1_halves[h][:]), E4M3, 0)
 
         quantize_xm1(0, 17664)
-        quantize(("g", 1), flat(g1[:, 0:HALF, :]), E5M2, 0)
+        quantize(("g", 1), flat(g1a[:]), E5M2, 0)
+        group_xm1(1, 0)
         for k in (2, 3):
             leave(0, k, late_banks[k - 2], HALF, N, 15616 + 1024 * (k - 2))
             scatter(0, k, 1)
-        heads((("w", 2), ("w", 3), ("v", 2), ("v", 3)), ("bank1", "bank0", "diff0", "diff1"),
-              squash_tile("th_w2", 1, 24576) + squash_tile("th_w3", 1, 30720) + squash_tile("th_v2", 1, 28672) + squash_tile("th_v3", 1, 26624))
+        for c, bank, th in zip((2, 3), student_banks, squash_tile("th_w23", 2, 12288)):
+            squash_rows("w", th, bank)
+            turn("w", 1, c, th)
+        heads((("v", 2), ("v", 3)), ("diff0", "diff1"), squash_tile("th_v23", 2, 24576))
         planes = scaled_planes(1, 1, 18432)
         leave(1, 0, product(("xm1", 0), 0, ("g_first", 0), "diff1"), 0, HALF, shift=HALF)
         scatter(1, 0, 0)
         second_bank = product(("xm1", 0), 1, ("g_first", 0), "bank2")
-        interleave(g1[:, HALF:N, :], planes[:])
-        quantize(("g", 1), flat(g1[:, HALF:N, :]), E5M2, HALF)
+        interleave(g1b[:], planes[:])
+        quantize(("g", 1), flat(g1b[:]), E5M2, HALF)
         quantize_xm1(1, 19968)
         leave(1, 1, second_bank, 0, HALF, 18944, shift=HALF)
         scatter(1, 1, 0)

@@ -148,7 +148,7 @@ def tile_attend_gds_nce_kernel(tc, xT, wT, vT, wt, xm, offs, out):
         def turn(name, b, c, th, t0=0, t1=PACK):
             first = name == "w"
             for t in range(t0, t1):
-                if b == 0:
+                if b == 0 and c < 2:
                     q, place = c, t
                     opens, closes = t == 0, t == PACK - 1
                 else:
@@ -219,8 +219,8 @@ def tile_attend_gds_nce_kernel(tc, xT, wT, vT, wt, xm, offs, out):
             nc.vector.tensor_copy(blocks[:, block, :], window_words("v", 1).indirect(offsets[:, q * 16 : (q + 1) * 16]))
 
         bring(vT, "v", 1, 0, 1024, 640, 16384)
-        bring(vT, "v", 1, 1024, 1792, 1024 + 192, 24576)
-        bring(vT, "v", 1, 1792, T, 1792 + (T - 1792) * 3 // 8, 24576 + 8 * (1792 - 1024))
+        bring(vT, "v", 1, 1024, 1792, 1024 + 128, 24576)
+        bring(vT, "v", 1, 1792, T, 1792 + 96, 24576 + 8 * (1792 - 1024))
         held = staged.tile([P, PACK, P], F32, name="held", offset=28672)
         score("w", 0, 3, held[:])
         xT1_rows = xT[1].rearrange("(p j) c -> p j c", j=PACK)
@@ -318,12 +318,6 @@ def tile_attend_gds_nce_kernel(tc, xT, wT, vT, wt, xm, offs, out):
 
         g0b = shared.tile([P, HALF, PACK], BF16, name="g0b", align_bytes=64, offset=11264)
 
-        def chunk_planes(c, pool, offset):
-            planes = pool.tile([P, PACK, P], BF16, name="planes%d" % c, align_bytes=64, offset=offset)
-            for t in range(PACK):
-                nc.scalar.activation(planes[:, t, :], diffs[0, c][:, t, :], COPY, scale=weights[:, 0, t : t + 1])
-            interleave_on_gpsimd(g0b[:, (c - 2) * P : (c - 1) * P, :], planes[:])
-
         def scaled_planes(b, h, offset):
             planes = shared.tile([P, PACK, HALF], BF16, name="planes%d%d" % (b, h), align_bytes=64, offset=offset)
             for t in range(PACK):
@@ -331,8 +325,7 @@ def tile_attend_gds_nce_kernel(tc, xT, wT, vT, wt, xm, offs, out):
                 nc.scalar.activation(planes[:, t, :], src, COPY, scale=weights[:, b, t : t + 1])
             return planes
 
-        chunk_planes(2, shared, 14336)
-        chunk_planes(3, shared, 15360)
+        interleave_on_gpsimd(g0b[:], scaled_planes(0, 1, 13312)[:])
         leave(0, 2, early_banks[0], 0, HALF, shift=HALF)
         scatter(0, 2, 0)
         quantize(("g", 0), flat(g0b[:]), E5M2, HALF)
@@ -390,7 +383,7 @@ def tile_attend_gds_nce_kernel(tc, xT, wT, vT, wt, xm, offs, out):
         for k in (2, 3):
             leave(0, k, late_banks[k - 2], HALF, N, 15616 + 1024 * (k - 2))
             scatter(0, k, 1)
-        for c, bank, th in zip((2, 3), student_banks, squash_tile("th_w23", 2, 12288)):
+        for c, bank, th in zip((2, 3), student_banks, squash_tile("th_w2", 1, 12288) + squash_tile("th_w3", 1, 30720)):
             squash_rows("w", th, bank)
             turn("w", 1, c, th)
         heads((("v", 2), ("v", 3)), ("diff0", "diff1"), squash_tile("th_v23", 2, 24576))

@@ -21,8 +21,16 @@ TANH = mybir.ActivationFunctionType.Tanh
 
 P = 128
 PACK = 4
-LIST_COLS = N // 16
+PER_COL = 16
 HALF = N // 2
+RUN = 4
+KB = 1024
+
+STUDENT_PIECES = (("w", 0, 0, T, 768, 0), ("w", 1, 0, T, 704, 16 * KB))
+TEACHER_PIECES = (
+    (("v", 0, 0, 1024, 1024, 0), ("v", 0, 1024, T, 512, 8 * KB)),
+    (("v", 1, 0, 1024, 640, 16 * KB), ("v", 1, 1024, 1792, 128, 24 * KB), ("v", 1, 1792, T, 96, 30 * KB)),
+)
 
 
 def tile_attend_gds_nce_kernel(tc, xT, wT, vT, wt, xm, offs, out):
@@ -33,89 +41,89 @@ def tile_attend_gds_nce_kernel(tc, xT, wT, vT, wt, xm, offs, out):
         staged = ctx.enter_context(tc.tile_pool(name="staged", bufs=1))
         shared = ctx.enter_context(tc.tile_pool(name="shared", bufs=1))
         ring = ctx.enter_context(tc.tile_pool(name="ring", bufs=4))
-        diff_psum = ctx.enter_context(tc.psum_pool(name="diff_psum", bufs=1))
+        psum = ctx.enter_context(tc.psum_pool(name="psum", bufs=1))
 
-        offsets = keep.tile([P, B * LIST_COLS], U16, name="offsets")
+        offsets = keep.tile([P, B * N // PER_COL], U16, name="offsets")
         weights = keep.tile([P, B, PACK], F32, name="weights")
         ident = keep.tile([P, P], F32, name="ident")
         placed = [keep.tile([P, T], F32, name="placed%d" % k) for k in range(D // P)]
 
         make_identity(nc, ident[:])
         for k, tile in enumerate(placed):
-            (nc.vector if k < 3 else nc.gpsimd).memset(tile[:], 0.0)
+            (nc.vector if k < len(placed) - 1 else nc.gpsimd).memset(tile[:], 0.0)
 
-        def group_offsets(b, i0=0, i1=N):
-            return offsets[:, b * LIST_COLS + i0 // 16 : b * LIST_COLS + i1 // 16]
+        def entries(first, count):
+            return offsets[:, first // PER_COL : (first + count) // PER_COL]
 
-        windows = {}
-        picked = {}
         codes = {}
         padded_words = keep.tile([P, HALF + N], U32, name="padded_words", align_bytes=64)
         padded_scales = keep.tile([P, HALF + N], U8, name="padded_scales", align_bytes=64)
         nc.gpsimd.memset(padded_words[:, 0:HALF], 0)
         nc.gpsimd.memset(padded_scales[:, 0:HALF], 0)
-        codes["g", 0] = (padded_words[:, HALF:], padded_scales[:, HALF:], E5M2)
-        for name in ("w", "v"):
+        codes["g"] = (padded_words[:, HALF:], padded_scales[:, HALF:], E5M2)
+        codes["g_first"] = (padded_words[:, 0:N], padded_scales[:, 0:N], E5M2)
+
+        tables = {"w": wT, "v": vT}
+        windows = {}
+        for name in tables:
             for u in range(2):
                 windows[name, u] = keep.tile([P, T, 2], BF16, name="win_%s%d" % (name, u), align_bytes=64)
 
-        def load_table(table, u, c0, c1, offset, name):
-            stage = staged.tile([P, 2, c1 - c0], F32, name=name, offset=offset)
-            rows = table.rearrange("(p j) c -> p j c", j=PACK)
-            nc.sync.dma_start(out=stage[:], in_=rows[:, 2 * u : 2 * u + 2, c0:c1])
-            return stage
-
-        def cast_table(name, u, base, c0, c1, stage, on_scalar):
-            src = stage[:, :, c0 - base : c1 - base].rearrange("p e (c i) -> p c e i", i=4)
-            dst = windows[name, u][:, c0:c1, :].rearrange("p (c i) e -> p c e i", i=4)
-            if on_scalar:
-                nc.scalar.activation(dst, src, COPY)
-            else:
-                nc.vector.tensor_copy(dst, src)
-
-        def load_rows(src, c0=0, c1=512):
-            stage = raw.tile([P, PACK, c1 - c0], F32, name="stage", tag="stage")
-            nc.sync.dma_start(out=stage[:], in_=src.rearrange("(p j) c -> p j c", j=PACK)[:, :, c0:c1])
-            return stage
-
-        def window_words(name, u):
-            return windows[name, u][:].rearrange("p c e -> p (c e)").bitcast(U32)
-
-        def gather(name, u, b, i0=0, i1=N):
-            if (name, b) not in picked:
-                tag = "picked_w%d" % b
-                picked[name, b] = keep.tile([P, N, 2], U32, name=tag, tag=tag, align_bytes=64)[:]
-            nc.vector.tensor_copy(picked[name, b][:, i0:i1, u], window_words(name, u).indirect(group_offsets(b, i0, i1)))
+        def by_rows(src):
+            return src.rearrange("(p t) c -> p t c", t=PACK)
 
         def flat(view):
             return view.rearrange("p a b -> p (a b)")
 
-        def quantize(key, values, fmt, c0):
+        def bring(name, u, c0, c1, on_scalar, offset):
+            stage = staged.tile([P, 2, c1 - c0], F32, name="stage_%s%d_%d" % (name, u, c0), offset=offset)
+            nc.sync.dma_start(out=stage[:], in_=by_rows(tables[name])[:, 2 * u : 2 * u + 2, c0:c1])
+            src = stage[:].rearrange("p e (c i) -> p c e i", i=RUN)
+            dst = windows[name, u][:, c0:c1, :].rearrange("p (c i) e -> p c e i", i=RUN)
+            split = on_scalar // RUN
+            nc.scalar.activation(dst[:, 0:split], src[:, 0:split], COPY)
+            if on_scalar < c1 - c0:
+                nc.vector.tensor_copy(dst[:, split:], src[:, split:])
+
+        def load(pool, name, src, c0, c1, **place):
+            stage = pool.tile([P, PACK, c1 - c0], F32, name=name, **place)
+            nc.sync.dma_start(out=stage[:], in_=by_rows(src)[:, :, c0:c1])
+            return stage
+
+        def gather(dst, name, u, first, count):
+            words = windows[name, u][:].rearrange("p c e -> p (c e)").bitcast(U32)
+            nc.vector.tensor_copy(dst, words.indirect(entries(first, count)))
+
+        def weave(dst, pairs, on_scalar):
+            if on_scalar:
+                move, dtype = nc.scalar.copy, U32
+            else:
+                move, dtype = nc.vector.tensor_copy, I32
+            move(
+                dst.bitcast(dtype).rearrange("p (c i u) -> p c u i", i=RUN, u=2),
+                pairs.bitcast(dtype).rearrange("p u (c i) -> p c u i", i=RUN),
+            )
+
+        def quantize(key, values, c0):
             if key not in codes:
-                words = keep.tile([P, 512], U32, name="words_%s%d" % key, align_bytes=64)
-                scales = keep.tile([P, 512], U8, name="scales_%s%d" % key, align_bytes=64)
-                codes[key] = (words, scales, fmt)
+                words = keep.tile([P, N], U32, name="words_" + key, align_bytes=64)
+                scales = keep.tile([P, N], U8, name="scales_" + key, align_bytes=64)
+                codes[key] = (words, scales, E4M3)
             words, scales, fmt = codes[key]
             c1 = c0 + values.shape[1] // PACK
             nc.vector.quantize_mx(out=words[:, c0:c1].bitcast(fmt), scales=scales[:, c0:c1], in_=values)
 
         def interleave(dst, src):
-            nc.scalar.copy(dst.rearrange("p (c i) j -> p c j i", i=4), src.rearrange("p j (c i) -> p c j i", i=4))
-
-        def deal(dst, src, m0, m1):
-            nc.scalar.copy(
-                dst.rearrange("p (t m) j -> p m j t", t=PACK)[:, m0:m1],
-                src.rearrange("p j (m t) -> p m j t", t=PACK)[:, m0:m1],
-            )
+            nc.scalar.copy(dst.rearrange("p (c i) t -> p c t i", i=RUN), src.rearrange("p t (c i) -> p c t i", i=RUN))
 
         def interleave_on_gpsimd(dst, src):
-            nc.gpsimd.tensor_scalar(dst, src.rearrange("p j c -> p c j"), 1.0, 0.0, MULT, ADD)
+            nc.gpsimd.tensor_scalar(dst, src.rearrange("p t c -> p c t"), 1.0, 0.0, MULT, ADD)
 
-        def product(stationary, k, moving, tag, n0=0, n1=512):
-            bank = diff_psum.tile([P, 512], F32, name=tag, tag=tag)
+        def product(stationary, block, moving, bank_name, n0=0, n1=N):
+            bank = psum.tile([P, N], F32, name=bank_name, tag=bank_name)
             s_words, s_scales, s_fmt = codes[stationary]
             m_words, m_scales, m_fmt = codes[moving]
-            cols = slice(k * P, (k + 1) * P)
+            cols = slice(block * P, (block + 1) * P)
             nc.tensor.matmul_mx(
                 out=bank[:, n0:n1],
                 lhsT=s_words[:, cols].bitcast(s_fmt),
@@ -127,26 +135,13 @@ def tile_attend_gds_nce_kernel(tc, xT, wT, vT, wt, xm, offs, out):
             )
             return bank
 
+        def squash(name, b, th, bank, t0=0, t1=PACK):
+            rows = bank[:].rearrange("p (t m) -> p t m" if b == 0 else "p (m t) -> p t m", t=PACK)
+            nc.scalar.activation(th[:, t0:t1, :], rows[:, t0:t1, :], TANH, scale=0.5 if name == "w" else -0.5)
+
         diffs = {}
 
-        def diff_bank(b, q):
-            if (b, q) not in diffs:
-                tag = "bank%d" % q if b == 1 and q >= 2 else "diff%d" % q
-                diffs[b, q] = diff_psum.tile([P, PACK, P], F32, name=tag, tag=tag)
-            return diffs[b, q]
-
-        def squash(name, th, bank, t0=0, t1=PACK):
-            nc.scalar.activation(flat(th[:, t0:t1, :]), bank[:, t0 * P : t1 * P], TANH, scale=0.5 if name == "w" else -0.5)
-
-        def squash_rows(name, th, bank):
-            nc.scalar.activation(th, bank[:].rearrange("p (m t) -> p t m", t=PACK), TANH, scale=0.5 if name == "w" else -0.5)
-
-        def score(name, b, c, th):
-            squash(name, th, product((name, b), c, ("xT", b), "bank%d" % c))
-            turn(name, b, c, th)
-
         def turn(name, b, c, th, t0=0, t1=PACK):
-            first = name == "w"
             for t in range(t0, t1):
                 if b == 0 and c < 2:
                     q, place = c, t
@@ -154,124 +149,22 @@ def tile_attend_gds_nce_kernel(tc, xT, wT, vT, wt, xm, offs, out):
                 else:
                     q, place = 2 * (c // 2) + t // 2, 2 * (t % 2) + c % 2
                     opens, closes = c % 2 == 0 and t % 2 == 0, c % 2 == 1 and t % 2 == 1
+                if (b, q) not in diffs:
+                    bank_name = "bank%d" % q if b == 1 and q >= 2 else "diff%d" % q
+                    diffs[b, q] = psum.tile([P, PACK, P], F32, name=bank_name, tag=bank_name)
                 nc.tensor.matmul(
-                    diff_bank(b, q)[:, place, :], th[:, t, :], ident[:], is_transpose=True,
-                    start=first and opens, stop=(not first) and closes,
+                    diffs[b, q][:, place, :], th[:, t, :], ident[:], is_transpose=True,
+                    start=name == "w" and opens, stop=name == "v" and closes,
                 )
 
         def ring_th():
             return ring.tile([P, PACK, P], F32, name="th", tag="th")[:]
 
-        dws = {}
+        def staged_th(name, count, offset):
+            tile = staged.tile([P, count, PACK, P], F32, name=name, offset=offset)
+            return [tile[:, j] for j in range(count)]
 
-        def leave(b, k, bank, i0, i1, offset=None, shift=0):
-            if offset is not None:
-                dw = shared.tile([P, i1 - i0], F32, name="held_dw", align_bytes=64, offset=offset)
-            else:
-                dw = ring.tile([P, i1 - i0], F32, name="dw", tag="dw")
-            nc.scalar.activation(dw[:], bank[:, shift + i0 : shift + i1], COPY, scale=0.5)
-            dws.setdefault((b, k), []).append((i0, i1, dw))
-
-        def gradient(b, k, tag, pieces):
-            bank = product(("xm", 0), k, ("g", 0), tag) if b == 0 else product(("xm1", k // 2), k % 2, ("g", 1), tag)
-            for i0, i1, offset in pieces:
-                leave(b, k, bank, i0, i1, offset)
-
-        def scatter(b, k, piece):
-            i0, i1, dw = dws[b, k][piece]
-            nc.vector.tensor_copy(placed[k][:].indirect(group_offsets(b, i0, i1)), dw[:])
-
-        def bring(table, name, u, c0, c1, split, offset):
-            stage = load_table(table, u, c0, c1, offset, "stage_%s%d_%d" % (name, u, c0))
-            if split > c0:
-                cast_table(name, u, c0, c0, split, stage, True)
-            if split < c1:
-                cast_table(name, u, c0, split, c1, stage, False)
-
-        bring(wT, "w", 0, 0, T, 768, 0)
-        nc.sync.dma_start(offsets[:], offs)
-        student = keep.tile([P, 2, B * N], U32, name="student", align_bytes=64)
-        nc.vector.tensor_copy(student[:, 0, :], window_words("w", 0).indirect(offsets[:]))
-        bring(wT, "w", 1, 0, T, 704, 16384)
-        for b in range(B):
-            nc.vector.tensor_copy(student[:, 1, b * N : (b + 1) * N], window_words("w", 1).indirect(group_offsets(b)))
-        for b in range(B):
-            picked["w", b] = keep.tile([P, N, 2], U32, name="picked_w%d" % b, align_bytes=64)[:]
-            nc.vector.tensor_copy(
-                picked["w", b].bitcast(I32).rearrange("p (c i) u -> p c u i", i=4),
-                student[:, :, b * N : (b + 1) * N].bitcast(I32).rearrange("p u (c i) -> p c u i", i=4),
-            )
-        quantize(("w", 0), flat(picked["w", 0]).bitcast(BF16), E4M3, 0)
-        xT0_grouped = keep.tile([P, 512, PACK], BF16, name="xT0_grouped", align_bytes=64)
-        deal(xT0_grouped[:], load_rows(xT[0])[:], 0, P)
-        quantize(("xT", 0), flat(xT0_grouped[:]), E4M3, 0)
-        quantize(("w", 1), flat(picked["w", 1]).bitcast(BF16), E4M3, 0)
-        bring(vT, "v", 0, 0, 1024, 1024, 0)
-        bring(vT, "v", 0, 1024, T, 1536, 8192)
-        early = staged.tile([P, 3, PACK, P], F32, name="early", offset=8192)
-        for c in range(3):
-            score("w", 0, c, early[:, c])
-        teacher = keep.tile([P, 16 * HALF], U32, name="teacher", align_bytes=64)
-        blocks = teacher[:].rearrange("p (k n) -> p k n", n=HALF)
-        nc.vector.tensor_copy(teacher[:, 0 : B * N], window_words("v", 0).indirect(offsets[:]))
-
-        def gather_half(q, block):
-            nc.vector.tensor_copy(blocks[:, block, :], window_words("v", 1).indirect(offsets[:, q * 16 : (q + 1) * 16]))
-
-        bring(vT, "v", 1, 0, 1024, 640, 16384)
-        bring(vT, "v", 1, 1024, 1792, 1024 + 128, 24576)
-        bring(vT, "v", 1, 1792, T, 1792 + 96, 24576 + 8 * (1792 - 1024))
-        held = staged.tile([P, PACK, P], F32, name="held", offset=28672)
-        score("w", 0, 3, held[:])
-        xT1_rows = xT[1].rearrange("(p j) c -> p j c", j=PACK)
-        xT1a = staged.tile([P, PACK, HALF], F32, name="xT1a", offset=0)
-        nc.sync.dma_start(out=xT1a[:], in_=xT1_rows[:, :, 0:HALF])
-        nc.sync.dma_start(out=weights[:], in_=wt.rearrange("b (p t) o -> p b (t o)", t=PACK))
-        xm0 = load_rows(xm[0], 0, HALF)
-        xT1b = staged.tile([P, PACK, HALF], F32, name="xT1b", offset=4096)
-        nc.sync.dma_start(out=xT1b[:], in_=xT1_rows[:, :, HALF:])
-        xm0b = staged.tile([P, PACK, HALF], F32, name="xm0b", offset=8192)
-        nc.sync.dma_start(out=xm0b[:], in_=xm[0].rearrange("(p j) c -> p j c", j=PACK)[:, :, HALF:])
-        xm1 = staged.tile([P, PACK, 512], F32, name="xm1", offset=16384)
-        nc.sync.dma_start(out=xm1[:], in_=xm[1].rearrange("(p j) c -> p j c", j=PACK))
-
-        pairs = teacher[:, 0 : 8 * HALF].rearrange("p (u n) -> p u n", u=2)
-        for q in range(2):
-            gather_half(q, 4 + q)
-        for c in range(2):
-            nc.scalar.copy(
-                teacher[:, (8 + c) * HALF + P : (9 + c) * HALF + P].rearrange("p (c i u) -> p c u i", i=4, u=2),
-                pairs[:, :, c * P : (c + 1) * P].rearrange("p u (c i) -> p c u i", i=4),
-            )
-            quantize(("v", 0), teacher[:, (8 + c) * HALF + P : (9 + c) * HALF + P].bitcast(BF16), E4M3, c * P)
-        for q in (2, 3):
-            gather_half(q, 7 + q)
-        woven = teacher[:, 7 * HALF : 9 * HALF]
-        nc.vector.tensor_copy(
-            woven.bitcast(I32).rearrange("p (c i u) -> p c u i", i=4, u=2),
-            pairs[:, :, HALF:N].bitcast(I32).rearrange("p u (c i) -> p c u i", i=4),
-        )
-        quantize(("v", 0), woven.bitcast(BF16), E4M3, HALF)
-        xT1_grouped = keep.tile([P, HALF, PACK], BF16, name="xT1_grouped", align_bytes=64)
-        interleave(xT1_grouped[:, 0:HALF, :], xT1a[:])
-        quantize(("xT", 1), flat(xT1_grouped[:, 0:HALF, :]), E4M3, 0)
-        xm0_parts = {}
-
-        def group_xm0(k):
-            xm0_parts[k] = shared.tile([P, P, PACK], BF16, name="xm0_%d" % k, align_bytes=64, offset=1024 * k)
-            interleave(xm0_parts[k][:], xm0[:, :, k * P : (k + 1) * P])
-
-        def quantize_xm0(k):
-            quantize(("xm", 0), flat(xm0_parts[k][:]), E4M3, k * P)
-
-        for c in range(2):
-            th = ring_th()
-            halves = [product(("v", 0), c, ("xT", 0), "bank%d" % (2 * c + h), h * HALF, (h + 1) * HALF) for h in range(2)]
-            for h in range(2):
-                squash("v", th, halves[h], 2 * h, 2 * h + 2)
-                turn("v", 0, c, th, 2 * h, 2 * h + 2)
-
-        def weigh(g, c):
+        def weigh_chunk(g, c):
             nc.vector.tensor_tensor(
                 g.rearrange("p (c i) t -> p c t i", i=2),
                 diffs[0, c][:].rearrange("p t (c i) -> p c t i", i=2),
@@ -279,131 +172,183 @@ def tile_attend_gds_nce_kernel(tc, xT, wT, vT, wt, xm, offs, out):
                 MULT,
             )
 
-        g0a = shared.tile([P, HALF, PACK], BF16, name="g0a", align_bytes=64, offset=8192)
-        for k in range(2):
-            group_xm0(k)
-        xT1b_grouped = keep.tile([P, HALF, PACK], BF16, name="xT1b_grouped", align_bytes=64)
-        interleave(xT1b_grouped[:], xT1b[:])
-        weigh(g0a[:, 0:128, :], 0)
-        weigh(g0a[:, 128:256, :], 1)
-        quantize_xm0(0)
-        quantize(("g", 0), flat(g0a[:]), E5M2, 0)
-        codes["g_first", 0] = (padded_words[:, 0:N], padded_scales[:, 0:N], E5M2)
-        first_bank = product(("xm", 0), 0, ("g_first", 0), "bank0")
-        squashed = {}
-        for c in (2, 3):
-            squashed[c] = ring_th()
-            squash("v", squashed[c], product(("v", 0), c, ("xT", 0), "diff%d" % (c - 2)))
-        leave(0, 0, first_bank, 0, HALF, shift=HALF)
-        scatter(0, 0, 0)
-        for c in (2, 3):
-            turn("v", 0, c, squashed[c])
-        picked_v1 = shared.tile([P, N, 2], U32, name="picked_v1", align_bytes=64, offset=1536)
-        nc.vector.tensor_copy(
-            picked_v1[:].bitcast(I32).rearrange("p (h c i) u -> p h c u i", h=2, i=4),
-            teacher[:, 2 * HALF : 2 * HALF + 14 * HALF].bitcast(I32).rearrange("p (u h c i) -> p h c u i", u=2, h=7, i=4)[:, 0:2],
-        )
-        quantize_xm0(1)
-        quantize(("xT", 1), flat(xT1b_grouped[:]), E4M3, HALF)
-        quantize(("v", 1), flat(picked_v1[:]).bitcast(BF16), E4M3, 0)
-        second_bank = product(("xm", 0), 1, ("g_first", 0), "bank1")
-        xm0_rest = shared.tile([P, HALF, PACK], BF16, name="xm0_rest", align_bytes=64, offset=9728)
-        interleave(xm0_rest[:], xm0b[:])
-        quantize(("xm", 0), flat(xm0_rest[:]), E4M3, HALF)
-        dw = staged.tile([P, HALF], F32, name="dw_after_xm0", offset=8192)
-        nc.scalar.activation(dw[:], second_bank[:, HALF:N], COPY, scale=0.5)
-        dws[0, 1] = [(0, HALF, dw)]
-        scatter(0, 1, 0)
-        early_banks = [product(("xm", 0), 2, ("g_first", 0), "bank2")]
-
-        g0b = shared.tile([P, HALF, PACK], BF16, name="g0b", align_bytes=64, offset=11264)
-
-        def scaled_planes(b, h, offset):
+        def weigh_half(b, h, offset):
             planes = shared.tile([P, PACK, HALF], BF16, name="planes%d%d" % (b, h), align_bytes=64, offset=offset)
             for t in range(PACK):
-                src = diffs[b, 2 * h + t // 2][:, 2 * (t % 2) : 2 * (t % 2) + 2, :].rearrange("p c i -> p (c i)")
+                src = flat(diffs[b, 2 * h + t // 2][:, 2 * (t % 2) : 2 * (t % 2) + 2, :])
                 nc.scalar.activation(planes[:, t, :], src, COPY, scale=weights[:, b, t : t + 1])
             return planes
 
-        interleave_on_gpsimd(g0b[:], scaled_planes(0, 1, 13312)[:])
-        leave(0, 2, early_banks[0], 0, HALF, shift=HALF)
-        scatter(0, 2, 0)
-        quantize(("g", 0), flat(g0b[:]), E5M2, HALF)
-        xm1_halves = {}
+        def put(b, k, bank, col0, slot0, count, pool=ring, **place):
+            dw = pool.tile([P, count], F32, name="dw", **place)
+            nc.scalar.activation(dw[:], bank[:, col0 : col0 + count], COPY, scale=0.5)
+            nc.vector.tensor_copy(placed[k][:].indirect(entries(b * N + slot0, count)), dw[:])
+
+        def put_first(b, k, bank, pool=ring, **place):
+            put(b, k, bank, HALF, 0, HALF, pool, **place)
+
+        def put_second(b, k, bank, pool=ring, **place):
+            put(b, k, bank, HALF, HALF, HALF, pool, **place)
+
+        def store(k):
+            nc.sync.dma_start(out=out[k * P : (k + 1) * P, :], in_=placed[k][:])
+
+        bring(*STUDENT_PIECES[0])
+        nc.sync.dma_start(offsets[:], offs)
+        student = keep.tile([P, 2, B * N], U32, name="student", align_bytes=64)
+        gather(student[:, 0, :], "w", 0, 0, B * N)
+        bring(*STUDENT_PIECES[1])
+        for b in range(B):
+            gather(student[:, 1, b * N : (b + 1) * N], "w", 1, b * N, N)
+        woven_w = []
+        for b in range(B):
+            woven_w.append(keep.tile([P, 2 * N], U32, name="woven_w%d" % b, align_bytes=64))
+            weave(woven_w[b][:], student[:, :, b * N : (b + 1) * N], False)
+        quantize("w0", woven_w[0][:].bitcast(BF16), 0)
+        xT0 = load(raw, "stage", xT[0], 0, R, tag="stage")
+        xT0_grouped = keep.tile([P, R, PACK], BF16, name="xT0_grouped", align_bytes=64)
+        nc.scalar.copy(
+            xT0_grouped[:].rearrange("p (t m) j -> p m j t", t=PACK), xT0[:].rearrange("p j (m t) -> p m j t", t=PACK)
+        )
+        quantize("xT0", flat(xT0_grouped[:]), 0)
+        quantize("w1", woven_w[1][:].bitcast(BF16), 0)
+
+        def student_scores(c, th):
+            squash("w", 0, th, product("w0", c, "xT0", "bank%d" % c))
+            turn("w", 0, c, th)
+
+        for piece in TEACHER_PIECES[0]:
+            bring(*piece)
+        for c, th in enumerate(staged_th("early", 3, 8 * KB)):
+            student_scores(c, th)
+        teacher = keep.tile([P, 16 * HALF], U32, name="teacher", align_bytes=64)
+        gather(teacher[:, 0 : B * N], "v", 0, 0, B * N)
+        for piece in TEACHER_PIECES[1]:
+            bring(*piece)
+        student_scores(3, staged_th("held", 1, 28 * KB)[0])
+
+        xT1a = load(staged, "xT1a", xT[1], 0, HALF, offset=0)
+        nc.sync.dma_start(out=weights[:], in_=wt.rearrange("b (p t) o -> p b (t o)", t=PACK))
+        xm0a = load(raw, "stage", xm[0], 0, HALF, tag="stage")
+        xT1b = load(staged, "xT1b", xT[1], HALF, R, offset=4 * KB)
+        xm0b = load(staged, "xm0b", xm[0], HALF, D, offset=8 * KB)
+        xm1 = load(staged, "xm1", xm[1], 0, D, offset=16 * KB)
+
+        pairs = teacher[:, 0 : 8 * HALF].rearrange("p (u n) -> p u n", u=2)
+        for h in range(2):
+            gather(pairs[:, 1, h * HALF : (h + 1) * HALF], "v", 1, h * HALF, HALF)
+        for c in range(2):
+            woven = teacher[:, (8 + c) * HALF + P : (9 + c) * HALF + P]
+            weave(woven, pairs[:, :, c * P : (c + 1) * P], True)
+            quantize("v0", woven.bitcast(BF16), c * P)
+        for h in range(2):
+            gather(teacher[:, (9 + h) * HALF : (10 + h) * HALF], "v", 1, N + h * HALF, HALF)
+        woven = teacher[:, 7 * HALF : 9 * HALF]
+        weave(woven, pairs[:, :, HALF:N], False)
+        quantize("v0", woven.bitcast(BF16), HALF)
+        xT1a_grouped = keep.tile([P, HALF, PACK], BF16, name="xT1a_grouped", align_bytes=64)
+        interleave(xT1a_grouped[:], xT1a[:])
+        quantize("xT1", flat(xT1a_grouped[:]), 0)
+        for c in range(2):
+            th = ring_th()
+            halves = [product("v0", c, "xT0", "bank%d" % (2 * c + h), h * HALF, (h + 1) * HALF) for h in range(2)]
+            for h in range(2):
+                squash("v", 0, th, halves[h], 2 * h, 2 * h + 2)
+                turn("v", 0, c, th, 2 * h, 2 * h + 2)
+        g0a = shared.tile([P, HALF, PACK], BF16, name="g0a", align_bytes=64, offset=8 * KB)
+        xm0a_grouped = shared.tile([P, HALF, PACK], BF16, name="xm0a_grouped", align_bytes=64, offset=0)
+        interleave(xm0a_grouped[:], xm0a[:])
+        xT1b_grouped = keep.tile([P, HALF, PACK], BF16, name="xT1b_grouped", align_bytes=64)
+        interleave(xT1b_grouped[:], xT1b[:])
+        for c in range(2):
+            weigh_chunk(g0a[:, c * P : (c + 1) * P, :], c)
+        quantize("xm0", flat(xm0a_grouped[:]), 0)
+        quantize("g", flat(g0a[:]), 0)
+        bank = product("xm0", 0, "g_first", "bank0")
+        late_th = {}
+        for c, bank_name in ((2, "bank3"), (3, "diff0")):
+            late_th[c] = ring_th()
+            squash("v", 0, late_th[c], product("v0", c, "xT0", bank_name))
+        put_first(0, 0, bank, tag="dw")
+        for c in (2, 3):
+            turn("v", 0, c, late_th[c])
+
+        woven_v1 = shared.tile([P, 2 * N], U32, name="woven_v1", align_bytes=64, offset=3 * KB // 2)
+        weave(woven_v1[:], teacher[:, 2 * HALF :].rearrange("p (u n) -> p u n", u=2)[:, :, 0:N], False)
+        quantize("xT1", flat(xT1b_grouped[:]), HALF)
+        quantize("v1", woven_v1[:].bitcast(BF16), 0)
+
+        bank = product("xm0", 1, "g_first", "bank1")
+        xm0b_grouped = shared.tile([P, HALF, PACK], BF16, name="xm0b_grouped", align_bytes=64, offset=19 * KB // 2)
+        interleave(xm0b_grouped[:], xm0b[:])
+        quantize("xm0", flat(xm0b_grouped[:]), HALF)
+        put_first(0, 1, bank, staged, offset=8 * KB)
+        bank = product("xm0", 2, "g_first", "bank2")
+        g0b = shared.tile([P, HALF, PACK], BF16, name="g0b", align_bytes=64, offset=11 * KB)
+        interleave_on_gpsimd(g0b[:], weigh_half(0, 1, 13 * KB)[:])
+        put_first(0, 2, bank, tag="dw")
+        quantize("g", flat(g0b[:]), HALF)
+
+        xm1_words = keep.tile([P, D], U32, name="xm1_words", align_bytes=64)
+        xm1_grouped = {}
 
         def group_xm1(h, offset):
-            xm1_halves[h] = shared.tile([P, HALF, PACK], BF16, name="xm1_grouped%d" % h, align_bytes=64, offset=offset)
+            xm1_grouped[h] = shared.tile([P, HALF, PACK], BF16, name="xm1_grouped%d" % h, align_bytes=64, offset=offset)
             for c in (0, P):
-                interleave_on_gpsimd(xm1_halves[h][:, c : c + P, :], xm1[:, :, h * HALF + c : h * HALF + c + P])
-
-        group_xm1(0, 10240)
-        g1a = shared.tile([P, HALF, PACK], BF16, name="g1a", align_bytes=64, offset=0)
-        g1b = keep.tile([P, HALF, PACK], BF16, name="g1b", align_bytes=64)
-        codes["g", 1] = codes["g", 0]
-
-        def heads(steps, tags, squashed):
-            banks = [product((name, 1), c, ("xT", 1), tag) for (name, c), tag in zip(steps, tags)]
-            for (name, c), bank, th in zip(steps, banks, squashed):
-                squash_rows(name, th, bank)
-                turn(name, 1, c, th)
-
-        def squash_tile(name, count, offset):
-            tile = staged.tile([P, count, PACK, P], F32, name=name, offset=offset)
-            return [tile[:, j] for j in range(count)]
-
-        first_steps = (("w", 0), ("w", 1), ("v", 0), ("v", 1))
-        score_banks = [product((name, 1), c, ("xT", 1), tag) for (name, c), tag in zip(first_steps, ("bank0", "bank1", "diff2", "diff3"))]
-        squashed = squash_tile("th_w01", 2, 24576) + squash_tile("th_v0", 1, 28672) + squash_tile("th_v1", 1, 30720)
-        for (name, c), bank, th in zip(first_steps, score_banks, squashed):
-            squash_rows(name, th, bank)
-            if (name, c) == ("w", 0):
-                leave(0, 3, product(("xm", 0), 3, ("g_first", 0), "bank0"), 0, HALF, shift=HALF)
-                scatter(0, 3, 0)
-            if (name, c) == ("w", 1):
-                student_banks = [product(("w", 1), c, ("xT", 1), tag) for c, tag in ((2, "bank3"), (3, "bank1"))]
-            if (name, c) == ("v", 1):
-                gradient(0, 0, "diff2", ((HALF, N, None),))
-                scatter(0, 0, 1)
-            turn(name, 1, c, th)
-        gradient(0, 1, "diff3", ((HALF, N, None),))
-        scatter(0, 1, 1)
-        planes = scaled_planes(1, 0, 16384)
-        interleave(g1a[:], planes[:])
-        late_banks = [product(("xm", 0), k, ("g", 0), tag) for k, tag in ((2, "diff2"), (3, "diff3"))]
-        xm1_words = keep.tile([P, N], U32, name="xm1_words", align_bytes=64)
+                interleave_on_gpsimd(xm1_grouped[h][:, c : c + P, :], xm1[:, :, h * HALF + c : h * HALF + c + P])
 
         def quantize_xm1(h, offset):
             scales = shared.tile([P, HALF], U8, name="xm1_scales%d" % h, align_bytes=64, offset=offset)
-            codes["xm1", h] = (xm1_words[:, h * HALF : (h + 1) * HALF], scales, E4M3)
-            quantize(("xm1", h), flat(xm1_halves[h][:]), E4M3, 0)
+            codes["xm1_%d" % h] = (xm1_words[:, h * HALF : (h + 1) * HALF], scales, E4M3)
+            quantize("xm1_%d" % h, flat(xm1_grouped[h][:]), 0)
 
-        quantize_xm1(0, 17664)
-        quantize(("g", 1), flat(g1a[:]), E5M2, 0)
+        group_xm1(0, 10 * KB)
+
+        steps = (("w", 0, "bank0"), ("w", 1, "bank1"), ("v", 0, "diff2"), ("v", 1, "diff3"))
+        scores = [product(name + "1", c, "xT1", bank_name) for name, c, bank_name in steps]
+        ths = staged_th("th_w01", 2, 24 * KB) + staged_th("th_v0", 1, 28 * KB) + staged_th("th_v1", 1, 30 * KB)
+        squash("w", 1, ths[0], scores[0])
+        put_first(0, 3, product("xm0", 3, "g_first", "bank0"), tag="dw")
+        turn("w", 1, 0, ths[0])
+        squash("w", 1, ths[1], scores[1])
+        late_scores = [product("w1", c, "xT1", bank_name) for c, bank_name in ((2, "bank3"), (3, "bank1"))]
+        turn("w", 1, 1, ths[1])
+        squash("v", 1, ths[2], scores[2])
+        turn("v", 1, 0, ths[2])
+        squash("v", 1, ths[3], scores[3])
+        put_second(0, 0, product("xm0", 0, "g", "diff2"), tag="dw")
+        turn("v", 1, 1, ths[3])
+        put_second(0, 1, product("xm0", 1, "g", "diff3"), tag="dw")
+        planes = weigh_half(1, 0, 16 * KB)
+        g1a = shared.tile([P, HALF, PACK], BF16, name="g1a", align_bytes=64, offset=0)
+        interleave(g1a[:], planes[:])
+        banks = [product("xm0", k, "g", "diff%d" % k) for k in (2, 3)]
+        quantize_xm1(0, 17 * KB + KB // 4)
+        quantize("g", flat(g1a[:]), 0)
         group_xm1(1, 0)
         for k in (2, 3):
-            leave(0, k, late_banks[k - 2], HALF, N, 15616 + 1024 * (k - 2))
-            scatter(0, k, 1)
-        for c, bank, th in zip((2, 3), student_banks, squash_tile("th_w2", 1, 12288) + squash_tile("th_w3", 1, 30720)):
-            squash_rows("w", th, bank)
+            put_second(0, k, banks[k - 2], shared, align_bytes=64, offset=(13 + k) * KB + KB // 4)
+
+        for c, bank, th in zip((2, 3), late_scores, staged_th("th_w2", 1, 12 * KB) + staged_th("th_w3", 1, 30 * KB)):
+            squash("w", 1, th, bank)
             turn("w", 1, c, th)
-        heads((("v", 2), ("v", 3)), ("diff0", "diff1"), squash_tile("th_v23", 2, 24576))
-        planes = scaled_planes(1, 1, 18432)
-        leave(1, 0, product(("xm1", 0), 0, ("g_first", 0), "diff1"), 0, HALF, shift=HALF)
-        scatter(1, 0, 0)
-        second_bank = product(("xm1", 0), 1, ("g_first", 0), "bank2")
+        scores = [product("v1", c, "xT1", "diff%d" % (c - 2)) for c in (2, 3)]
+        for c, bank, th in zip((2, 3), scores, staged_th("th_v23", 2, 24 * KB)):
+            squash("v", 1, th, bank)
+            turn("v", 1, c, th)
+        planes = weigh_half(1, 1, 18 * KB)
+        put_first(1, 0, product("xm1_0", 0, "g_first", "diff1"), tag="dw")
+        bank = product("xm1_0", 1, "g_first", "bank2")
+        g1b = keep.tile([P, HALF, PACK], BF16, name="g1b", align_bytes=64)
         interleave(g1b[:], planes[:])
-        quantize(("g", 1), flat(g1b[:]), E5M2, HALF)
-        quantize_xm1(1, 19968)
-        leave(1, 1, second_bank, 0, HALF, 18944, shift=HALF)
-        scatter(1, 1, 0)
+        quantize("g", flat(g1b[:]), HALF)
+        quantize_xm1(1, 19 * KB + KB // 2)
+        put_first(1, 1, bank, shared, align_bytes=64, offset=18 * KB + KB // 2)
         for k in range(2):
-            gradient(1, k, "diff%d" % (k + 2), ((HALF, N, None),))
-            scatter(1, k, 1)
-            nc.sync.dma_start(out=out[k * P : (k + 1) * P, :], in_=placed[k][:])
-        gradient(1, 2, "bank0", ((0, N, None),))
-        scatter(1, 2, 0)
-        nc.sync.dma_start(out=out[2 * P : 3 * P, :], in_=placed[2][:])
-        gradient(1, 3, "bank1", ((0, N, None),))
-        scatter(1, 3, 0)
+            put_second(1, k, product("xm1_0", k, "g", "diff%d" % (k + 2)), tag="dw")
+            store(k)
+        put(1, 2, product("xm1_1", 0, "g", "bank0"), 0, 0, N, tag="dw")
+        store(2)
+        put(1, 3, product("xm1_1", 1, "g", "bank1"), 0, 0, N, tag="dw")
         nc.sync.dma_start(out=out[3 * P :, 0 : T // 2], in_=placed[3][:, 0 : T // 2])
         nc.scalar.dma_start(out=out[3 * P :, T // 2 :], in_=placed[3][:, T // 2 :])

@@ -9,7 +9,6 @@ FLOPS = 3 * 2 * B * N * D * R
 F32 = mybir.dt.float32
 BF16 = mybir.dt.bfloat16
 U32 = mybir.dt.uint32
-I32 = mybir.dt.int32
 U16 = mybir.dt.uint16
 U8 = mybir.dt.uint8
 E4M3 = mybir.dt.float8_e4m3fn_x4
@@ -25,21 +24,15 @@ PER_COL = 16
 HALF = N // 2
 RUN = 4
 KB = 1024
-
-STUDENT_PIECES = (("w", 0, 0, T, 768, 0), ("w", 1, 0, T, 704, 16 * KB))
-TEACHER_PIECES = (
-    (("v", 0, 0, 1024, 1024, 0), ("v", 0, 1024, T, 512, 8 * KB)),
-    (("v", 1, 0, 1024, 640, 16 * KB), ("v", 1, 1024, 1792, 128, 24 * KB), ("v", 1, 1792, T, 96, 30 * KB)),
-)
+SHARE_3 = 352
 
 
 def tile_attend_gds_nce_kernel(tc, xT, wT, vT, wt, xm, offs, out):
     nc = tc.nc
     with ExitStack() as ctx:
         keep = ctx.enter_context(tc.tile_pool(name="keep", bufs=1))
-        raw = ctx.enter_context(tc.tile_pool(name="raw", bufs=2))
-        staged = ctx.enter_context(tc.tile_pool(name="staged", bufs=1))
         shared = ctx.enter_context(tc.tile_pool(name="shared", bufs=1))
+        reused = ctx.enter_context(tc.tile_pool(name="reused", bufs=1))
         ring = ctx.enter_context(tc.tile_pool(name="ring", bufs=4))
         psum = ctx.enter_context(tc.psum_pool(name="psum", bufs=1))
 
@@ -50,24 +43,10 @@ def tile_attend_gds_nce_kernel(tc, xT, wT, vT, wt, xm, offs, out):
 
         make_identity(nc, ident[:])
         for k, tile in enumerate(placed):
-            (nc.vector if k < len(placed) - 1 else nc.gpsimd).memset(tile[:], 0.0)
+            (nc.vector if k < 2 else nc.gpsimd).memset(tile[:], 0.0)
 
         def entries(first, count):
             return offsets[:, first // PER_COL : (first + count) // PER_COL]
-
-        codes = {}
-        padded_words = keep.tile([P, HALF + N], U32, name="padded_words", align_bytes=64)
-        padded_scales = keep.tile([P, HALF + N], U8, name="padded_scales", align_bytes=64)
-        nc.gpsimd.memset(padded_words[:, 0:HALF], 0)
-        nc.gpsimd.memset(padded_scales[:, 0:HALF], 0)
-        codes["g"] = (padded_words[:, HALF:], padded_scales[:, HALF:], E5M2)
-        codes["g_first"] = (padded_words[:, 0:N], padded_scales[:, 0:N], E5M2)
-
-        tables = {"w": wT, "v": vT}
-        windows = {}
-        for name in tables:
-            for u in range(2):
-                windows[name, u] = keep.tile([P, T, 2], BF16, name="win_%s%d" % (name, u), align_bytes=64)
 
         def by_rows(src):
             return src.rearrange("(p t) c -> p t c", t=PACK)
@@ -75,57 +54,62 @@ def tile_attend_gds_nce_kernel(tc, xT, wT, vT, wt, xm, offs, out):
         def flat(view):
             return view.rearrange("p a b -> p (a b)")
 
-        def bring(name, u, c0, c1, on_scalar, offset):
-            stage = staged.tile([P, 2, c1 - c0], F32, name="stage_%s%d_%d" % (name, u, c0), offset=offset)
-            nc.sync.dma_start(out=stage[:], in_=by_rows(tables[name])[:, 2 * u : 2 * u + 2, c0:c1])
-            src = stage[:].rearrange("p e (c i) -> p c e i", i=RUN)
-            dst = windows[name, u][:, c0:c1, :].rearrange("p (c i) e -> p c e i", i=RUN)
-            split = on_scalar // RUN
-            nc.scalar.activation(dst[:, 0:split], src[:, 0:split], COPY)
-            if on_scalar < c1 - c0:
-                nc.vector.tensor_copy(dst[:, split:], src[:, split:])
+        tables = {"w": wT, "v": vT}
+        planes = {}
 
-        def load(pool, name, src, c0, c1, **place):
-            stage = pool.tile([P, PACK, c1 - c0], F32, name=name, **place)
+        def bring(name, t):
+            if name == "w":
+                planes[name, t] = reused.tile([P, T], F32, name="plane_w%d" % t, offset=8 * KB * t)
+            else:
+                planes[name, t] = keep.tile([P, T], F32, name="plane_v%d" % t)
+            nc.sync.dma_start(out=planes[name, t][:], in_=by_rows(tables[name])[:, t, :])
+
+        def load(name, src, c0, c1):
+            stage = keep.tile([P, PACK, c1 - c0], F32, name=name)
             nc.sync.dma_start(out=stage[:], in_=by_rows(src)[:, :, c0:c1])
             return stage
 
-        def gather(dst, name, u, first, count):
-            words = windows[name, u][:].rearrange("p c e -> p (c e)").bitcast(U32)
-            nc.vector.tensor_copy(dst, words.indirect(entries(first, count)))
+        def gather_into_words(dst, name, t, first, count):
+            nc.vector.tensor_copy(dst[:, :, t], planes[name, t][:].indirect(entries(first, count)))
 
-        def weave(dst, pairs, on_scalar):
-            if on_scalar:
-                move, dtype = nc.scalar.copy, U32
-            else:
-                move, dtype = nc.vector.tensor_copy, I32
-            move(
-                dst.bitcast(dtype).rearrange("p (c i u) -> p c u i", i=RUN, u=2),
-                pairs.bitcast(dtype).rearrange("p u (c i) -> p c u i", i=RUN),
-            )
+        def gather_plane(dst, name, t, first, count):
+            nc.scalar.activation(dst[:, t, :], planes[name, t][:].indirect(entries(first, count)), COPY)
 
-        def quantize(key, values, c0):
-            if key not in codes:
-                words = keep.tile([P, N], U32, name="words_" + key, align_bytes=64)
-                scales = keep.tile([P, N], U8, name="scales_" + key, align_bytes=64)
-                codes[key] = (words, scales, E4M3)
-            words, scales, fmt = codes[key]
-            c1 = c0 + values.shape[1] // PACK
-            nc.vector.quantize_mx(out=words[:, c0:c1].bitcast(fmt), scales=scales[:, c0:c1], in_=values)
-
-        def interleave(dst, src):
-            nc.scalar.copy(dst.rearrange("p (c i) t -> p c t i", i=RUN), src.rearrange("p t (c i) -> p c t i", i=RUN))
+        def interleave(move, dst, src):
+            move(dst.rearrange("p (c i) t -> p c t i", i=RUN), src.rearrange("p t (c i) -> p c t i", i=RUN))
 
         def interleave_on_gpsimd(dst, src):
             nc.gpsimd.tensor_scalar(dst, src.rearrange("p t c -> p c t"), 1.0, 0.0, MULT, ADD)
 
-        def product(stationary, block, moving, bank_name, n0=0, n1=N):
-            bank = psum.tile([P, N], F32, name=bank_name, tag=bank_name)
+        def deal(move, dst, src):
+            move(dst.rearrange("p (t m) j -> p m j t", t=PACK), src.rearrange("p j (m t) -> p m j t", t=PACK))
+
+        codes = {}
+
+        def quantize(key, values, c0, fmt=E4M3, scales_at=None):
+            if key not in codes:
+                words = keep.tile([P, N], U32, name="words_" + key, align_bytes=64)
+                if scales_at is None:
+                    scales = keep.tile([P, N], U8, name="scales_" + key, align_bytes=64)
+                else:
+                    scales = shared.tile([P, N], U8, name="scales_" + key, align_bytes=64, offset=scales_at)
+                codes[key] = (words, scales, fmt)
+            words, scales, fmt = codes[key]
+            c1 = c0 + values.shape[1] // PACK
+            nc.vector.quantize_mx(out=words[:, c0:c1].bitcast(fmt), scales=scales[:, c0:c1], in_=values)
+
+        def new_bank(bank_name):
+            return psum.tile([P, N], F32, name=bank_name, tag=bank_name)
+
+        def product(stationary, block, moving, bank, n0=0, n1=N, at=None):
+            if isinstance(bank, str):
+                bank = new_bank(bank)
+            at = n0 if at is None else at
             s_words, s_scales, s_fmt = codes[stationary]
             m_words, m_scales, m_fmt = codes[moving]
             cols = slice(block * P, (block + 1) * P)
             nc.tensor.matmul_mx(
-                out=bank[:, n0:n1],
+                out=bank[:, at : at + n1 - n0],
                 lhsT=s_words[:, cols].bitcast(s_fmt),
                 lhsT_scale=s_scales[:, cols],
                 rhs=m_words[:, n0:n1].bitcast(m_fmt),
@@ -135,220 +119,218 @@ def tile_attend_gds_nce_kernel(tc, xT, wT, vT, wt, xm, offs, out):
             )
             return bank
 
-        def squash(name, b, th, bank, t0=0, t1=PACK):
-            rows = bank[:].rearrange("p (t m) -> p t m" if b == 0 else "p (m t) -> p t m", t=PACK)
+        def squash(name, th, bank, t0=0, t1=PACK):
+            rows = bank[:].rearrange("p (t m) -> p t m", t=PACK)
             nc.scalar.activation(th[:, t0:t1, :], rows[:, t0:t1, :], TANH, scale=0.5 if name == "w" else -0.5)
 
         diffs = {}
 
         def turn(name, b, c, th, t0=0, t1=PACK):
+            if (b, c) not in diffs:
+                diffs[b, c] = psum.tile([P, PACK, P], F32, name="diff%d" % c, tag="diff%d" % c)
             for t in range(t0, t1):
-                if b == 0 and c < 2:
-                    q, place = c, t
-                    opens, closes = t == 0, t == PACK - 1
-                else:
-                    q, place = 2 * (c // 2) + t // 2, 2 * (t % 2) + c % 2
-                    opens, closes = c % 2 == 0 and t % 2 == 0, c % 2 == 1 and t % 2 == 1
-                if (b, q) not in diffs:
-                    bank_name = "bank%d" % q if b == 1 and q >= 2 else "diff%d" % q
-                    diffs[b, q] = psum.tile([P, PACK, P], F32, name=bank_name, tag=bank_name)
                 nc.tensor.matmul(
-                    diffs[b, q][:, place, :], th[:, t, :], ident[:], is_transpose=True,
-                    start=name == "w" and opens, stop=name == "v" and closes,
+                    diffs[b, c][:, t, :], th[:, t, :], ident[:], is_transpose=True,
+                    start=name == "w" and t == 0, stop=name == "v" and t == PACK - 1,
                 )
 
         def ring_th():
             return ring.tile([P, PACK, P], F32, name="th", tag="th")[:]
 
-        def staged_th(name, count, offset):
-            tile = staged.tile([P, count, PACK, P], F32, name=name, offset=offset)
-            return [tile[:, j] for j in range(count)]
-
-        def weigh_chunk(g, c):
+        def weigh(g, b, c):
             nc.vector.tensor_tensor(
-                g.rearrange("p (c i) t -> p c t i", i=2),
-                diffs[0, c][:].rearrange("p t (c i) -> p c t i", i=2),
-                weights[:, 0:1, :].rearrange("p o (t z) -> p o t z", z=1).to_broadcast([P, P // 2, PACK, 2]),
+                g[:, (c % 2) * P : (c % 2 + 1) * P, :].rearrange("p (c i) t -> p c t i", i=2),
+                diffs[b, c][:].rearrange("p t (c i) -> p c t i", i=2),
+                weights[:, b : b + 1, :].rearrange("p o (t z) -> p o t z", z=1).to_broadcast([P, P // 2, PACK, 2]),
                 MULT,
             )
 
-        def weigh_half(b, h, offset):
-            planes = shared.tile([P, PACK, HALF], BF16, name="planes%d%d" % (b, h), align_bytes=64, offset=offset)
-            for t in range(PACK):
-                src = flat(diffs[b, 2 * h + t // 2][:, 2 * (t % 2) : 2 * (t % 2) + 2, :])
-                nc.scalar.activation(planes[:, t, :], src, COPY, scale=weights[:, b, t : t + 1])
-            return planes
+        def held(name, shape, dtype, offset):
+            return shared.tile(shape, dtype, name=name, align_bytes=64, offset=offset)
 
-        def put(b, k, bank, col0, slot0, count, pool=ring, **place):
-            dw = pool.tile([P, count], F32, name="dw", **place)
-            nc.scalar.activation(dw[:], bank[:, col0 : col0 + count], COPY, scale=0.5)
-            nc.vector.tensor_copy(placed[k][:].indirect(entries(b * N + slot0, count)), dw[:])
+        def fetch(on_scalar, bank, n0, n1, dw):
+            if on_scalar:
+                nc.scalar.activation(dw[:], bank[:, n0:n1], COPY, scale=0.5)
+            else:
+                nc.vector.tensor_scalar(dw[:], bank[:, n0:n1], 0.5, None, MULT)
+            return dw
 
-        def put_first(b, k, bank, pool=ring, **place):
-            put(b, k, bank, HALF, 0, HALF, pool, **place)
-
-        def put_second(b, k, bank, pool=ring, **place):
-            put(b, k, bank, HALF, HALF, HALF, pool, **place)
+        def scatter(on_scalar, b, k, slot0, values):
+            window = placed[k][:].indirect(entries(b * N + slot0, values.shape[1]))
+            if on_scalar:
+                nc.scalar.activation(window, values, COPY)
+            else:
+                nc.vector.tensor_copy(window, values)
 
         def store(k):
             nc.sync.dma_start(out=out[k * P : (k + 1) * P, :], in_=placed[k][:])
 
-        bring(*STUDENT_PIECES[0])
+        bring("w", 0)
         nc.sync.dma_start(offsets[:], offs)
-        student = keep.tile([P, 2, B * N], U32, name="student", align_bytes=64)
-        gather(student[:, 0, :], "w", 0, 0, B * N)
-        bring(*STUDENT_PIECES[1])
-        for b in range(B):
-            gather(student[:, 1, b * N : (b + 1) * N], "w", 1, b * N, N)
-        woven_w = []
-        for b in range(B):
-            woven_w.append(keep.tile([P, 2 * N], U32, name="woven_w%d" % b, align_bytes=64))
-            weave(woven_w[b][:], student[:, :, b * N : (b + 1) * N], False)
-        quantize("w0", woven_w[0][:].bitcast(BF16), 0)
-        xT0 = load(raw, "stage", xT[0], 0, R, tag="stage")
-        xT0_grouped = keep.tile([P, R, PACK], BF16, name="xT0_grouped", align_bytes=64)
-        nc.scalar.copy(
-            xT0_grouped[:].rearrange("p (t m) j -> p m j t", t=PACK), xT0[:].rearrange("p j (m t) -> p m j t", t=PACK)
-        )
-        quantize("xT0", flat(xT0_grouped[:]), 0)
-        quantize("w1", woven_w[1][:].bitcast(BF16), 0)
+        for t in range(1, PACK):
+            bring("w", t)
+        xT_raw = [load("xT%d" % b, xT[b], 0, R) for b in range(B)]
+        for t in range(PACK):
+            bring("v", t)
+        xm_raw = {}
+        xm_raw[0, 0] = load("xm00", xm[0], 0, HALF)
+        nc.sync.dma_start(out=weights[:], in_=wt.rearrange("b (p t) o -> p b (t o)", t=PACK))
+        xm_raw[0, 1] = load("xm01", xm[0], HALF, D)
+        xm_raw[1, 0] = load("xm10", xm[1], 0, HALF)
+        xm_raw[1, 1] = load("xm11", xm[1], HALF, D)
 
-        def student_scores(c, th):
-            squash("w", 0, th, product("w0", c, "xT0", "bank%d" % c))
+        w0 = keep.tile([P, N, PACK], BF16, name="w0", align_bytes=64)
+        w1 = keep.tile([P, N, PACK], BF16, name="w1", align_bytes=64)
+        w1_planes = keep.tile([P, PACK, N], BF16, name="w1_planes", align_bytes=64)
+        for t in range(PACK):
+            gather_into_words(w0[:], "w", t, 0, N)
+            gather_plane(w1_planes[:], "w", t, N, N)
+        quantize("w0", flat(w0[:]), 0)
+        interleave(nc.scalar.copy, w1[:], w1_planes[:])
+        xT0_grouped = held("xT0_grouped", [P, R, PACK], BF16, 12 * KB)
+        xT1_grouped = keep.tile([P, R, PACK], BF16, name="xT1_grouped", align_bytes=64)
+        deal(nc.vector.tensor_copy, xT0_grouped[:], xT_raw[0][:])
+        quantize("xT0", flat(xT0_grouped[:]), 0)
+        deal(nc.vector.tensor_copy, xT1_grouped[:], xT_raw[1][:])
+        quantize("w1", flat(w1[:]), 0, scales_at=12 * KB)
+        quantize("xT1", flat(xT1_grouped[:]), 0)
+        for c in range(PACK):
+            th = ring_th()
+            squash("w", th, product("w0", c, "xT0", "bank%d" % c))
             turn("w", 0, c, th)
 
-        for piece in TEACHER_PIECES[0]:
-            bring(*piece)
-        for c, th in enumerate(staged_th("early", 3, 8 * KB)):
-            student_scores(c, th)
-        teacher = keep.tile([P, 16 * HALF], U32, name="teacher", align_bytes=64)
-        gather(teacher[:, 0 : B * N], "v", 0, 0, B * N)
-        for piece in TEACHER_PIECES[1]:
-            bring(*piece)
-        student_scores(3, staged_th("held", 1, 28 * KB)[0])
-
-        xT1a = load(staged, "xT1a", xT[1], 0, HALF, offset=0)
-        nc.sync.dma_start(out=weights[:], in_=wt.rearrange("b (p t) o -> p b (t o)", t=PACK))
-        xm0a = load(raw, "stage", xm[0], 0, HALF, tag="stage")
-        xT1b = load(staged, "xT1b", xT[1], HALF, R, offset=4 * KB)
-        xm0b = load(staged, "xm0b", xm[0], HALF, D, offset=8 * KB)
-        xm1 = load(staged, "xm1", xm[1], 0, D, offset=16 * KB)
-
-        pairs = teacher[:, 0 : 8 * HALF].rearrange("p (u n) -> p u n", u=2)
-        for h in range(2):
-            gather(pairs[:, 1, h * HALF : (h + 1) * HALF], "v", 1, h * HALF, HALF)
-        for c in range(2):
-            woven = teacher[:, (8 + c) * HALF + P : (9 + c) * HALF + P]
-            weave(woven, pairs[:, :, c * P : (c + 1) * P], True)
-            quantize("v0", woven.bitcast(BF16), c * P)
-        for h in range(2):
-            gather(teacher[:, (9 + h) * HALF : (10 + h) * HALF], "v", 1, N + h * HALF, HALF)
-        woven = teacher[:, 7 * HALF : 9 * HALF]
-        weave(woven, pairs[:, :, HALF:N], False)
-        quantize("v0", woven.bitcast(BF16), HALF)
-        xT1a_grouped = keep.tile([P, HALF, PACK], BF16, name="xT1a_grouped", align_bytes=64)
-        interleave(xT1a_grouped[:], xT1a[:])
-        quantize("xT1", flat(xT1a_grouped[:]), 0)
-        for c in range(2):
-            th = ring_th()
-            halves = [product("v0", c, "xT0", "bank%d" % (2 * c + h), h * HALF, (h + 1) * HALF) for h in range(2)]
+        v0 = [keep.tile([P, HALF, PACK], BF16, name="v0%d" % h, align_bytes=64) for h in range(2)]
+        v1 = [keep.tile([P, HALF, PACK], BF16, name="v1%d" % h, align_bytes=64) for h in range(2)]
+        v1_planes = keep.tile([P, PACK, N], BF16, name="v1_planes", align_bytes=64)
+        v0_last = keep.tile([P, HALF], BF16, name="v0_last", align_bytes=64)
+        th_w1 = reused.tile([P, PACK, PACK, P], F32, name="th_w1", offset=24 * KB)
+        last = PACK - 1
+        for t in range(last):
             for h in range(2):
-                squash("v", 0, th, halves[h], 2 * h, 2 * h + 2)
-                turn("v", 0, c, th, 2 * h, 2 * h + 2)
-        g0a = shared.tile([P, HALF, PACK], BF16, name="g0a", align_bytes=64, offset=8 * KB)
-        xm0a_grouped = shared.tile([P, HALF, PACK], BF16, name="xm0a_grouped", align_bytes=64, offset=0)
-        interleave(xm0a_grouped[:], xm0a[:])
-        xT1b_grouped = keep.tile([P, HALF, PACK], BF16, name="xT1b_grouped", align_bytes=64)
-        interleave(xT1b_grouped[:], xT1b[:])
+                gather_into_words(v0[h][:], "v", t, h * HALF, HALF)
+            if t == 1:
+                nc.vector.tensor_copy(v1_planes[:, t, 0:HALF], planes["v", t][:].indirect(entries(N, HALF)))
+                gather_plane(v1_planes[:, :, HALF:N], "v", t, N + HALF, HALF)
+            else:
+                gather_plane(v1_planes[:], "v", t, N, N)
+            for c in ((0, 1), (2, 3), ())[t]:
+                squash("w", th_w1[:, c], product("w1", c, "xT1", "bank%d" % c))
+        nc.scalar.activation(v0_last[:], planes["v", last][:].indirect(entries(HALF, HALF)), COPY)
+        for h in range(2):
+            gather_plane(v1_planes[:, :, h * HALF : (h + 1) * HALF], "v", last, N + h * HALF, HALF)
+        gather_into_words(v0[0][:], "v", last, 0, HALF)
+        quantize("v0", flat(v0[0][:]), 0)
+        nc.vector.tensor_copy(v0[1][:, :, last], v0_last[:])
+        quantize("v0", flat(v0[1][:]), HALF)
         for c in range(2):
-            weigh_chunk(g0a[:, c * P : (c + 1) * P, :], c)
-        quantize("xm0", flat(xm0a_grouped[:]), 0)
-        quantize("g", flat(g0a[:]), 0)
-        bank = product("xm0", 0, "g_first", "bank0")
-        late_th = {}
-        for c, bank_name in ((2, "bank3"), (3, "diff0")):
-            late_th[c] = ring_th()
-            squash("v", 0, late_th[c], product("v0", c, "xT0", bank_name))
-        put_first(0, 0, bank, tag="dw")
+            interleave(nc.vector.tensor_copy, v1[0][:, c * P : (c + 1) * P, :], v1_planes[:, :, c * P : (c + 1) * P])
+        xm0a = keep.tile([P, HALF, PACK], BF16, name="xm0a", align_bytes=64)
+        interleave(nc.vector.tensor_copy, xm0a[:], xm_raw[0, 0][:])
+        quantize("v1", flat(v1[0][:]), 0)
+        interleave(nc.vector.tensor_copy, v1[1][:], v1_planes[:, :, HALF:N])
+        quantize("xm0", flat(xm0a[:]), 0)
+        quantize("v1", flat(v1[1][:]), HALF)
+        xm0b = keep.tile([P, HALF, PACK], BF16, name="xm0b", align_bytes=64)
+        interleave(nc.vector.tensor_copy, xm0b[:], xm_raw[0, 1][:])
+
+        ths = [ring_th() for c in range(PACK)]
+        halves = [product("v0", q // 2, "xT0", "bank%d" % q, (q % 2) * HALF, (q % 2 + 1) * HALF) for q in range(PACK)]
+        late = []
+        for q in range(PACK):
+            h = q % 2
+            squash("v", ths[q // 2], halves[q], 2 * h, 2 * h + 2)
+            if q < 2:
+                late.append(product("v0", 2 + q, "xT0", "bank%d" % q))
+            turn("v", 0, q // 2, ths[q // 2], 2 * h, 2 * h + 2)
+        scores_1 = [product("v1", c, "xT1", "bank%d" % (c + 2)) for c in (0, 1)]
         for c in (2, 3):
-            turn("v", 0, c, late_th[c])
+            squash("v", ths[c], late[c - 2])
+            scores_1.append(product("v1", c, "xT1", "bank%d" % (c - 2)))
+        for c in (2, 3):
+            turn("v", 0, c, ths[c])
+        th_v1 = reused.tile([P, PACK, PACK, P], F32, name="th_v1", offset=16 * KB)
+        for c in range(PACK):
+            squash("v", th_v1[:, c], scores_1[c])
 
-        woven_v1 = shared.tile([P, 2 * N], U32, name="woven_v1", align_bytes=64, offset=3 * KB // 2)
-        weave(woven_v1[:], teacher[:, 2 * HALF :].rearrange("p (u n) -> p u n", u=2)[:, :, 0:N], False)
-        quantize("xT1", flat(xT1b_grouped[:]), HALF)
-        quantize("v1", woven_v1[:].bitcast(BF16), 0)
+        def xm_block(b, k):
+            return xm_raw[b, k // 2][:, :, (k % 2) * P : (k % 2 + 1) * P]
 
-        bank = product("xm0", 1, "g_first", "bank1")
-        xm0b_grouped = shared.tile([P, HALF, PACK], BF16, name="xm0b_grouped", align_bytes=64, offset=19 * KB // 2)
-        interleave(xm0b_grouped[:], xm0b[:])
-        quantize("xm0", flat(xm0b_grouped[:]), HALF)
-        put_first(0, 1, bank, staged, offset=8 * KB)
-        bank = product("xm0", 2, "g_first", "bank2")
-        g0b = shared.tile([P, HALF, PACK], BF16, name="g0b", align_bytes=64, offset=11 * KB)
-        interleave_on_gpsimd(g0b[:], weigh_half(0, 1, 13 * KB)[:])
-        put_first(0, 2, bank, tag="dw")
-        quantize("g", flat(g0b[:]), HALF)
+        def small(name):
+            return keep.tile([P, HALF], F32, name=name)
 
-        xm1_words = keep.tile([P, D], U32, name="xm1_words", align_bytes=64)
-        xm1_grouped = {}
+        def wide(name):
+            return keep.tile([P, N], F32, name=name)
 
-        def group_xm1(h, offset):
-            xm1_grouped[h] = shared.tile([P, HALF, PACK], BF16, name="xm1_grouped%d" % h, align_bytes=64, offset=offset)
-            for c in (0, P):
-                interleave_on_gpsimd(xm1_grouped[h][:, c : c + P, :], xm1[:, :, h * HALF + c : h * HALF + c + P])
+        def turn_1(c):
+            turn("w", 1, c, th_w1[:, c])
+            turn("v", 1, c, th_v1[:, c])
 
-        def quantize_xm1(h, offset):
-            scales = shared.tile([P, HALF], U8, name="xm1_scales%d" % h, align_bytes=64, offset=offset)
-            codes["xm1_%d" % h] = (xm1_words[:, h * HALF : (h + 1) * HALF], scales, E4M3)
-            quantize("xm1_%d" % h, flat(xm1_grouped[h][:]), 0)
+        dw = [reused.tile([P, B * N], F32, name="dw%d" % k, offset=4 * KB * k) for k in range(D // P)]
 
-        group_xm1(0, 10 * KB)
+        def gradients_0(h, tiles, bank_name):
+            bank = new_bank(bank_name)
+            for j, k in enumerate(tiles):
+                product("xm0", k, "g0", bank, h * HALF, (h + 1) * HALF, at=j * HALF)
+            for j, k in enumerate(tiles):
+                fetch(True, bank, j * HALF, (j + 1) * HALF, dw[k][:, h * HALF : (h + 1) * HALF])
 
-        steps = (("w", 0, "bank0"), ("w", 1, "bank1"), ("v", 0, "diff2"), ("v", 1, "diff3"))
-        scores = [product(name + "1", c, "xT1", bank_name) for name, c, bank_name in steps]
-        ths = staged_th("th_w01", 2, 24 * KB) + staged_th("th_v0", 1, 28 * KB) + staged_th("th_v1", 1, 30 * KB)
-        squash("w", 1, ths[0], scores[0])
-        put_first(0, 3, product("xm0", 3, "g_first", "bank0"), tag="dw")
-        turn("w", 1, 0, ths[0])
-        squash("w", 1, ths[1], scores[1])
-        late_scores = [product("w1", c, "xT1", bank_name) for c, bank_name in ((2, "bank3"), (3, "bank1"))]
-        turn("w", 1, 1, ths[1])
-        squash("v", 1, ths[2], scores[2])
-        turn("v", 1, 0, ths[2])
-        squash("v", 1, ths[3], scores[3])
-        put_second(0, 0, product("xm0", 0, "g", "diff2"), tag="dw")
-        turn("v", 1, 1, ths[3])
-        put_second(0, 1, product("xm0", 1, "g", "diff3"), tag="dw")
-        planes = weigh_half(1, 0, 16 * KB)
-        g1a = shared.tile([P, HALF, PACK], BF16, name="g1a", align_bytes=64, offset=0)
-        interleave(g1a[:], planes[:])
-        banks = [product("xm0", k, "g", "diff%d" % k) for k in (2, 3)]
-        quantize_xm1(0, 17 * KB + KB // 4)
-        quantize("g", flat(g1a[:]), 0)
-        group_xm1(1, 0)
-        for k in (2, 3):
-            put_second(0, k, banks[k - 2], shared, align_bytes=64, offset=(13 + k) * KB + KB // 4)
+        def put(on_scalar, k, i0, i1):
+            scatter(on_scalar, 0, k, i0, dw[k][:, i0:i1])
 
-        for c, bank, th in zip((2, 3), late_scores, staged_th("th_w2", 1, 12 * KB) + staged_th("th_w3", 1, 30 * KB)):
-            squash("w", 1, th, bank)
-            turn("w", 1, c, th)
-        scores = [product("v1", c, "xT1", "diff%d" % (c - 2)) for c in (2, 3)]
-        for c, bank, th in zip((2, 3), scores, staged_th("th_v23", 2, 24 * KB)):
-            squash("v", 1, th, bank)
-            turn("v", 1, c, th)
-        planes = weigh_half(1, 1, 18 * KB)
-        put_first(1, 0, product("xm1_0", 0, "g_first", "diff1"), tag="dw")
-        bank = product("xm1_0", 1, "g_first", "bank2")
-        g1b = keep.tile([P, HALF, PACK], BF16, name="g1b", align_bytes=64)
-        interleave(g1b[:], planes[:])
-        quantize("g", flat(g1b[:]), HALF)
-        quantize_xm1(1, 19 * KB + KB // 2)
-        put_first(1, 1, bank, shared, align_bytes=64, offset=18 * KB + KB // 2)
+        xm1a = held("xm1a", [P, HALF, PACK], BF16, 6 * KB)
         for k in range(2):
-            put_second(1, k, product("xm1_0", k, "g", "diff%d" % (k + 2)), tag="dw")
-            store(k)
-        put(1, 2, product("xm1_1", 0, "g", "bank0"), 0, 0, N, tag="dw")
-        store(2)
-        put(1, 3, product("xm1_1", 1, "g", "bank1"), 0, 0, N, tag="dw")
-        nc.sync.dma_start(out=out[3 * P :, 0 : T // 2], in_=placed[3][:, 0 : T // 2])
-        nc.scalar.dma_start(out=out[3 * P :, T // 2 :], in_=placed[3][:, T // 2 :])
+            interleave(nc.scalar.copy, xm1a[:, k * P : (k + 1) * P, :], xm_block(1, k))
+        g0a = held("g0a", [P, HALF, PACK], BF16, 0)
+        weigh(g0a[:], 0, 0)
+        weigh(g0a[:], 0, 1)
+        quantize("xm0", flat(xm0b[:]), HALF)
+        quantize("g0", flat(g0a[:]), 0, E5M2)
+        gradients_0(0, (1, 0), "bank0")
+        put(True, 1, 0, HALF)
+
+        g0b = held("g0b", [P, HALF, PACK], BF16, 2 * KB)
+        weigh(g0b[:], 0, 2)
+        weigh(g0b[:], 0, 3)
+        quantize("g0", flat(g0b[:]), HALF, E5M2)
+        xm13 = held("xm13", [P, P, PACK], BF16, 2 * KB)
+        interleave_on_gpsimd(xm13[:], xm_block(1, 3))
+        gradients_0(1, (1, 0), "bank1")
+        put(True, 1, HALF, N)
+        gradients_0(0, (3, 2), "bank2")
+        put(True, 0, 0, HALF)
+        gradients_0(1, (3, 2), "bank3")
+        put(True, 0, HALF, N)
+        put(True, 3, 0, SHARE_3)
+        for c in range(PACK):
+            turn_1(c)
+        g1a = held("g1a", [P, HALF, PACK], BF16, 4 * KB)
+        weigh(g1a[:], 1, 0)
+        weigh(g1a[:], 1, 1)
+        quantize("g1", flat(g1a[:]), 0, E5M2)
+        quantize("xm1", flat(xm1a[:]), 0, scales_at=4 * KB)
+        xm12 = held("xm12", [P, P, PACK], BF16, 6 * KB)
+        interleave_on_gpsimd(xm12[:], xm_block(1, 2))
+        g1b = held("g1b", [P, HALF, PACK], BF16, 8 * KB)
+        weigh(g1b[:], 1, 2)
+        third = product("xm1", 1, "g1", "diff2", 0, HALF)
+        weigh(g1b[:], 1, 3)
+        fetch(False, third, 0, HALF, dw[1][:, N : N + HALF])
+        quantize("g1", flat(g1b[:]), HALF, E5M2)
+        quantize("xm13", flat(xm13[:]), 0, scales_at=8 * KB)
+        quantize("xm12", flat(xm12[:]), 0, scales_at=9 * KB)
+        put(False, 1, N, N + HALF)
+        fetch(False, product("xm1", 1, "g1", "diff3", HALF, N), HALF, N, dw[1][:, N + HALF :])
+        fetch(False, product("xm1", 0, "g1", "diff0"), 0, N, dw[0][:, N:])
+        put(False, 1, N + HALF, B * N)
+        store(1)
+        put(False, 0, N, B * N)
+        store(0)
+        fetch(True, product("xm13", 0, "g1", "diff1"), 0, N, dw[3][:, N:])
+        fetch(True, product("xm12", 0, "g1", "diff2"), 0, N, dw[2][:, N:])
+        put(False, 3, SHARE_3, B * N)
+        store(3)
+        put(True, 2, 640, B * N)
+        put(True, 2, HALF, 640)
+        put(True, 2, 0, HALF)
+        nc.sync.dma_start(out=out[2 * P : 3 * P, 0 : T // 2], in_=placed[2][:, 0 : T // 2])
+        nc.scalar.dma_start(out=out[2 * P : 3 * P, T // 2 :], in_=placed[2][:, T // 2 :])

@@ -24,7 +24,6 @@ PER_COL = 16
 HALF = N // 2
 RUN = 4
 KB = 1024
-SHARE_3 = 352
 
 
 def tile_attend_gds_nce_kernel(tc, xT, wT, vT, wt, xm, offs, out):
@@ -86,13 +85,11 @@ def tile_attend_gds_nce_kernel(tc, xT, wT, vT, wt, xm, offs, out):
 
         codes = {}
 
-        def quantize(key, values, c0, fmt=E4M3, scales_at=None):
+        def quantize(key, values, c0, fmt=E4M3, scales=None):
             if key not in codes:
                 words = keep.tile([P, N], U32, name="words_" + key, align_bytes=64)
-                if scales_at is None:
+                if scales is None:
                     scales = keep.tile([P, N], U8, name="scales_" + key, align_bytes=64)
-                else:
-                    scales = shared.tile([P, N], U8, name="scales_" + key, align_bytes=64, offset=scales_at)
                 codes[key] = (words, scales, fmt)
             words, scales, fmt = codes[key]
             c1 = c0 + values.shape[1] // PACK
@@ -165,11 +162,12 @@ def tile_attend_gds_nce_kernel(tc, xT, wT, vT, wt, xm, offs, out):
         def store(k):
             nc.sync.dma_start(out=out[k * P : (k + 1) * P, :], in_=placed[k][:])
 
-        bring("w", 0)
+        xT0_raw = load("xT0", xT[0], 0, R)
         nc.sync.dma_start(offsets[:], offs)
-        for t in range(1, PACK):
+        for t in range(PACK):
             bring("w", t)
-        xT_raw = [load("xT%d" % b, xT[b], 0, R) for b in range(B)]
+        xT1_raw = reused.tile([P, PACK, R], F32, name="xT1", offset=32 * KB)
+        nc.sync.dma_start(out=xT1_raw[:], in_=by_rows(xT[1]))
         for t in range(PACK):
             bring("v", t)
         xm_raw = {}
@@ -179,59 +177,73 @@ def tile_attend_gds_nce_kernel(tc, xT, wT, vT, wt, xm, offs, out):
         xm_raw[1, 0] = load("xm10", xm[1], 0, HALF)
         xm_raw[1, 1] = load("xm11", xm[1], HALF, D)
 
-        w0 = keep.tile([P, N, PACK], BF16, name="w0", align_bytes=64)
+        xT_grouped = [keep.tile([P, R, PACK], BF16, name="xT_grouped%d" % b, align_bytes=64) for b in range(B)]
+        deal(nc.vector.tensor_copy, xT_grouped[0][:], xT0_raw[:])
+        quantize("xT0", flat(xT_grouped[0][:]), 0)
+        w0 = [keep.tile([P, HALF, PACK], BF16, name="w0%d" % h, align_bytes=64) for h in range(2)]
         w1 = keep.tile([P, N, PACK], BF16, name="w1", align_bytes=64)
         w1_planes = keep.tile([P, PACK, N], BF16, name="w1_planes", align_bytes=64)
         for t in range(PACK):
-            gather_into_words(w0[:], "w", t, 0, N)
+            for h in range(2):
+                gather_into_words(w0[h][:], "w", t, h * HALF, HALF)
             gather_plane(w1_planes[:], "w", t, N, N)
-        quantize("w0", flat(w0[:]), 0)
-        interleave(nc.scalar.copy, w1[:], w1_planes[:])
-        xT0_grouped = held("xT0_grouped", [P, R, PACK], BF16, 12 * KB)
-        xT1_grouped = keep.tile([P, R, PACK], BF16, name="xT1_grouped", align_bytes=64)
-        deal(nc.vector.tensor_copy, xT0_grouped[:], xT_raw[0][:])
-        quantize("xT0", flat(xT0_grouped[:]), 0)
-        deal(nc.vector.tensor_copy, xT1_grouped[:], xT_raw[1][:])
-        quantize("w1", flat(w1[:]), 0, scales_at=12 * KB)
-        quantize("xT1", flat(xT1_grouped[:]), 0)
+            if t % 2 == 1:
+                interleave(nc.scalar.copy, w1[:, :, t - 1 : t + 1], w1_planes[:, t - 1 : t + 1, :])
+        for h in range(2):
+            quantize("w0", flat(w0[h][:]), h * HALF)
+        deal(nc.vector.tensor_copy, xT_grouped[1][:], xT1_raw[:])
+        w1_scales = reused.tile([P, N], U8, name="w1_scales", align_bytes=64, offset=32 * KB)
+        quantize("w1", flat(w1[:]), 0, scales=w1_scales)
+        quantize("xT1", flat(xT_grouped[1][:]), 0)
         for c in range(PACK):
             th = ring_th()
             squash("w", th, product("w0", c, "xT0", "bank%d" % c))
             turn("w", 0, c, th)
 
         v0 = [keep.tile([P, HALF, PACK], BF16, name="v0%d" % h, align_bytes=64) for h in range(2)]
-        v1 = [keep.tile([P, HALF, PACK], BF16, name="v1%d" % h, align_bytes=64) for h in range(2)]
+        v1 = [held("v1%d" % h, [P, HALF, PACK], BF16, (8 + 2 * h) * KB) for h in range(2)]
+        v0_planes = keep.tile([P, PACK, HALF], BF16, name="v0_planes", align_bytes=64)
         v1_planes = keep.tile([P, PACK, N], BF16, name="v1_planes", align_bytes=64)
-        v0_last = keep.tile([P, HALF], BF16, name="v0_last", align_bytes=64)
         th_w1 = reused.tile([P, PACK, PACK, P], F32, name="th_w1", offset=24 * KB)
+
+        def pair_up(u):
+            pair = slice(2 * u, 2 * u + 2)
+            interleave(nc.vector.tensor_copy, v0[1][:, :, pair], v0_planes[:, pair, :])
+
         last = PACK - 1
         for t in range(last):
-            for h in range(2):
-                gather_into_words(v0[h][:], "v", t, h * HALF, HALF)
+            gather_into_words(v0[0][:], "v", t, 0, HALF)
+            nc.vector.tensor_copy(v0_planes[:, t, :], planes["v", t][:].indirect(entries(HALF, HALF)))
             if t == 1:
                 nc.vector.tensor_copy(v1_planes[:, t, 0:HALF], planes["v", t][:].indirect(entries(N, HALF)))
+                pair_up(0)
                 gather_plane(v1_planes[:, :, HALF:N], "v", t, N + HALF, HALF)
             else:
                 gather_plane(v1_planes[:], "v", t, N, N)
             for c in ((0, 1), (2, 3), ())[t]:
                 squash("w", th_w1[:, c], product("w1", c, "xT1", "bank%d" % c))
-        nc.scalar.activation(v0_last[:], planes["v", last][:].indirect(entries(HALF, HALF)), COPY)
+        gather_plane(v0_planes[:], "v", last, HALF, HALF)
         for h in range(2):
             gather_plane(v1_planes[:, :, h * HALF : (h + 1) * HALF], "v", last, N + h * HALF, HALF)
         gather_into_words(v0[0][:], "v", last, 0, HALF)
         quantize("v0", flat(v0[0][:]), 0)
-        nc.vector.tensor_copy(v0[1][:, :, last], v0_last[:])
+        pair_up(1)
         quantize("v0", flat(v0[1][:]), HALF)
-        for c in range(2):
-            interleave(nc.vector.tensor_copy, v1[0][:, c * P : (c + 1) * P, :], v1_planes[:, :, c * P : (c + 1) * P])
-        xm0a = keep.tile([P, HALF, PACK], BF16, name="xm0a", align_bytes=64)
-        interleave(nc.vector.tensor_copy, xm0a[:], xm_raw[0, 0][:])
-        quantize("v1", flat(v1[0][:]), 0)
-        interleave(nc.vector.tensor_copy, v1[1][:], v1_planes[:, :, HALF:N])
-        quantize("xm0", flat(xm0a[:]), 0)
-        quantize("v1", flat(v1[1][:]), HALF)
-        xm0b = keep.tile([P, HALF, PACK], BF16, name="xm0b", align_bytes=64)
-        interleave(nc.vector.tensor_copy, xm0b[:], xm_raw[0, 1][:])
+        for h in range(2):
+            for c in range(2):
+                interleave(nc.vector.tensor_copy, v1[h][:, c * P : (c + 1) * P, :], v1_planes[:, :, (2 * h + c) * P : (2 * h + c + 1) * P])
+            for c in range(2):
+                quantize("v1", flat(v1[h][:, c * P : (c + 1) * P, :]), (2 * h + c) * P)
+
+        def group_xm(b, h, offset):
+            grouped = held("xm%d%d" % (b, h), [P, HALF, PACK], BF16, offset)
+            interleave(nc.vector.tensor_copy, grouped[:], xm_raw[b, h][:])
+            return grouped
+
+        def quantize_xm(b, h, grouped):
+            quantize("xm%d" % b, flat(grouped[:]), h * HALF)
+
+        xm00 = group_xm(0, 0, 11 * KB)
 
         ths = [ring_th() for c in range(PACK)]
         halves = [product("v0", q // 2, "xT0", "bank%d" % q, (q % 2) * HALF, (q % 2 + 1) * HALF) for q in range(PACK)]
@@ -277,47 +289,42 @@ def tile_attend_gds_nce_kernel(tc, xT, wT, vT, wt, xm, offs, out):
         def put(on_scalar, k, i0, i1):
             scatter(on_scalar, 0, k, i0, dw[k][:, i0:i1])
 
-        xm1a = held("xm1a", [P, HALF, PACK], BF16, 6 * KB)
-        for k in range(2):
-            interleave(nc.scalar.copy, xm1a[:, k * P : (k + 1) * P, :], xm_block(1, k))
         g0a = held("g0a", [P, HALF, PACK], BF16, 0)
         weigh(g0a[:], 0, 0)
+        quantize_xm(0, 0, xm00)
         weigh(g0a[:], 0, 1)
-        quantize("xm0", flat(xm0b[:]), HALF)
         quantize("g0", flat(g0a[:]), 0, E5M2)
-        gradients_0(0, (1, 0), "bank0")
+        gradients_0(0, (1, 0), "bank2")
         put(True, 1, 0, HALF)
 
         g0b = held("g0b", [P, HALF, PACK], BF16, 2 * KB)
         weigh(g0b[:], 0, 2)
         weigh(g0b[:], 0, 3)
+        xm01 = group_xm(0, 1, 0)
         quantize("g0", flat(g0b[:]), HALF, E5M2)
-        xm13 = held("xm13", [P, P, PACK], BF16, 2 * KB)
-        interleave_on_gpsimd(xm13[:], xm_block(1, 3))
-        gradients_0(1, (1, 0), "bank1")
+        quantize_xm(0, 1, xm01)
+        gradients_0(1, (1, 0), "bank3")
         put(True, 1, HALF, N)
-        gradients_0(0, (3, 2), "bank2")
+        gradients_0(0, (3, 2), "bank0")
         put(True, 0, 0, HALF)
-        gradients_0(1, (3, 2), "bank3")
+        gradients_0(1, (3, 2), "bank1")
+        put(True, 3, 0, HALF)
         put(True, 0, HALF, N)
-        put(True, 3, 0, SHARE_3)
+        put(True, 3, HALF, N)
         for c in range(PACK):
             turn_1(c)
         g1a = held("g1a", [P, HALF, PACK], BF16, 4 * KB)
         weigh(g1a[:], 1, 0)
         weigh(g1a[:], 1, 1)
         quantize("g1", flat(g1a[:]), 0, E5M2)
-        quantize("xm1", flat(xm1a[:]), 0, scales_at=4 * KB)
-        xm12 = held("xm12", [P, P, PACK], BF16, 6 * KB)
-        interleave_on_gpsimd(xm12[:], xm_block(1, 2))
-        g1b = held("g1b", [P, HALF, PACK], BF16, 8 * KB)
+        g1b = held("g1b", [P, HALF, PACK], BF16, 6 * KB)
         weigh(g1b[:], 1, 2)
+        for h in range(2):
+            quantize_xm(1, h, group_xm(1, h, 2 * KB * h))
         third = product("xm1", 1, "g1", "diff2", 0, HALF)
         weigh(g1b[:], 1, 3)
         fetch(False, third, 0, HALF, dw[1][:, N : N + HALF])
         quantize("g1", flat(g1b[:]), HALF, E5M2)
-        quantize("xm13", flat(xm13[:]), 0, scales_at=8 * KB)
-        quantize("xm12", flat(xm12[:]), 0, scales_at=9 * KB)
         put(False, 1, N, N + HALF)
         fetch(False, product("xm1", 1, "g1", "diff3", HALF, N), HALF, N, dw[1][:, N + HALF :])
         fetch(False, product("xm1", 0, "g1", "diff0"), 0, N, dw[0][:, N:])
@@ -325,9 +332,9 @@ def tile_attend_gds_nce_kernel(tc, xT, wT, vT, wt, xm, offs, out):
         store(1)
         put(False, 0, N, B * N)
         store(0)
-        fetch(True, product("xm13", 0, "g1", "diff1"), 0, N, dw[3][:, N:])
-        fetch(True, product("xm12", 0, "g1", "diff2"), 0, N, dw[2][:, N:])
-        put(False, 3, SHARE_3, B * N)
+        fetch(True, product("xm1", 2, "g1", "diff2"), 0, N, dw[2][:, N:])
+        fetch(True, product("xm1", 3, "g1", "diff1"), 0, N, dw[3][:, N:])
+        put(False, 3, N, B * N)
         store(3)
         put(True, 2, 640, B * N)
         put(True, 2, HALF, 640)

@@ -24,6 +24,7 @@ PER_COL = 16
 HALF = N // 2
 RUN = 4
 KB = 1024
+HELP = (0, 0, 0)
 
 
 def tile_attend_gds_nce_kernel(tc, xT, wT, vT, wt, xm, offs, out):
@@ -57,8 +58,9 @@ def tile_attend_gds_nce_kernel(tc, xT, wT, vT, wt, xm, offs, out):
         planes = {}
 
         def bring(name, t):
-            if name == "w":
-                planes[name, t] = reused.tile([P, T], F32, name="plane_w%d" % t, offset=8 * KB * t)
+            if name == "w" or t == 1:
+                place = 8 * KB * (t if name == "w" else PACK)
+                planes[name, t] = reused.tile([P, T], F32, name="plane_%s%d" % (name, t), offset=place)
             else:
                 planes[name, t] = keep.tile([P, T], F32, name="plane_v%d" % t)
             nc.sync.dma_start(out=planes[name, t][:], in_=by_rows(tables[name])[:, t, :])
@@ -166,10 +168,9 @@ def tile_attend_gds_nce_kernel(tc, xT, wT, vT, wt, xm, offs, out):
         nc.sync.dma_start(offsets[:], offs)
         for t in range(PACK):
             bring("w", t)
-        xT1_raw = reused.tile([P, PACK, R], F32, name="xT1", offset=32 * KB)
-        nc.sync.dma_start(out=xT1_raw[:], in_=by_rows(xT[1]))
         for t in range(PACK):
             bring("v", t)
+        xT1_raw = [load("xT1%d" % h, xT[1], h * HALF, (h + 1) * HALF) for h in range(2)]
         xm_raw = {}
         xm_raw[0, 0] = load("xm00", xm[0], 0, HALF)
         nc.sync.dma_start(out=weights[:], in_=wt.rearrange("b (p t) o -> p b (t o)", t=PACK))
@@ -188,52 +189,54 @@ def tile_attend_gds_nce_kernel(tc, xT, wT, vT, wt, xm, offs, out):
                 gather_into_words(w0[h][:], "w", t, h * HALF, HALF)
             gather_plane(w1_planes[:], "w", t, N, N)
             if t % 2 == 1:
-                interleave(nc.scalar.copy, w1[:, :, t - 1 : t + 1], w1_planes[:, t - 1 : t + 1, :])
+                interleave(nc.vector.tensor_copy, w1[:, :, t - 1 : t + 1], w1_planes[:, t - 1 : t + 1, :])
         for h in range(2):
             quantize("w0", flat(w0[h][:]), h * HALF)
-        deal(nc.vector.tensor_copy, xT_grouped[1][:], xT1_raw[:])
-        w1_scales = reused.tile([P, N], U8, name="w1_scales", align_bytes=64, offset=32 * KB)
-        quantize("w1", flat(w1[:]), 0, scales=w1_scales)
-        quantize("xT1", flat(xT_grouped[1][:]), 0)
-        for c in range(PACK):
-            th = ring_th()
+
+        def student_scores(c, th):
             squash("w", th, product("w0", c, "xT0", "bank%d" % c))
             turn("w", 0, c, th)
 
-        v0 = [keep.tile([P, HALF, PACK], BF16, name="v0%d" % h, align_bytes=64) for h in range(2)]
-        v1 = [held("v1%d" % h, [P, HALF, PACK], BF16, (8 + 2 * h) * KB) for h in range(2)]
-        v0_planes = keep.tile([P, PACK, HALF], BF16, name="v0_planes", align_bytes=64)
+        quarters = [keep.tile([P, HALF, PACK], BF16, name="v_q%d" % q, align_bytes=64) for q in range(PACK)]
+        v_planes = [keep.tile([P, PACK, HALF], BF16, name="v0_planes", align_bytes=64)]
         v1_planes = keep.tile([P, PACK, N], BF16, name="v1_planes", align_bytes=64)
-        th_w1 = reused.tile([P, PACK, PACK, P], F32, name="th_w1", offset=24 * KB)
+        sources = {1: v_planes[0][:], 2: v1_planes[:, :, 0:HALF], 3: v1_planes[:, :, HALF:N]}
 
-        def pair_up(u):
+        def pair_up(q, u, move=nc.vector.tensor_copy):
             pair = slice(2 * u, 2 * u + 2)
-            interleave(nc.vector.tensor_copy, v0[1][:, :, pair], v0_planes[:, pair, :])
+            interleave(move, quarters[q][:, :, pair], sources[q][:, pair, :])
 
         last = PACK - 1
         for t in range(last):
-            gather_into_words(v0[0][:], "v", t, 0, HALF)
-            nc.vector.tensor_copy(v0_planes[:, t, :], planes["v", t][:].indirect(entries(HALF, HALF)))
+            gather_into_words(quarters[0][:], "v", t, 0, HALF)
+            nc.vector.tensor_copy(sources[1][:, t, :], planes["v", t][:].indirect(entries(HALF, HALF)))
+            share = HELP[t]
+            if share:
+                nc.vector.tensor_copy(v1_planes[:, t, 0:share], planes["v", t][:].indirect(entries(N, share)))
+            gather_plane(v1_planes[:, :, share:N], "v", t, N + share, N - share)
+            if t == 0:
+                quantize("w1", flat(w1[:]), 0)
+                student_scores(0, ring_th())
+                student_scores(1, ring_th())
             if t == 1:
-                nc.vector.tensor_copy(v1_planes[:, t, 0:HALF], planes["v", t][:].indirect(entries(N, HALF)))
-                pair_up(0)
-                gather_plane(v1_planes[:, :, HALF:N], "v", t, N + HALF, HALF)
-            else:
-                gather_plane(v1_planes[:], "v", t, N, N)
-            for c in ((0, 1), (2, 3), ())[t]:
-                squash("w", th_w1[:, c], product("w1", c, "xT1", "bank%d" % c))
-        gather_plane(v0_planes[:], "v", last, HALF, HALF)
+                for q in range(1, PACK):
+                    pair_up(q, 0)
+                held_th = reused.tile([P, 2, PACK, P], F32, name="held_th", offset=32 * KB)
+                student_scores(2, held_th[:, 0])
+                student_scores(3, held_th[:, 1])
+        for q in range(1, PACK):
+            gather_plane(sources[q], "v", last, q * HALF, HALF)
+        pair_up(2, 1, nc.scalar.copy)
+        gather_into_words(quarters[0][:], "v", last, 0, HALF)
+        quantize("v0", flat(quarters[0][:]), 0)
+        pair_up(1, 1)
+        quantize("v0", flat(quarters[1][:]), HALF)
         for h in range(2):
-            gather_plane(v1_planes[:, :, h * HALF : (h + 1) * HALF], "v", last, N + h * HALF, HALF)
-        gather_into_words(v0[0][:], "v", last, 0, HALF)
-        quantize("v0", flat(v0[0][:]), 0)
-        pair_up(1)
-        quantize("v0", flat(v0[1][:]), HALF)
-        for h in range(2):
-            for c in range(2):
-                interleave(nc.vector.tensor_copy, v1[h][:, c * P : (c + 1) * P, :], v1_planes[:, :, (2 * h + c) * P : (2 * h + c + 1) * P])
-            for c in range(2):
-                quantize("v1", flat(v1[h][:, c * P : (c + 1) * P, :]), (2 * h + c) * P)
+            deal(nc.vector.tensor_copy, xT_grouped[1][:, h * HALF : (h + 1) * HALF, :], xT1_raw[h][:])
+            if h == 1:
+                pair_up(3, 1)
+            quantize("xT1", flat(xT_grouped[1][:, h * HALF : (h + 1) * HALF, :]), h * HALF)
+            quantize("v1", flat(quarters[2 + h][:]), h * HALF)
 
         def group_xm(b, h, offset):
             grouped = held("xm%d%d" % (b, h), [P, HALF, PACK], BF16, offset)
@@ -243,7 +246,8 @@ def tile_attend_gds_nce_kernel(tc, xT, wT, vT, wt, xm, offs, out):
         def quantize_xm(b, h, grouped):
             quantize("xm%d" % b, flat(grouped[:]), h * HALF)
 
-        xm00 = group_xm(0, 0, 11 * KB)
+        xm00 = group_xm(0, 0, 12 * KB)
+        quantize_xm(0, 0, xm00)
 
         ths = [ring_th() for c in range(PACK)]
         halves = [product("v0", q // 2, "xT0", "bank%d" % q, (q % 2) * HALF, (q % 2 + 1) * HALF) for q in range(PACK)]
@@ -254,15 +258,20 @@ def tile_attend_gds_nce_kernel(tc, xT, wT, vT, wt, xm, offs, out):
             if q < 2:
                 late.append(product("v0", 2 + q, "xT0", "bank%d" % q))
             turn("v", 0, q // 2, ths[q // 2], 2 * h, 2 * h + 2)
-        scores_1 = [product("v1", c, "xT1", "bank%d" % (c + 2)) for c in (0, 1)]
         for c in (2, 3):
             squash("v", ths[c], late[c - 2])
-            scores_1.append(product("v1", c, "xT1", "bank%d" % (c - 2)))
-        for c in (2, 3):
-            turn("v", 0, c, ths[c])
-        th_v1 = reused.tile([P, PACK, PACK, P], F32, name="th_v1", offset=16 * KB)
+        th_1 = reused.tile([P, 2 * PACK, PACK, P], F32, name="th_1", offset=16 * KB)
         for c in range(PACK):
-            squash("v", th_v1[:, c], scores_1[c])
+            for j, name in enumerate("wv"):
+                bank = product(name + "1", c, "xT1", "bank%d" % ((2 * c + j + 2) % PACK))
+                nc.scalar.activation(
+                    th_1[:, 2 * c + j].rearrange("p t (h m) -> p t h m", h=2),
+                    bank[:].rearrange("p (h t m) -> p t h m", h=2, t=PACK),
+                    TANH, scale=0.5 if name == "w" else -0.5,
+                )
+            if c == 0:
+                for c0 in (2, 3):
+                    turn("v", 0, c0, ths[c0])
 
         def xm_block(b, k):
             return xm_raw[b, k // 2][:, :, (k % 2) * P : (k % 2 + 1) * P]
@@ -274,8 +283,8 @@ def tile_attend_gds_nce_kernel(tc, xT, wT, vT, wt, xm, offs, out):
             return keep.tile([P, N], F32, name=name)
 
         def turn_1(c):
-            turn("w", 1, c, th_w1[:, c])
-            turn("v", 1, c, th_v1[:, c])
+            turn("w", 1, c, th_1[:, 2 * c])
+            turn("v", 1, c, th_1[:, 2 * c + 1])
 
         dw = [reused.tile([P, B * N], F32, name="dw%d" % k, offset=4 * KB * k) for k in range(D // P)]
 
@@ -291,11 +300,10 @@ def tile_attend_gds_nce_kernel(tc, xT, wT, vT, wt, xm, offs, out):
 
         g0a = held("g0a", [P, HALF, PACK], BF16, 0)
         weigh(g0a[:], 0, 0)
-        quantize_xm(0, 0, xm00)
         weigh(g0a[:], 0, 1)
         quantize("g0", flat(g0a[:]), 0, E5M2)
-        gradients_0(0, (1, 0), "bank2")
-        put(True, 1, 0, HALF)
+        gradients_0(0, (0, 1), "bank2")
+        put(True, 0, 0, HALF)
 
         g0b = held("g0b", [P, HALF, PACK], BF16, 2 * KB)
         weigh(g0b[:], 0, 2)
@@ -303,14 +311,16 @@ def tile_attend_gds_nce_kernel(tc, xT, wT, vT, wt, xm, offs, out):
         xm01 = group_xm(0, 1, 0)
         quantize("g0", flat(g0b[:]), HALF, E5M2)
         quantize_xm(0, 1, xm01)
-        gradients_0(1, (1, 0), "bank3")
-        put(True, 1, HALF, N)
-        gradients_0(0, (3, 2), "bank0")
-        put(True, 0, 0, HALF)
-        gradients_0(1, (3, 2), "bank1")
-        put(True, 3, 0, HALF)
+        gradients_0(1, (0, 1), "bank3")
         put(True, 0, HALF, N)
-        put(True, 3, HALF, N)
+        fetch(True, product("xm0", 3, "g0", "bank0"), 0, N, dw[3][:, 0:N])
+        fetch(True, product("xm0", 2, "g0", "bank1"), 0, N, dw[2][:, 0:N])
+        put(True, 3, 0, HALF)
+        put(True, 2, 0, 384)
+        for h in range(2):
+            quantize_xm(1, h, group_xm(1, h, 2 * KB * (1 - h)))
+        put(False, 1, 0, HALF)
+        put(False, 1, HALF, N)
         for c in range(PACK):
             turn_1(c)
         g1a = held("g1a", [P, HALF, PACK], BF16, 4 * KB)
@@ -319,25 +329,25 @@ def tile_attend_gds_nce_kernel(tc, xT, wT, vT, wt, xm, offs, out):
         quantize("g1", flat(g1a[:]), 0, E5M2)
         g1b = held("g1b", [P, HALF, PACK], BF16, 6 * KB)
         weigh(g1b[:], 1, 2)
-        for h in range(2):
-            quantize_xm(1, h, group_xm(1, h, 2 * KB * h))
         third = product("xm1", 1, "g1", "diff2", 0, HALF)
         weigh(g1b[:], 1, 3)
         fetch(False, third, 0, HALF, dw[1][:, N : N + HALF])
         quantize("g1", flat(g1b[:]), HALF, E5M2)
         put(False, 1, N, N + HALF)
         fetch(False, product("xm1", 1, "g1", "diff3", HALF, N), HALF, N, dw[1][:, N + HALF :])
-        fetch(False, product("xm1", 0, "g1", "diff0"), 0, N, dw[0][:, N:])
+        fetch(False, product("xm1", 3, "g1", "diff1"), 0, N, dw[3][:, N:])
         put(False, 1, N + HALF, B * N)
         store(1)
-        put(False, 0, N, B * N)
+        bank_01 = product("xm1", 0, "g1", "bank2")
+        for h in range(2):
+            fetch(True, bank_01, h * HALF, (h + 1) * HALF, dw[0][:, N + h * HALF : N + (h + 1) * HALF])
+        for h in range(2):
+            put(True, 0, N + h * HALF, N + (h + 1) * HALF)
         store(0)
-        fetch(True, product("xm1", 2, "g1", "diff2"), 0, N, dw[2][:, N:])
-        fetch(True, product("xm1", 3, "g1", "diff1"), 0, N, dw[3][:, N:])
-        put(False, 3, N, B * N)
+        fetch(False, product("xm1", 2, "g1", "diff0"), 0, N, dw[2][:, N:])
+        put(False, 3, HALF, B * N)
         store(3)
-        put(True, 2, 640, B * N)
-        put(True, 2, HALF, 640)
-        put(True, 2, 0, HALF)
+        put(True, 2, 384, 768)
+        put(True, 2, 768, B * N)
         nc.sync.dma_start(out=out[2 * P : 3 * P, 0 : T // 2], in_=placed[2][:, 0 : T // 2])
         nc.scalar.dma_start(out=out[2 * P : 3 * P, T // 2 :], in_=placed[2][:, T // 2 :])

@@ -188,10 +188,10 @@ def tile_attend_gds_nce_kernel(tc, xT, wT, vT, wt, xm, offs, out):
             for h in range(2):
                 gather_into_words(w0[h][:], "w", t, h * HALF, HALF)
             gather_plane(w1_planes[:], "w", t, N, N)
-            if t % 2 == 1:
-                interleave(nc.vector.tensor_copy, w1[:, :, t - 1 : t + 1], w1_planes[:, t - 1 : t + 1, :])
         for h in range(2):
             quantize("w0", flat(w0[h][:]), h * HALF)
+        for h, move in enumerate((nc.scalar.copy, nc.vector.tensor_copy)):
+            interleave(move, w1[:, h * HALF : (h + 1) * HALF, :], w1_planes[:, :, h * HALF : (h + 1) * HALF])
 
         def student_scores(c, th):
             squash("w", th, product("w0", c, "xT0", "bank%d" % c))
@@ -202,9 +202,8 @@ def tile_attend_gds_nce_kernel(tc, xT, wT, vT, wt, xm, offs, out):
         v1_planes = keep.tile([P, PACK, N], BF16, name="v1_planes", align_bytes=64)
         sources = {1: v_planes[0][:], 2: v1_planes[:, :, 0:HALF], 3: v1_planes[:, :, HALF:N]}
 
-        def pair_up(q, u, move=nc.vector.tensor_copy):
-            pair = slice(2 * u, 2 * u + 2)
-            interleave(move, quarters[q][:, :, pair], sources[q][:, pair, :])
+        def word_up(q, c0=0, c1=HALF, move=nc.vector.tensor_copy):
+            interleave(move, quarters[q][:, c0:c1, :], sources[q][:, :, c0:c1])
 
         last = PACK - 1
         for t in range(last):
@@ -216,54 +215,43 @@ def tile_attend_gds_nce_kernel(tc, xT, wT, vT, wt, xm, offs, out):
             gather_plane(v1_planes[:, :, share:N], "v", t, N + share, N - share)
             if t == 0:
                 quantize("w1", flat(w1[:]), 0)
-                student_scores(0, ring_th())
-                student_scores(1, ring_th())
-            if t == 1:
-                for q in range(1, PACK):
-                    pair_up(q, 0)
-                held_th = reused.tile([P, 2, PACK, P], F32, name="held_th", offset=32 * KB)
-                student_scores(2, held_th[:, 0])
-                student_scores(3, held_th[:, 1])
+                for c in range(PACK):
+                    student_scores(c, ring_th())
         for q in range(1, PACK):
             gather_plane(sources[q], "v", last, q * HALF, HALF)
-        pair_up(2, 1, nc.scalar.copy)
+        word_up(2, 0, P, nc.scalar.copy)
         gather_into_words(quarters[0][:], "v", last, 0, HALF)
         quantize("v0", flat(quarters[0][:]), 0)
-        pair_up(1, 1)
+        word_up(1)
         quantize("v0", flat(quarters[1][:]), HALF)
         for h in range(2):
             deal(nc.vector.tensor_copy, xT_grouped[1][:, h * HALF : (h + 1) * HALF, :], xT1_raw[h][:])
-            if h == 1:
-                pair_up(3, 1)
+            word_up(2 + h, P * (1 - h), HALF - P * h)
             quantize("xT1", flat(xT_grouped[1][:, h * HALF : (h + 1) * HALF, :]), h * HALF)
+            if h == 1:
+                word_up(3, P)
             quantize("v1", flat(quarters[2 + h][:]), h * HALF)
 
-        def group_xm(b, h, offset):
+        def group_xm(b, h, offset, move=nc.vector.tensor_copy):
             grouped = held("xm%d%d" % (b, h), [P, HALF, PACK], BF16, offset)
-            interleave(nc.vector.tensor_copy, grouped[:], xm_raw[b, h][:])
+            interleave(move, grouped[:], xm_raw[b, h][:])
             return grouped
 
         def quantize_xm(b, h, grouped):
             quantize("xm%d" % b, flat(grouped[:]), h * HALF)
 
-        xm00 = group_xm(0, 0, 12 * KB)
-        quantize_xm(0, 0, xm00)
 
         ths = [ring_th() for c in range(PACK)]
-        halves = [product("v0", q // 2, "xT0", "bank%d" % q, (q % 2) * HALF, (q % 2 + 1) * HALF) for q in range(PACK)]
-        late = []
-        for q in range(PACK):
-            h = q % 2
-            squash("v", ths[q // 2], halves[q], 2 * h, 2 * h + 2)
-            if q < 2:
-                late.append(product("v0", 2 + q, "xT0", "bank%d" % q))
-            turn("v", 0, q // 2, ths[q // 2], 2 * h, 2 * h + 2)
-        for c in (2, 3):
-            squash("v", ths[c], late[c - 2])
+        scores_0 = [product("v0", c, "xT0", "bank%d" % c) for c in range(PACK)]
+        for c in range(PACK):
+            squash("v", ths[c], scores_0[c])
+        xm00 = group_xm(0, 0, 12 * KB, nc.scalar.copy)
+        for c in (0, 1):
+            turn("v", 0, c, ths[c])
         th_1 = reused.tile([P, 2 * PACK, PACK, P], F32, name="th_1", offset=16 * KB)
         for c in range(PACK):
             for j, name in enumerate("wv"):
-                bank = product(name + "1", c, "xT1", "bank%d" % ((2 * c + j + 2) % PACK))
+                bank = product(name + "1", c, "xT1", "bank%d" % ((2 * c + j) % PACK))
                 nc.scalar.activation(
                     th_1[:, 2 * c + j].rearrange("p t (h m) -> p t h m", h=2),
                     bank[:].rearrange("p (h t m) -> p t h m", h=2, t=PACK),
@@ -302,23 +290,26 @@ def tile_attend_gds_nce_kernel(tc, xT, wT, vT, wt, xm, offs, out):
         weigh(g0a[:], 0, 0)
         weigh(g0a[:], 0, 1)
         quantize("g0", flat(g0a[:]), 0, E5M2)
-        gradients_0(0, (0, 1), "bank2")
+        quantize("xm0", flat(xm00[:]), 0, scales=held("xm0_scales", [P, N], U8, KB))
+        gradients_0(0, (0, 1), "bank0")
         put(True, 0, 0, HALF)
 
         g0b = held("g0b", [P, HALF, PACK], BF16, 2 * KB)
         weigh(g0b[:], 0, 2)
         weigh(g0b[:], 0, 3)
-        xm01 = group_xm(0, 1, 0)
+        xm01 = group_xm(0, 1, 14 * KB)
         quantize("g0", flat(g0b[:]), HALF, E5M2)
         quantize_xm(0, 1, xm01)
-        gradients_0(1, (0, 1), "bank3")
+        gradients_0(1, (0, 1), "bank1")
         put(True, 0, HALF, N)
-        fetch(True, product("xm0", 3, "g0", "bank0"), 0, N, dw[3][:, 0:N])
-        fetch(True, product("xm0", 2, "g0", "bank1"), 0, N, dw[2][:, 0:N])
+        fetch(True, product("xm0", 3, "g0", "bank2"), 0, N, dw[3][:, 0:N])
+        fetch(True, product("xm0", 2, "g0", "bank3"), 0, N, dw[2][:, 0:N])
         put(True, 3, 0, HALF)
         put(True, 2, 0, 384)
-        for h in range(2):
-            quantize_xm(1, h, group_xm(1, h, 2 * KB * (1 - h)))
+        quantize_xm(1, 0, group_xm(1, 0, 12 * KB))
+        xm11 = held("xm11", [P, HALF, PACK], BF16, 12 * KB)
+        for k in (2, 3):
+            interleave_on_gpsimd(xm11[:, (k - 2) * P : (k - 1) * P, :], xm_block(1, k))
         put(False, 1, 0, HALF)
         put(False, 1, HALF, N)
         for c in range(PACK):
@@ -327,6 +318,7 @@ def tile_attend_gds_nce_kernel(tc, xT, wT, vT, wt, xm, offs, out):
         weigh(g1a[:], 1, 0)
         weigh(g1a[:], 1, 1)
         quantize("g1", flat(g1a[:]), 0, E5M2)
+        quantize("xm1b", flat(xm11[:]), 0, scales=held("xm1b_scales", [P, N], U8, 4 * KB))
         g1b = held("g1b", [P, HALF, PACK], BF16, 6 * KB)
         weigh(g1b[:], 1, 2)
         third = product("xm1", 1, "g1", "diff2", 0, HALF)
@@ -335,16 +327,16 @@ def tile_attend_gds_nce_kernel(tc, xT, wT, vT, wt, xm, offs, out):
         quantize("g1", flat(g1b[:]), HALF, E5M2)
         put(False, 1, N, N + HALF)
         fetch(False, product("xm1", 1, "g1", "diff3", HALF, N), HALF, N, dw[1][:, N + HALF :])
-        fetch(False, product("xm1", 3, "g1", "diff1"), 0, N, dw[3][:, N:])
+        fetch(False, product("xm1b", 1, "g1", "diff1"), 0, N, dw[3][:, N:])
         put(False, 1, N + HALF, B * N)
         store(1)
-        bank_01 = product("xm1", 0, "g1", "bank2")
+        bank_01 = product("xm1", 0, "g1", "bank0")
         for h in range(2):
             fetch(True, bank_01, h * HALF, (h + 1) * HALF, dw[0][:, N + h * HALF : N + (h + 1) * HALF])
         for h in range(2):
             put(True, 0, N + h * HALF, N + (h + 1) * HALF)
         store(0)
-        fetch(False, product("xm1", 2, "g1", "diff0"), 0, N, dw[2][:, N:])
+        fetch(False, product("xm1b", 0, "g1", "diff0"), 0, N, dw[2][:, N:])
         put(False, 3, HALF, B * N)
         store(3)
         put(True, 2, 384, 768)

@@ -183,7 +183,7 @@ def tile_attend_gds_nce_kernel(tc, xT, wT, vT, wt, xm, offs, out):
         quantize("xT0", flat(xT_grouped[0][:]), 0)
         w0 = [keep.tile([P, HALF, PACK], BF16, name="w0%d" % h, align_bytes=64) for h in range(2)]
         w1 = keep.tile([P, N, PACK], BF16, name="w1", align_bytes=64)
-        w1_planes = keep.tile([P, PACK, N], BF16, name="w1_planes", align_bytes=64)
+        w1_planes = keep.tile([P, PACK, N], F32, name="w1_planes")
         for t in range(PACK):
             for h in range(2):
                 gather_into_words(w0[h][:], "w", t, h * HALF, HALF)
@@ -198,8 +198,8 @@ def tile_attend_gds_nce_kernel(tc, xT, wT, vT, wt, xm, offs, out):
             turn("w", 0, c, th)
 
         quarters = [keep.tile([P, HALF, PACK], BF16, name="v_q%d" % q, align_bytes=64) for q in range(PACK)]
-        v_planes = [keep.tile([P, PACK, HALF], BF16, name="v0_planes", align_bytes=64)]
-        v1_planes = keep.tile([P, PACK, N], BF16, name="v1_planes", align_bytes=64)
+        v_planes = [keep.tile([P, PACK, HALF], F32, name="v0_planes")]
+        v1_planes = keep.tile([P, PACK, N], F32, name="v1_planes")
         sources = {1: v_planes[0][:], 2: v1_planes[:, :, 0:HALF], 3: v1_planes[:, :, HALF:N]}
 
         def word_up(q, c0=0, c1=HALF, move=nc.vector.tensor_copy):
@@ -276,13 +276,6 @@ def tile_attend_gds_nce_kernel(tc, xT, wT, vT, wt, xm, offs, out):
 
         dw = [reused.tile([P, B * N], F32, name="dw%d" % k, offset=4 * KB * k) for k in range(D // P)]
 
-        def gradients_0(h, tiles, bank_name):
-            bank = new_bank(bank_name)
-            for j, k in enumerate(tiles):
-                product("xm0", k, "g0", bank, h * HALF, (h + 1) * HALF, at=j * HALF)
-            for j, k in enumerate(tiles):
-                fetch(True, bank, j * HALF, (j + 1) * HALF, dw[k][:, h * HALF : (h + 1) * HALF])
-
         def put(on_scalar, k, i0, i1):
             scatter(on_scalar, 0, k, i0, dw[k][:, i0:i1])
 
@@ -291,8 +284,6 @@ def tile_attend_gds_nce_kernel(tc, xT, wT, vT, wt, xm, offs, out):
         weigh(g0a[:], 0, 1)
         quantize("g0", flat(g0a[:]), 0, E5M2)
         quantize("xm0", flat(xm00[:]), 0, scales=held("xm0_scales", [P, N], U8, KB))
-        gradients_0(0, (0, 1), "bank0")
-        put(True, 0, 0, HALF)
 
         g0b = held("g0b", [P, HALF, PACK], BF16, 2 * KB)
         weigh(g0b[:], 0, 2)
@@ -300,18 +291,23 @@ def tile_attend_gds_nce_kernel(tc, xT, wT, vT, wt, xm, offs, out):
         xm01 = group_xm(0, 1, 14 * KB)
         quantize("g0", flat(g0b[:]), HALF, E5M2)
         quantize_xm(0, 1, xm01)
-        gradients_0(1, (0, 1), "bank1")
-        put(True, 0, HALF, N)
+        bank_00 = product("xm0", 0, "g0", "bank0")
+        bank_10 = product("xm0", 1, "g0", "bank1")
+        for h in range(2):
+            fetch(True, bank_00, h * HALF, (h + 1) * HALF, dw[0][:, h * HALF : (h + 1) * HALF])
+        put(True, 0, 0, HALF)
         fetch(True, product("xm0", 3, "g0", "bank2"), 0, N, dw[3][:, 0:N])
+        put(True, 0, HALF, N)
         fetch(True, product("xm0", 2, "g0", "bank3"), 0, N, dw[2][:, 0:N])
         put(True, 3, 0, HALF)
         put(True, 2, 0, 384)
-        quantize_xm(1, 0, group_xm(1, 0, 12 * KB))
+        xm10 = group_xm(1, 0, 12 * KB)
+        fetch(False, bank_10, 0, N, dw[1][:, 0:N])
+        quantize_xm(1, 0, xm10)
         xm11 = held("xm11", [P, HALF, PACK], BF16, 12 * KB)
         for k in (2, 3):
             interleave_on_gpsimd(xm11[:, (k - 2) * P : (k - 1) * P, :], xm_block(1, k))
-        put(False, 1, 0, HALF)
-        put(False, 1, HALF, N)
+        put(False, 1, 0, N)
         for c in range(PACK):
             turn_1(c)
         g1a = held("g1a", [P, HALF, PACK], BF16, 4 * KB)

@@ -329,10 +329,10 @@ def tile_attend_gds_nce_kernel(tc, xT, wT, vT, wt, xm, offs, out):
         bank_01 = product("xm1", 0, "g1", "bank0")
         for h in range(2):
             fetch(True, bank_01, h * HALF, (h + 1) * HALF, dw[0][:, N + h * HALF : N + (h + 1) * HALF])
-        for h in range(2):
-            put(True, 0, N + h * HALF, N + (h + 1) * HALF)
+        put(True, 0, N, N + HALF)
+        fetch(True, product("xm1b", 0, "g1", "diff0"), 0, N, dw[2][:, N:])
+        put(True, 0, N + HALF, B * N)
         store(0)
-        fetch(False, product("xm1b", 0, "g1", "diff0"), 0, N, dw[2][:, N:])
         put(False, 3, HALF, B * N)
         store(3)
         put(True, 2, 384, 768)

@@ -138,9 +138,9 @@ def tile_attend_gds_nce_kernel(tc, xT, wT, vT, wt, xm, offs, out):
 
         def weigh(g, b, c):
             nc.vector.tensor_tensor(
-                g[:, (c % 2) * P : (c % 2 + 1) * P, :].rearrange("p (c i) t -> p c t i", i=2),
-                diffs[b, c][:].rearrange("p t (c i) -> p c t i", i=2),
-                weights[:, b : b + 1, :].rearrange("p o (t z) -> p o t z", z=1).to_broadcast([P, P // 2, PACK, 2]),
+                g[:, (c % 2) * P : (c % 2 + 1) * P, :],
+                diffs[b, c][:].rearrange("p t s -> p s t"),
+                weights[:, b : b + 1, :].to_broadcast([P, P, PACK]),
                 MULT,
             )
 

@@ -39,7 +39,7 @@ def tile_attend_gds_nce_kernel(tc, xT, wT, vT, wt, xm, offs, out):
         offsets = keep.tile([P, B * N // PER_COL], U16, name="offsets")
         weights = keep.tile([P, B, PACK], F32, name="weights")
         ident = keep.tile([P, P], F32, name="ident")
-        placed = [keep.tile([P, T], F32, name="placed%d" % k) for k in range(D // P)]
+        placed = [keep.tile([P, T], F32, name="placed%d" % k, align_bytes=256) for k in range(D // P)]
 
         make_identity(nc, ident[:])
         for k, tile in enumerate(placed):
@@ -60,13 +60,13 @@ def tile_attend_gds_nce_kernel(tc, xT, wT, vT, wt, xm, offs, out):
         def bring(name, t):
             if name == "w" or t == 1:
                 place = 8 * KB * (t if name == "w" else PACK)
-                planes[name, t] = reused.tile([P, T], F32, name="plane_%s%d" % (name, t), offset=place)
+                planes[name, t] = reused.tile([P, T], F32, name="plane_%s%d" % (name, t), align_bytes=256, offset=place)
             else:
-                planes[name, t] = keep.tile([P, T], F32, name="plane_v%d" % t)
+                planes[name, t] = keep.tile([P, T], F32, name="plane_v%d" % t, align_bytes=256)
             nc.sync.dma_start(out=planes[name, t][:], in_=by_rows(tables[name])[:, t, :])
 
         def load(name, src, c0, c1):
-            stage = keep.tile([P, PACK, c1 - c0], F32, name=name)
+            stage = keep.tile([P, PACK, c1 - c0], F32, name=name, align_bytes=256)
             nc.sync.dma_start(out=stage[:], in_=by_rows(src)[:, :, c0:c1])
             return stage
 

@@ -299,7 +299,7 @@ def tile_attend_gds_nce_kernel(tc, xT, wT, vT, wt, xm, offs, out):
         fetch(True, product("xm0", 3, "g0", "bank2"), 0, N, dw[3][:, 0:N])
         put(True, 0, HALF, N)
         fetch(True, product("xm0", 2, "g0", "bank3"), 0, N, dw[2][:, 0:N])
-        put(True, 3, 0, HALF)
+        put(True, 3, 0, 288)
         put(True, 2, 0, 384)
         xm10 = group_xm(1, 0, 12 * KB)
         fetch(False, bank_10, 0, N, dw[1][:, 0:N])
@@ -318,22 +318,25 @@ def tile_attend_gds_nce_kernel(tc, xT, wT, vT, wt, xm, offs, out):
         g1b = held("g1b", [P, HALF, PACK], BF16, 6 * KB)
         weigh(g1b[:], 1, 2)
         third = product("xm1", 1, "g1", "diff2", 0, HALF)
+        late = {0: product("xm1", 0, "g1", "bank0", 0, HALF)}
+        for k, bank_name in ((3, "diff1"), (2, "diff0")):
+            late[k] = product("xm1b", k - 2, "g1", bank_name, 0, HALF)
         weigh(g1b[:], 1, 3)
         fetch(False, third, 0, HALF, dw[1][:, N : N + HALF])
         quantize("g1", flat(g1b[:]), HALF, E5M2)
         put(False, 1, N, N + HALF)
+        bank_01 = product("xm1", 0, "g1", late[0], HALF, N)
         fetch(False, product("xm1", 1, "g1", "diff3", HALF, N), HALF, N, dw[1][:, N + HALF :])
-        fetch(False, product("xm1b", 1, "g1", "diff1"), 0, N, dw[3][:, N:])
+        fetch(False, product("xm1b", 1, "g1", late[3], HALF, N), 0, N, dw[3][:, N:])
         put(False, 1, N + HALF, B * N)
         store(1)
-        bank_01 = product("xm1", 0, "g1", "bank0")
         for h in range(2):
             fetch(True, bank_01, h * HALF, (h + 1) * HALF, dw[0][:, N + h * HALF : N + (h + 1) * HALF])
         put(True, 0, N, N + HALF)
-        fetch(True, product("xm1b", 0, "g1", "diff0"), 0, N, dw[2][:, N:])
+        fetch(True, product("xm1b", 0, "g1", late[2], HALF, N), 0, N, dw[2][:, N:])
         put(True, 0, N + HALF, B * N)
         store(0)
-        put(False, 3, HALF, B * N)
+        put(False, 3, 288, B * N)
         store(3)
         put(True, 2, 384, 768)
         put(True, 2, 768, B * N)

from contextlib import ExitStack

import concourse.mybir as mybir
from concourse.masks import make_identity

B, N, T, D, R = 2, 512, 2048, 512, 512
FLOPS = 3 * 2 * B * N * D * R

F32 = mybir.dt.float32
BF16 = mybir.dt.bfloat16
U32 = mybir.dt.uint32
U16 = mybir.dt.uint16
U8 = mybir.dt.uint8
E4M3 = mybir.dt.float8_e4m3fn_x4
E5M2 = mybir.dt.float8_e5m2_x4
MULT = mybir.AluOpType.mult
ADD = mybir.AluOpType.add
COPY = mybir.ActivationFunctionType.Copy
TANH = mybir.ActivationFunctionType.Tanh

P = 128
PACK = 4
PER_COL = 16
HALF = N // 2
RUN = 4
KB = 1024
HELP = (0, 0, 0)


def tile_attend_gds_nce_kernel(tc, xT, wT, vT, wt, xm, offs, out):
    nc = tc.nc
    with ExitStack() as ctx:
        keep = ctx.enter_context(tc.tile_pool(name="keep", bufs=1))
        shared = ctx.enter_context(tc.tile_pool(name="shared", bufs=1))
        reused = ctx.enter_context(tc.tile_pool(name="reused", bufs=1))
        ring = ctx.enter_context(tc.tile_pool(name="ring", bufs=4))
        psum = ctx.enter_context(tc.psum_pool(name="psum", bufs=1))

        offsets = keep.tile([P, B * N // PER_COL], U16, name="offsets")
        weights = keep.tile([P, B, PACK], F32, name="weights")
        ident = keep.tile([P, P], F32, name="ident")
        placed = [keep.tile([P, T], F32, name="placed%d" % k, align_bytes=256) for k in range(D // P)]

        make_identity(nc, ident[:])
        for k, tile in enumerate(placed):
            (nc.vector if k < 2 else nc.gpsimd).memset(tile[:], 0.0)

        def entries(first, count):
            return offsets[:, first // PER_COL : (first + count) // PER_COL]

        def by_rows(src):
            return src.rearrange("(p t) c -> p t c", t=PACK)

        def flat(view):
            return view.rearrange("p a b -> p (a b)")

        tables = {"w": wT, "v": vT}
        planes = {}

        def bring(name, t):
            if name == "w" or t == 1:
                place = 8 * KB * (t if name == "w" else PACK)
                planes[name, t] = reused.tile([P, T], F32, name="plane_%s%d" % (name, t), align_bytes=256, offset=place)
            else:
                planes[name, t] = keep.tile([P, T], F32, name="plane_v%d" % t, align_bytes=256)
            nc.sync.dma_start(out=planes[name, t][:], in_=by_rows(tables[name])[:, t, :])

        def load(name, src, c0, c1):
            stage = keep.tile([P, PACK, c1 - c0], F32, name=name, align_bytes=256)
            nc.sync.dma_start(out=stage[:], in_=by_rows(src)[:, :, c0:c1])
            return stage

        def gather_into_words(dst, name, t, first, count):
            nc.vector.tensor_copy(dst[:, :, t], planes[name, t][:].indirect(entries(first, count)))

        def gather_plane(dst, name, t, first, count):
            nc.scalar.activation(dst[:, t, :], planes[name, t][:].indirect(entries(first, count)), COPY)

        def interleave(move, dst, src):
            move(dst.rearrange("p (c i) t -> p c t i", i=RUN), src.rearrange("p t (c i) -> p c t i", i=RUN))

        def interleave_on_gpsimd(dst, src):
            nc.gpsimd.tensor_scalar(dst, src.rearrange("p t c -> p c t"), 1.0, 0.0, MULT, ADD)

        def deal(move, dst, src):
            move(dst.rearrange("p (t m) j -> p m j t", t=PACK), src.rearrange("p j (m t) -> p m j t", t=PACK))

        codes = {}

        def quantize(key, values, c0, fmt=E4M3, scales=None):
            if key not in codes:
                words = keep.tile([P, N], U32, name="words_" + key, align_bytes=64)
                if scales is None:
                    scales = keep.tile([P, N], U8, name="scales_" + key, align_bytes=64)
                codes[key] = (words, scales, fmt)
            words, scales, fmt = codes[key]
            c1 = c0 + values.shape[1] // PACK
            nc.vector.quantize_mx(out=words[:, c0:c1].bitcast(fmt), scales=scales[:, c0:c1], in_=values)

        def new_bank(bank_name):
            return psum.tile([P, N], F32, name=bank_name, tag=bank_name)

        def product(stationary, block, moving, bank, n0=0, n1=N, at=None):
            if isinstance(bank, str):
                bank = new_bank(bank)
            at = n0 if at is None else at
            s_words, s_scales, s_fmt = codes[stationary]
            m_words, m_scales, m_fmt = codes[moving]
            cols = slice(block * P, (block + 1) * P)
            nc.tensor.matmul_mx(
                out=bank[:, at : at + n1 - n0],
                lhsT=s_words[:, cols].bitcast(s_fmt),
                lhsT_scale=s_scales[:, cols],
                rhs=m_words[:, n0:n1].bitcast(m_fmt),
                rhs_scale=m_scales[:, n0:n1],
                start=True,
                stop=True,
            )
            return bank

        def squash(name, th, bank, t0=0, t1=PACK):
            rows = bank[:].rearrange("p (t m) -> p t m", t=PACK)
            nc.scalar.activation(th[:, t0:t1, :], rows[:, t0:t1, :], TANH, scale=0.5 if name == "w" else -0.5)

        diffs = {}

        def turn(name, b, c, th, t0=0, t1=PACK):
            if (b, c) not in diffs:
                diffs[b, c] = psum.tile([P, PACK, P], F32, name="diff%d" % c, tag="diff%d" % c)
            for t in range(t0, t1):
                nc.tensor.matmul(
                    diffs[b, c][:, t, :], th[:, t, :], ident[:], is_transpose=True,
                    start=name == "w" and t == 0, stop=name == "v" and t == PACK - 1,
                )

        def ring_th():
            return ring.tile([P, PACK, P], F32, name="th", tag="th")[:]

        def weigh(g, b, c):
            nc.vector.tensor_tensor(
                g[:, (c % 2) * P : (c % 2 + 1) * P, :],
                diffs[b, c][:].rearrange("p t s -> p s t"),
                weights[:, b : b + 1, :].to_broadcast([P, P, PACK]),
                MULT,
            )

        def held(name, shape, dtype, offset):
            return shared.tile(shape, dtype, name=name, align_bytes=64, offset=offset)

        def fetch(on_scalar, bank, n0, n1, dw):
            if on_scalar:
                nc.scalar.activation(dw[:], bank[:, n0:n1], COPY, scale=0.5)
            else:
                nc.vector.tensor_scalar(dw[:], bank[:, n0:n1], 0.5, None, MULT)
            return dw

        def scatter(on_scalar, b, k, slot0, values):
            window = placed[k][:].indirect(entries(b * N + slot0, values.shape[1]))
            if on_scalar:
                nc.scalar.activation(window, values, COPY)
            else:
                nc.vector.tensor_copy(window, values)

        def store(k):
            nc.sync.dma_start(out=out[k * P : (k + 1) * P, :], in_=placed[k][:])

        xT0_raw = load("xT0", xT[0], 0, R)
        nc.sync.dma_start(offsets[:], offs)
        for t in range(PACK):
            bring("w", t)
        for t in range(PACK):
            bring("v", t)
        xT1_raw = [load("xT1%d" % h, xT[1], h * HALF, (h + 1) * HALF) for h in range(2)]
        xm_raw = {}
        xm_raw[0, 0] = load("xm00", xm[0], 0, HALF)
        nc.sync.dma_start(out=weights[:], in_=wt.rearrange("b (p t) o -> p b (t o)", t=PACK))
        xm_raw[0, 1] = load("xm01", xm[0], HALF, D)
        xm_raw[1, 0] = load("xm10", xm[1], 0, HALF)
        xm_raw[1, 1] = load("xm11", xm[1], HALF, D)

        xT_grouped = [keep.tile([P, R, PACK], BF16, name="xT_grouped%d" % b, align_bytes=64) for b in range(B)]
        deal(nc.vector.tensor_copy, xT_grouped[0][:], xT0_raw[:])
        quantize("xT0", flat(xT_grouped[0][:]), 0)
        w0 = [keep.tile([P, HALF, PACK], BF16, name="w0%d" % h, align_bytes=64) for h in range(2)]
        w1 = keep.tile([P, N, PACK], BF16, name="w1", align_bytes=64)
        w1_planes = keep.tile([P, PACK, N], F32, name="w1_planes")
        for t in range(PACK):
            for h in range(2):
                gather_into_words(w0[h][:], "w", t, h * HALF, HALF)
            gather_plane(w1_planes[:], "w", t, N, N)
        for h in range(2):
            quantize("w0", flat(w0[h][:]), h * HALF)
        for h, move in enumerate((nc.scalar.copy, nc.vector.tensor_copy)):
            interleave(move, w1[:, h * HALF : (h + 1) * HALF, :], w1_planes[:, :, h * HALF : (h + 1) * HALF])

        def student_scores(c, th):
            squash("w", th, product("w0", c, "xT0", "bank%d" % c))
            turn("w", 0, c, th)

        quarters = [keep.tile([P, HALF, PACK], BF16, name="v_q%d" % q, align_bytes=64) for q in range(PACK)]
        v_planes = [keep.tile([P, PACK, HALF], F32, name="v0_planes")]
        v1_planes = keep.tile([P, PACK, N], F32, name="v1_planes")
        sources = {1: v_planes[0][:], 2: v1_planes[:, :, 0:HALF], 3: v1_planes[:, :, HALF:N]}

        def word_up(q, c0=0, c1=HALF, move=nc.vector.tensor_copy):
            interleave(move, quarters[q][:, c0:c1, :], sources[q][:, :, c0:c1])

        last = PACK - 1
        for t in range(last):
            gather_into_words(quarters[0][:], "v", t, 0, HALF)
            nc.vector.tensor_copy(sources[1][:, t, :], planes["v", t][:].indirect(entries(HALF, HALF)))
            share = HELP[t]
            if share:
                nc.vector.tensor_copy(v1_planes[:, t, 0:share], planes["v", t][:].indirect(entries(N, share)))
            gather_plane(v1_planes[:, :, share:N], "v", t, N + share, N - share)
            if t == 0:
                quantize("w1", flat(w1[:]), 0)
                for c in range(PACK):
                    student_scores(c, ring_th())
        for q in range(1, PACK):
            gather_plane(sources[q], "v", last, q * HALF, HALF)
        word_up(2, 0, P, nc.scalar.copy)
        gather_into_words(quarters[0][:], "v", last, 0, HALF)
        quantize("v0", flat(quarters[0][:]), 0)
        word_up(1)
        quantize("v0", flat(quarters[1][:]), HALF)
        for h in range(2):
            deal(nc.vector.tensor_copy, xT_grouped[1][:, h * HALF : (h + 1) * HALF, :], xT1_raw[h][:])
            word_up(2 + h, P * (1 - h), HALF - P * h)
            quantize("xT1", flat(xT_grouped[1][:, h * HALF : (h + 1) * HALF, :]), h * HALF)
            if h == 1:
                word_up(3, P)
            quantize("v1", flat(quarters[2 + h][:]), h * HALF)

        def group_xm(b, h, offset, move=nc.vector.tensor_copy):
            grouped = held("xm%d%d" % (b, h), [P, HALF, PACK], BF16, offset)
            interleave(move, grouped[:], xm_raw[b, h][:])
            return grouped

        def quantize_xm(b, h, grouped):
            quantize("xm%d" % b, flat(grouped[:]), h * HALF)


        ths = [ring_th() for c in range(PACK)]
        scores_0 = [product("v0", c, "xT0", "bank%d" % c) for c in range(PACK)]
        for c in range(PACK):
            squash("v", ths[c], scores_0[c])
        xm00 = group_xm(0, 0, 12 * KB, nc.scalar.copy)
        for c in (0, 1):
            turn("v", 0, c, ths[c])
        th_1 = reused.tile([P, 2 * PACK, PACK, P], F32, name="th_1", offset=16 * KB)
        for c in range(PACK):
            for j, name in enumerate("wv"):
                bank = product(name + "1", c, "xT1", "bank%d" % ((2 * c + j) % PACK))
                nc.scalar.activation(
                    th_1[:, 2 * c + j].rearrange("p t (h m) -> p t h m", h=2),
                    bank[:].rearrange("p (h t m) -> p t h m", h=2, t=PACK),
                    TANH, scale=0.5 if name == "w" else -0.5,
                )
            if c == 0:
                for c0 in (2, 3):
                    turn("v", 0, c0, ths[c0])

        def xm_block(b, k):
            return xm_raw[b, k // 2][:, :, (k % 2) * P : (k % 2 + 1) * P]

        def small(name):
            return keep.tile([P, HALF], F32, name=name)

        def wide(name):
            return keep.tile([P, N], F32, name=name)

        def turn_1(c):
            turn("w", 1, c, th_1[:, 2 * c])
            turn("v", 1, c, th_1[:, 2 * c + 1])

        dw = [reused.tile([P, B * N], F32, name="dw%d" % k, offset=4 * KB * k) for k in range(D // P)]

        def put(on_scalar, k, i0, i1):
            scatter(on_scalar, 0, k, i0, dw[k][:, i0:i1])

        g0a = held("g0a", [P, HALF, PACK], BF16, 0)
        weigh(g0a[:], 0, 0)
        weigh(g0a[:], 0, 1)
        quantize("g0", flat(g0a[:]), 0, E5M2)
        quantize("xm0", flat(xm00[:]), 0, scales=held("xm0_scales", [P, N], U8, KB))

        g0b = held("g0b", [P, HALF, PACK], BF16, 2 * KB)
        weigh(g0b[:], 0, 2)
        weigh(g0b[:], 0, 3)
        xm01 = group_xm(0, 1, 14 * KB)
        quantize("g0", flat(g0b[:]), HALF, E5M2)
        quantize_xm(0, 1, xm01)
        bank_00 = product("xm0", 0, "g0", "bank0")
        bank_10 = product("xm0", 1, "g0", "bank1")
        for h in range(2):
            fetch(True, bank_00, h * HALF, (h + 1) * HALF, dw[0][:, h * HALF : (h + 1) * HALF])
        put(True, 0, 0, HALF)
        fetch(True, product("xm0", 3, "g0", "bank2"), 0, N, dw[3][:, 0:N])
        put(True, 0, HALF, N)
        fetch(True, product("xm0", 2, "g0", "bank3"), 0, N, dw[2][:, 0:N])
        put(True, 3, 0, 288)
        put(True, 2, 0, 384)
        xm10 = group_xm(1, 0, 12 * KB)
        fetch(False, bank_10, 0, N, dw[1][:, 0:N])
        quantize_xm(1, 0, xm10)
        xm11 = held("xm11", [P, HALF, PACK], BF16, 12 * KB)
        for k in (2, 3):
            interleave_on_gpsimd(xm11[:, (k - 2) * P : (k - 1) * P, :], xm_block(1, k))
        put(False, 1, 0, N)
        for c in range(PACK):
            turn_1(c)
        g1a = held("g1a", [P, HALF, PACK], BF16, 4 * KB)
        weigh(g1a[:], 1, 0)
        weigh(g1a[:], 1, 1)
        quantize("g1", flat(g1a[:]), 0, E5M2)
        quantize("xm1b", flat(xm11[:]), 0, scales=held("xm1b_scales", [P, N], U8, 4 * KB))
        g1b = held("g1b", [P, HALF, PACK], BF16, 6 * KB)
        weigh(g1b[:], 1, 2)
        third = product("xm1", 1, "g1", "diff2", 0, HALF)
        late = {0: product("xm1", 0, "g1", "bank0", 0, HALF)}
        for k, bank_name in ((3, "diff1"), (2, "diff0")):
            late[k] = product("xm1b", k - 2, "g1", bank_name, 0, HALF)
        weigh(g1b[:], 1, 3)
        fetch(False, third, 0, HALF, dw[1][:, N : N + HALF])
        quantize("g1", flat(g1b[:]), HALF, E5M2)
        put(False, 1, N, N + HALF)
        bank_01 = product("xm1", 0, "g1", late[0], HALF, N)
        fetch(False, product("xm1", 1, "g1", "diff3", HALF, N), HALF, N, dw[1][:, N + HALF :])
        fetch(False, product("xm1b", 1, "g1", late[3], HALF, N), 0, N, dw[3][:, N:])
        put(False, 1, N + HALF, B * N)
        store(1)
        for h in range(2):
            fetch(True, bank_01, h * HALF, (h + 1) * HALF, dw[0][:, N + h * HALF : N + (h + 1) * HALF])
        put(True, 0, N, N + HALF)
        fetch(True, product("xm1b", 0, "g1", late[2], HALF, N), 0, N, dw[2][:, N:])
        put(True, 0, N + HALF, B * N)
        store(0)
        put(False, 3, 288, B * N)
        store(3)
        put(True, 2, 384, 768)
        put(True, 2, 768, B * N)
        nc.sync.dma_start(out=out[2 * P : 3 * P, 0 : T // 2], in_=placed[2][:, 0 : T // 2])
        nc.scalar.dma_start(out=out[2 * P : 3 * P, T // 2 :], in_=placed[2][:, T // 2 :])
